import numpy as np
import ml_dtypes


def mxq(x, axis, fmt="e4m3"):
    dtype, down = {"e4m3": (ml_dtypes.float8_e4m3fn, 7), "e5m2": (ml_dtypes.float8_e5m2, 14)}[fmt]
    v = np.moveaxis(np.asarray(x, np.float32).astype(ml_dtypes.bfloat16).astype(np.float64), axis, -1)
    blocks = v.reshape(v.shape[:-1] + (-1, 32))
    amax = np.abs(blocks).max(-1, keepdims=True)
    byte = np.maximum(np.where(amax > 0, np.frexp(amax)[1] - 1 + 127, 0) - down, 1)
    scale = np.exp2(byte - 127.0)
    codes = (blocks / scale).astype(np.float32).astype(dtype).astype(np.float64)
    return np.moveaxis((codes * scale).reshape(v.shape), -1, axis)


WIDE = False


def mx_kscale(k):
    if not WIDE:
        return np.ones(k)
    levels = np.array([10, -10, 5, -5, 0])
    if k % 512:
        return np.exp2(np.random.permutation(np.resize(levels, k // 32))).repeat(32)
    a = np.empty((k // 512, 16))
    for p in range(k // 512):
        a[p, :8] = np.random.permutation(np.resize(levels, 8))
        for g in range(8):
            far = levels[np.abs(levels - a[p, g]) >= 10]
            a[p, g + 8] = far[np.random.randint(len(far))]
    return np.exp2(a.ravel()).repeat(32)


def f64(x):
    return np.asarray(x).astype(np.float64)


def striped(idx):
    return np.tile(idx.reshape(-1, 16).T, (8, 1)).astype(np.uint16)


def unstriped(offs):
    return offs[:16].T.reshape(-1).astype(np.int64)


def striped8(idx):
    return np.concatenate([x.reshape(-1, 16).T for x in idx]).astype(np.uint16)


def runs(offs, k):
    lists = np.stack([offs[16 * r : 16 * r + 16].T.reshape(-1) for r in range(8)]).astype(np.int64)
    return lists[np.arange(k) % 512 // 64]


def pack_weight(w):
    k, n = w.shape
    w = f64(np.asarray(w, np.float32).astype(ml_dtypes.bfloat16)).reshape(k // 32, 32, n)
    amax = np.abs(w).max(1)
    byte = np.clip(np.where(amax > 0, np.frexp(amax)[1] - 1 + 127 - 7, 1), 1, 254)
    scaled = (w * np.exp2(127.0 - byte)[:, None, :]).reshape(k, n).astype(np.float32)
    words = np.ascontiguousarray(scaled.reshape(k // 512, 128, 4, n).transpose(0, 1, 3, 2)).astype(ml_dtypes.float8_e4m3fn).view(np.uint8)
    return words, np.ascontiguousarray(byte.astype(np.uint8).reshape(k // 512, 16, n))


def unpack_weight(words, scales):
    g, p, n, _ = words.shape
    vals = np.ascontiguousarray(words).view(ml_dtypes.float8_e4m3fn).astype(np.float64) * np.repeat(np.exp2(scales.astype(np.float64) - 127.0), 8, axis=1)[..., None]
    return vals.transpose(0, 1, 3, 2).reshape(g * 512, n)


E2M1 = np.array([0.0, 0.5, 1.0, 1.5, 2.0, 3.0, 4.0, 6.0, -0.0, -0.5, -1.0, -1.5, -2.0, -3.0, -4.0, -6.0])


def pack_fp4(w):
    k, n = w.shape
    w = f64(np.asarray(w, np.float32).astype(ml_dtypes.bfloat16)).reshape(k // 32, 32, n)
    amax = np.abs(w).max(1)
    mant, ex = np.frexp(amax / 6.0)
    byte = np.clip(np.where(amax > 0, np.where(mant > 0.5, ex, ex - 1) + 127, 1), 1, 254)
    scaled = (w * np.exp2(127.0 - byte)[:, None, :]).reshape(k, n).astype(np.float32)
    c = np.ascontiguousarray(scaled.reshape(k // 512, 128, 4, n).transpose(0, 1, 3, 2)).astype(ml_dtypes.float4_e2m1fn).view(np.uint8) & 0xF
    words = (c[..., 0::2] | (c[..., 1::2] << 4)).reshape(k // 512, 128, 2 * n)
    return np.ascontiguousarray(words), np.ascontiguousarray(byte.astype(np.uint8).reshape(k // 512, 16, n))


def unpack_fp4(words, scales):
    g, _, n = scales.shape
    words = np.ascontiguousarray(words).reshape(g, 128, n, 2)
    nib = np.empty((g, 128, n, 4), np.uint8)
    nib[..., 0::2] = words & 0xF
    nib[..., 1::2] = words >> 4
    vals = E2M1[nib] * np.repeat(np.exp2(scales.astype(np.float64) - 127.0), 8, axis=1)[..., None]
    return vals.transpose(0, 1, 3, 2).reshape(g * 512, n)


def planes(y):
    n, m = y.shape
    v = y.astype(np.float32).astype(ml_dtypes.bfloat16).astype(np.float64).reshape(n // 32, 32, m)
    top = np.abs(v).max(1)
    byte = np.clip(np.where(top > 0, np.frexp(top)[1] - 1 + 127 - 7, 1), 1, 254)
    codes = (v * np.exp2(127.0 - byte)[:, None, :]).reshape(n, m).astype(np.float32).astype(ml_dtypes.float8_e4m3fn).view(np.uint8)
    words = codes.reshape(n // 512, 128, 4, m).transpose(0, 1, 3, 2)
    return np.ascontiguousarray(words), np.ascontiguousarray(byte.astype(np.uint8).reshape(n // 512, 16, m))


K, T, S, H = 512, 2048, 512, 512


def setup_inputs():
    n = np.random.standard_normal
    s = mx_kscale(K)[:, None]
    u = mx_kscale(H)
    packed_xT = pack_weight(n((K, T)) * s)
    packed_w1 = pack_fp4(n((K, H)) / np.sqrt(K) / s)
    packed_w2 = pack_fp4(n((H, H)) / np.sqrt(H) / u[:, None])
    return {
        "x_words": packed_xT[0],
        "x_scales": packed_xT[1],
        "w1_words": packed_w1[0],
        "w1_scales": packed_w1[1],
        "gn": (np.random.uniform(0.5, 1.5, (H, 1)) * u[:, None]).astype(np.float32),
        "w2_words": packed_w2[0],
        "w2_scales": packed_w2[1],
        "offs": striped(np.random.permutation(T)[:S]),
        "nb": striped8(np.stack([np.random.permutation(S) for _ in range(8)])),
    }


def reference(x_words, x_scales, w1_words, w1_scales, gn, w2_words, w2_scales, offs, nb):
    xq = unpack_weight(x_words, x_scales)[:, unstriped(offs)]
    y = unpack_fp4(w1_words, w1_scales).T @ xq
    z = f64(gn) * (y[np.arange(H)[:, None], runs(nb, H)])
    w2q = unpack_fp4(w2_words, w2_scales)
    k1 = np.tanh(w2q.T @ mxq(z, 0, "e4m3"))
    h = y + 0.5 * k1
    z2 = f64(gn) * (h[np.arange(H)[:, None], runs(nb, H)])
    k2 = np.tanh(w2q.T @ mxq(z2, 0, "e4m3"))
    out_0 = y + 0.25 * (k1 + k2)
    return (out_0,) + planes(out_0)

@@ -1,0 +1,192 @@
+from contextlib import ExitStack
+
+import concourse.mybir as mybir
+
+K, T, S, H = 512, 2048, 512, 512
+FLOPS = 3 * 2 * 512 * 512 * 512
+
+F32 = mybir.dt.float32
+BF16 = mybir.dt.bfloat16
+I32 = mybir.dt.int32
+U32 = mybir.dt.uint32
+U16 = mybir.dt.uint16
+U8 = mybir.dt.uint8
+FP8X4 = mybir.dt.float8_e4m3fn_x4
+FP4X4 = mybir.dt.float4_e2m1fn_x4
+MULT = mybir.AluOpType.mult
+ADD = mybir.AluOpType.add
+ACT = mybir.ActivationFunctionType
+
+P = 128
+PACK = 4
+CH = 128
+NCH = S // CH
+
+
+def load_scale_rows(queue, plane, scales):
+    for q in range(4):
+        queue.dma_start(plane[32 * q : 32 * q + 4, :].bitcast(I32), scales[0, 4 * q : 4 * q + 4, :].bitcast(I32))
+
+
+def deal_words(eng, dealt, raw):
+    eng.tensor_copy(
+        dealt[:].rearrange("p (t m b) -> p t m b", t=PACK, b=2),
+        raw[:].rearrange("p (m t b) -> p t m b", t=PACK, b=2),
+    )
+
+
+def deal_scales(eng, dealt, raw):
+    eng.tensor_copy(
+        dealt[:].rearrange("p (t m) -> p t m", t=PACK),
+        raw[:].rearrange("p (m t) -> p t m", t=PACK),
+    )
+
+
+def weave(copy, woven, rows):
+    copy(
+        woven.rearrange("p (c i t) -> p c t i", i=4, t=PACK),
+        rows.rearrange("p t (c i) -> p c t i", i=4),
+    )
+
+
+def tile_picked_heun_none_po_kernel(
+    tc, x_words, x_scales, w1_words, w1_scales, gn, w2_words, w2_scales, offs, nb, out_0, out_1, out_2
+):
+    nc = tc.nc
+    with ExitStack() as ctx:
+        keep = ctx.enter_context(tc.tile_pool(name="keep", bufs=1))
+        ring = ctx.enter_context(tc.tile_pool(name="ring", bufs=2))
+        psum = ctx.enter_context(tc.psum_pool(name="psum", bufs=1))
+
+        offs_sb = keep.tile([P, S // 16], U16, name="offs_sb")
+        nb_sb = keep.tile([P, S // 16], U16, name="nb_sb")
+        xw = keep.tile([P, T], U32, name="xw", align_bytes=64)
+        xs = keep.tile([P, T], U8, name="xs", align_bytes=64)
+        w1w_raw = keep.tile([P, 2 * H], U8, name="w1w_raw", align_bytes=64)
+        w2w_raw = keep.tile([P, 2 * H], U8, name="w2w_raw", align_bytes=64)
+        w1s_raw = keep.tile([P, H], U8, name="w1s_raw", align_bytes=64)
+        w2s_raw = keep.tile([P, H], U8, name="w2s_raw", align_bytes=64)
+        gain = keep.tile([P, PACK], F32, name="gain", tag="gain_then_w2s", align_bytes=64)
+        half_gain = keep.tile([P, PACK], F32, name="half_gain")
+
+        nc.gpsimd.memset(xs[:].bitcast(I32), 0)
+        nc.gpsimd.dma_start(gain[:], gn.rearrange("(p t) o -> p (t o)", t=PACK))
+        nc.vector.memset(w1s_raw[:].bitcast(I32), 0)
+        nc.vector.memset(w2s_raw[:].bitcast(I32), 0)
+
+        x_view = x_words[0].rearrange("p n r -> p (n r)").bitcast(I32)
+        nc.sync.dma_start(offs_sb[:], offs)
+        nc.sync.dma_start(w1w_raw[:].bitcast(I32), w1_words[0].bitcast(I32))
+        nc.sync.dma_start(xw[:, : T // 2].bitcast(I32), x_view[:, : T // 2])
+        load_scale_rows(nc.sync, xs, x_scales)
+        nc.sync.dma_start(xw[:, T // 2 :].bitcast(I32), x_view[:, T // 2 :])
+        load_scale_rows(nc.sync, w1s_raw, w1_scales)
+        nc.sync.dma_start(nb_sb[:], nb)
+        nc.sync.dma_start(w2w_raw[:].bitcast(I32), w2_words[0].bitcast(I32))
+        load_scale_rows(nc.sync, w2s_raw, w2_scales)
+
+        w1w = keep.tile([P, 2 * H], U8, name="w1w", align_bytes=64)
+        w2w = keep.tile([P, 2 * H], U8, name="w2w", align_bytes=64)
+        w1s = keep.tile([P, H], U8, name="w1s", align_bytes=64)
+        xqw = keep.tile([P, S], U32, name="xqw", align_bytes=64)
+        xqs = keep.tile([P, S], U8, name="xqs", align_bytes=64)
+
+        deal_words(nc.vector, w1w, w1w_raw)
+        nc.vector.tensor_copy(xqs[:], xs[:].indirect(offs_sb[:]))
+        nc.vector.tensor_copy(xqw[:], xw[:].indirect(offs_sb[:]))
+        w1s_by_t = w1s[:].rearrange("p (t m) -> p t m", t=PACK)
+        w1s_raw_by_t = w1s_raw[:].rearrange("p (m t) -> p t m", t=PACK)
+        nc.vector.tensor_copy(w1s_by_t[:, 0, :], w1s_raw_by_t[:, 0, :])
+        nc.vector.tensor_copy(w1s_by_t[:, 1:, :], w1s_raw_by_t[:, 1:, :])
+        deal_words(nc.vector, w2w, w2w_raw)
+        nc.gpsimd.tensor_scalar(half_gain[:], gain[:], 0.5, 0.0, MULT, ADD)
+
+        def product(acc, words, scales, t, codes, code_scales):
+            nc.tensor.matmul_mx(
+                out=acc,
+                lhsT=words[:, 2 * P * t : 2 * P * (t + 1)].bitcast(FP4X4),
+                lhsT_scale=scales[:, P * t : P * (t + 1)],
+                rhs=codes.bitcast(FP8X4),
+                rhs_scale=code_scales,
+                start=True,
+                stop=True,
+            )
+
+        y = [psum.tile([P, S], F32, name=f"y{t}") for t in range(PACK)]
+        gy = [keep.tile([P, S], F32, name=f"gy{t}") for t in range(PACK)]
+        gh = [keep.tile([P, S], F32, name=f"gh{t}") for t in range(PACK)]
+        for t in range(PACK):
+            product(y[t][:], w1w, w1s, t, xqw[:], xqs[:])
+            nc.scalar.activation(gy[t][:], y[t][:], ACT.Copy, scale=gain[:, t : t + 1])
+
+        w2s = keep.tile([P, H], U8, name="w2s", tag="gain_then_w2s", align_bytes=64)
+
+        def velocity(name, windows, k, before_first_product):
+            woven = {}
+
+            def fetch(c):
+                rows = ring.tile([P, PACK, CH], BF16, name=f"{name}_rows{c}", tag="rows", align_bytes=64)
+                for t in range(PACK):
+                    nc.vector.tensor_copy(
+                        rows[:, t, :], windows[t][:].indirect(nb_sb[:, c * CH // 16 : (c + 1) * CH // 16])
+                    )
+                tag = f"{name}_codes{c - 2}" if c >= 2 else f"{name}_woven{c}"
+                woven[c] = keep.tile([P, PACK * CH], BF16, name=f"{name}_woven{c}", tag=tag, align_bytes=64)
+                weave(nc.scalar.copy, woven[c][:], rows[:])
+
+            def multiply(c):
+                codes = keep.tile([P, CH], U32, name=f"{name}_codes{c}", tag=f"{name}_codes{c}", align_bytes=64)
+                scales = keep.tile([P, CH], U8, name=f"{name}_scales{c}", align_bytes=64)
+                nc.vector.quantize_mx(out=codes[:].bitcast(FP8X4), scales=scales[:], in_=woven[c][:])
+                acc = psum.tile([P, PACK, CH], F32, name=f"acc{c}")
+                for t in range(PACK):
+                    product(acc[:, t, :], w2w, w2s, t, codes[:], scales[:])
+                nc.scalar.activation(k[:, :, c * CH : (c + 1) * CH], acc[:], ACT.Tanh)
+
+            fetch(0)
+            fetch(1)
+            before_first_product()
+            for c in range(NCH):
+                multiply(c)
+                if c + 2 < NCH:
+                    fetch(c + 2)
+
+        k1 = keep.tile([P, PACK, S], F32, name="k1")
+        k2 = keep.tile([P, PACK, S], F32, name="k2")
+        part = keep.tile([P, PACK, S], F32, name="part")
+        velocity("start", gy, k1, lambda: deal_scales(nc.vector, w2s, w2s_raw))
+
+        def midpoint(cols):
+            for t in range(PACK):
+                nc.vector.scalar_tensor_tensor(
+                    gh[t][:, cols], k1[:, t, cols], half_gain[:, t : t + 1], gy[t][:, cols], MULT, ADD
+                )
+
+        def partial(cols):
+            for t in range(PACK):
+                nc.vector.scalar_tensor_tensor(part[:, t, cols], k1[:, t, cols], 0.25, y[t][:, cols], MULT, ADD)
+
+        midpoint(slice(0, S // 2))
+        partial(slice(0, S // 2))
+        midpoint(slice(S // 2, S))
+        velocity("end", gh, k2, lambda: partial(slice(S // 2, S)))
+
+        out_rows = out_0.rearrange("(p t) s -> p t s", t=PACK)
+        out_words = out_1[0].rearrange("p n r -> p (n r)").bitcast(I32)
+        out_codes = keep.tile([P, S], U32, name="out_codes", align_bytes=64)
+        out_scales = keep.tile([P, S], U8, name="out_scales", align_bytes=64)
+        for c in range(NCH):
+            cols = slice(c * CH, (c + 1) * CH)
+            if c < 2:
+                result = ring.tile([P, PACK, CH], F32, name=f"result{c}", tag="rows", align_bytes=64)
+            else:
+                result = keep.tile([P, PACK, CH], F32, name=f"result{c}")
+            rounded = keep.tile([P, PACK * CH], BF16, name=f"rounded{c}", align_bytes=64)
+            nc.vector.scalar_tensor_tensor(result[:], k2[:, :, cols], 0.25, part[:, :, cols], MULT, ADD)
+            nc.sync.dma_start(out_rows[:, :, cols], result[:])
+            weave(nc.scalar.copy if c < NCH - 1 else nc.vector.tensor_copy, rounded[:], result[:])
+            nc.vector.quantize_mx(out=out_codes[:, cols].bitcast(FP8X4), scales=out_scales[:, cols], in_=rounded[:])
+            nc.sync.dma_start(out_words[:, cols], out_codes[:, cols].bitcast(I32))
+        for q in range(4):
+            queue = nc.sync if q % 2 == 0 else nc.scalar
+            queue.dma_start(out_2[0, 4 * q : 4 * q + 4, :].bitcast(I32), out_scales[32 * q : 32 * q + 4, :].bitcast(I32))

@@ -21,6 +21,7 @@ P = 128
 PACK = 4
 CH = 128
 NCH = S // CH
+X_FIRST = 640
 
 
 def load_scale_rows(queue, plane, scales):
@@ -55,7 +56,6 @@ def tile_picked_heun_none_po_kernel(
     nc = tc.nc
     with ExitStack() as ctx:
         keep = ctx.enter_context(tc.tile_pool(name="keep", bufs=1))
-        ring = ctx.enter_context(tc.tile_pool(name="ring", bufs=2))
         psum = ctx.enter_context(tc.psum_pool(name="psum", bufs=1))
 
         offs_sb = keep.tile([P, S // 16], U16, name="offs_sb")
@@ -66,21 +66,22 @@ def tile_picked_heun_none_po_kernel(
         w2w_raw = keep.tile([P, 2 * H], U8, name="w2w_raw", align_bytes=64)
         w1s_raw = keep.tile([P, H], U8, name="w1s_raw", align_bytes=64)
         w2s_raw = keep.tile([P, H], U8, name="w2s_raw", align_bytes=64)
-        gain = keep.tile([P, PACK], F32, name="gain", tag="gain_then_w2s", align_bytes=64)
-        half_gain = keep.tile([P, PACK], F32, name="half_gain")
+        gain = keep.tile([P, PACK], F32, name="gain", tag="start_late", align_bytes=64)
+        half_gain = keep.tile([P, PACK], F32, name="half_gain", tag="end_late", align_bytes=64)
 
-        nc.gpsimd.memset(xs[:].bitcast(I32), 0)
-        nc.gpsimd.dma_start(gain[:], gn.rearrange("(p t) o -> p (t o)", t=PACK))
+        nc.gpsimd.memset(xs[:, : T // 2].bitcast(I32), 0)
+        nc.vector.memset(xs[:, T // 2 :].bitcast(I32), 0)
         nc.vector.memset(w1s_raw[:].bitcast(I32), 0)
         nc.vector.memset(w2s_raw[:].bitcast(I32), 0)
 
         x_view = x_words[0].rearrange("p n r -> p (n r)").bitcast(I32)
         nc.sync.dma_start(offs_sb[:], offs)
         nc.sync.dma_start(w1w_raw[:].bitcast(I32), w1_words[0].bitcast(I32))
-        nc.sync.dma_start(xw[:, : T // 2].bitcast(I32), x_view[:, : T // 2])
+        nc.sync.dma_start(xw[:, :X_FIRST].bitcast(I32), x_view[:, :X_FIRST])
         load_scale_rows(nc.sync, xs, x_scales)
-        nc.sync.dma_start(xw[:, T // 2 :].bitcast(I32), x_view[:, T // 2 :])
+        nc.sync.dma_start(xw[:, X_FIRST:].bitcast(I32), x_view[:, X_FIRST:])
         load_scale_rows(nc.sync, w1s_raw, w1_scales)
+        nc.sync.dma_start(gain[:], gn.rearrange("(p t) o -> p (t o)", t=PACK))
         nc.sync.dma_start(nb_sb[:], nb)
         nc.sync.dma_start(w2w_raw[:].bitcast(I32), w2_words[0].bitcast(I32))
         load_scale_rows(nc.sync, w2s_raw, w2_scales)
@@ -88,18 +89,18 @@ def tile_picked_heun_none_po_kernel(
         w1w = keep.tile([P, 2 * H], U8, name="w1w", align_bytes=64)
         w2w = keep.tile([P, 2 * H], U8, name="w2w", align_bytes=64)
         w1s = keep.tile([P, H], U8, name="w1s", align_bytes=64)
-        xqw = keep.tile([P, S], U32, name="xqw", align_bytes=64)
+        w2s = keep.tile([P, H], U8, name="w2s", align_bytes=64)
+        xqw = [keep.tile([P, S // 2], U32, name=f"xqw{half}", align_bytes=64) for half in range(2)]
         xqs = keep.tile([P, S], U8, name="xqs", align_bytes=64)
 
+        nc.scalar.activation(half_gain[:], gain[:], ACT.Copy, scale=0.5)
         deal_words(nc.vector, w1w, w1w_raw)
         nc.vector.tensor_copy(xqs[:], xs[:].indirect(offs_sb[:]))
-        nc.vector.tensor_copy(xqw[:], xw[:].indirect(offs_sb[:]))
-        w1s_by_t = w1s[:].rearrange("p (t m) -> p t m", t=PACK)
-        w1s_raw_by_t = w1s_raw[:].rearrange("p (m t) -> p t m", t=PACK)
-        nc.vector.tensor_copy(w1s_by_t[:, 0, :], w1s_raw_by_t[:, 0, :])
-        nc.vector.tensor_copy(w1s_by_t[:, 1:, :], w1s_raw_by_t[:, 1:, :])
+        nc.vector.tensor_copy(xqw[0][:], xw[:].indirect(offs_sb[:, : S // 32]))
+        deal_scales(nc.vector, w1s, w1s_raw)
+        nc.vector.tensor_copy(xqw[1][:], xw[:].indirect(offs_sb[:, S // 32 :]))
         deal_words(nc.vector, w2w, w2w_raw)
-        nc.gpsimd.tensor_scalar(half_gain[:], gain[:], 0.5, 0.0, MULT, ADD)
+        deal_scales(nc.vector, w2s, w2s_raw)
 
         def product(acc, words, scales, t, codes, code_scales):
             nc.tensor.matmul_mx(
@@ -112,64 +113,73 @@ def tile_picked_heun_none_po_kernel(
                 stop=True,
             )
 
-        y = [psum.tile([P, S], F32, name=f"y{t}") for t in range(PACK)]
+        y_banks = [psum.tile([P, 2, S // 2], F32, name=f"y_bank{b}") for b in range(PACK)]
+        y = {(t, half): y_banks[2 * half + t % 2][:, t // 2, :] for t in range(PACK) for half in range(2)}
+        acc = [psum.tile([P, S], F32, name=f"acc{t}") for t in range(PACK)]
         gy = [keep.tile([P, S], F32, name=f"gy{t}") for t in range(PACK)]
         gh = [keep.tile([P, S], F32, name=f"gh{t}") for t in range(PACK)]
-        for t in range(PACK):
-            product(y[t][:], w1w, w1s, t, xqw[:], xqs[:])
-            nc.scalar.activation(gy[t][:], y[t][:], ACT.Copy, scale=gain[:, t : t + 1])
 
-        w2s = keep.tile([P, H], U8, name="w2s", tag="gain_then_w2s", align_bytes=64)
+        for pair in range(0, PACK, 2):
+            for half in range(2):
+                cols = slice(half * S // 2, (half + 1) * S // 2)
+                for t in (pair, pair + 1):
+                    product(y[t, half], w1w, w1s, t, xqw[half][:], xqs[:, cols])
+                    nc.scalar.activation(gy[t][:, cols], y[t, half], ACT.Copy, scale=gain[:, t : t + 1])
 
-        def velocity(name, windows, k, before_first_product):
+        def velocity(name, windows, k, last_copy):
             woven = {}
 
             def fetch(c):
-                rows = ring.tile([P, PACK, CH], BF16, name=f"{name}_rows{c}", tag="rows", align_bytes=64)
+                tag = {2: f"{name}_late", 3: f"{name}_rows1"}.get(c, f"{name}_rows{c}")
+                rows = keep.tile([P, PACK, CH], BF16, name=f"{name}_rows{c}", tag=tag, align_bytes=64)
                 for t in range(PACK):
                     nc.vector.tensor_copy(
                         rows[:, t, :], windows[t][:].indirect(nb_sb[:, c * CH // 16 : (c + 1) * CH // 16])
                     )
-                tag = f"{name}_codes{c - 2}" if c >= 2 else f"{name}_woven{c}"
-                woven[c] = keep.tile([P, PACK * CH], BF16, name=f"{name}_woven{c}", tag=tag, align_bytes=64)
-                weave(nc.scalar.copy, woven[c][:], rows[:])
+                woven[c] = keep.tile([P, PACK * CH], BF16, name=f"{name}_woven{c}", align_bytes=64)
+                weave(last_copy if c == NCH - 1 else nc.scalar.copy, woven[c][:], rows[:])
 
             def multiply(c):
-                codes = keep.tile([P, CH], U32, name=f"{name}_codes{c}", tag=f"{name}_codes{c}", align_bytes=64)
+                cols = slice(c * CH, (c + 1) * CH)
+                codes = keep.tile([P, CH], U32, name=f"{name}_codes{c}", align_bytes=64)
                 scales = keep.tile([P, CH], U8, name=f"{name}_scales{c}", align_bytes=64)
                 nc.vector.quantize_mx(out=codes[:].bitcast(FP8X4), scales=scales[:], in_=woven[c][:])
-                acc = psum.tile([P, PACK, CH], F32, name=f"acc{c}")
                 for t in range(PACK):
-                    product(acc[:, t, :], w2w, w2s, t, codes[:], scales[:])
-                nc.scalar.activation(k[:, :, c * CH : (c + 1) * CH], acc[:], ACT.Tanh)
+                    product(acc[t][:, cols], w2w, w2s, t, codes[:], scales[:])
+                    nc.scalar.activation(k[:, t, cols], acc[t][:, cols], ACT.Tanh)
 
             fetch(0)
             fetch(1)
-            before_first_product()
-            for c in range(NCH):
-                multiply(c)
-                if c + 2 < NCH:
-                    fetch(c + 2)
+            fetch(2)
+            multiply(0)
+            multiply(1)
+            fetch(3)
+            multiply(2)
+            multiply(3)
 
         k1 = keep.tile([P, PACK, S], F32, name="k1")
         k2 = keep.tile([P, PACK, S], F32, name="k2")
-        part = keep.tile([P, PACK, S], F32, name="part")
-        velocity("start", gy, k1, lambda: deal_scales(nc.vector, w2s, w2s_raw))
+        velocity("start", gy, k1, nc.scalar.copy)
 
-        def midpoint(cols):
+        def midpoint(c):
+            cols = slice(c * CH, (c + 1) * CH)
             for t in range(PACK):
                 nc.vector.scalar_tensor_tensor(
                     gh[t][:, cols], k1[:, t, cols], half_gain[:, t : t + 1], gy[t][:, cols], MULT, ADD
                 )
 
-        def partial(cols):
+        def partial(half, tag):
+            cols = slice(half * S // 2, (half + 1) * S // 2)
+            part = keep.tile([P, PACK, S // 2], F32, name=f"part{half}", tag=tag, align_bytes=64)
             for t in range(PACK):
-                nc.vector.scalar_tensor_tensor(part[:, t, cols], k1[:, t, cols], 0.25, y[t][:, cols], MULT, ADD)
+                nc.vector.scalar_tensor_tensor(part[:, t, :], k1[:, t, cols], 0.25, y[t, half], MULT, ADD)
+            return part
 
-        midpoint(slice(0, S // 2))
-        partial(slice(0, S // 2))
-        midpoint(slice(S // 2, S))
-        velocity("end", gh, k2, lambda: partial(slice(S // 2, S)))
+        midpoint(0)
+        part = partial(0, "part0")
+        for c in range(1, NCH):
+            midpoint(c)
+        velocity("end", gh, k2, nc.vector.tensor_copy)
 
         out_rows = out_0.rearrange("(p t) s -> p t s", t=PACK)
         out_words = out_1[0].rearrange("p n r -> p (n r)").bitcast(I32)
@@ -177,12 +187,16 @@ def tile_picked_heun_none_po_kernel(
         out_scales = keep.tile([P, S], U8, name="out_scales", align_bytes=64)
         for c in range(NCH):
             cols = slice(c * CH, (c + 1) * CH)
-            if c < 2:
-                result = ring.tile([P, PACK, CH], F32, name=f"result{c}", tag="rows", align_bytes=64)
-            else:
-                result = keep.tile([P, PACK, CH], F32, name=f"result{c}")
+            part_cols = slice(c % 2 * CH, (c % 2 + 1) * CH)
+            if c == 2:
+                part = partial(1, "end_late")
+            result = keep.tile([P, PACK, CH], F32, name=f"result{c}")
             rounded = keep.tile([P, PACK * CH], BF16, name=f"rounded{c}", align_bytes=64)
-            nc.vector.scalar_tensor_tensor(result[:], k2[:, :, cols], 0.25, part[:, :, cols], MULT, ADD)
+            if c < NCH - 1:
+                nc.vector.scalar_tensor_tensor(result[:], k2[:, :, cols], 0.25, part[:, :, part_cols], MULT, ADD)
+            else:
+                for t in range(PACK):
+                    nc.vector.scalar_tensor_tensor(result[:, t, :], k2[:, t, cols], 0.25, part[:, t, part_cols], MULT, ADD)
             nc.sync.dma_start(out_rows[:, :, cols], result[:])
             weave(nc.scalar.copy if c < NCH - 1 else nc.vector.tensor_copy, rounded[:], result[:])
             nc.vector.quantize_mx(out=out_codes[:, cols].bitcast(FP8X4), scales=out_scales[:, cols], in_=rounded[:])

@@ -21,12 +21,12 @@ P = 128
 PACK = 4
 CH = 128
 NCH = S // CH
-X_FIRST = 640
+X_FIRST = 1536
 
 
 def load_scale_rows(queue, plane, scales):
-    for q in range(4):
-        queue.dma_start(plane[32 * q : 32 * q + 4, :].bitcast(I32), scales[0, 4 * q : 4 * q + 4, :].bitcast(I32))
+    for r in range(4):
+        queue.dma_start(plane[r:P:32, :].bitcast(I32), scales[0, r:16:4, :].bitcast(I32))
 
 
 def deal_words(eng, dealt, raw):
@@ -77,10 +77,10 @@ def tile_picked_heun_none_po_kernel(
         x_view = x_words[0].rearrange("p n r -> p (n r)").bitcast(I32)
         nc.sync.dma_start(offs_sb[:], offs)
         nc.sync.dma_start(w1w_raw[:].bitcast(I32), w1_words[0].bitcast(I32))
-        nc.sync.dma_start(xw[:, :X_FIRST].bitcast(I32), x_view[:, :X_FIRST])
         load_scale_rows(nc.sync, xs, x_scales)
-        nc.sync.dma_start(xw[:, X_FIRST:].bitcast(I32), x_view[:, X_FIRST:])
+        nc.sync.dma_start(xw[:, :X_FIRST].bitcast(I32), x_view[:, :X_FIRST])
         load_scale_rows(nc.sync, w1s_raw, w1_scales)
+        nc.sync.dma_start(xw[:, X_FIRST:].bitcast(I32), x_view[:, X_FIRST:])
         nc.sync.dma_start(gain[:], gn.rearrange("(p t) o -> p (t o)", t=PACK))
         nc.sync.dma_start(nb_sb[:], nb)
         nc.sync.dma_start(w2w_raw[:].bitcast(I32), w2_words[0].bitcast(I32))
@@ -96,8 +96,8 @@ def tile_picked_heun_none_po_kernel(
         nc.scalar.activation(half_gain[:], gain[:], ACT.Copy, scale=0.5)
         deal_words(nc.vector, w1w, w1w_raw)
         nc.vector.tensor_copy(xqs[:], xs[:].indirect(offs_sb[:]))
-        nc.vector.tensor_copy(xqw[0][:], xw[:].indirect(offs_sb[:, : S // 32]))
         deal_scales(nc.vector, w1s, w1s_raw)
+        nc.vector.tensor_copy(xqw[0][:], xw[:].indirect(offs_sb[:, : S // 32]))
         nc.vector.tensor_copy(xqw[1][:], xw[:].indirect(offs_sb[:, S // 32 :]))
         deal_words(nc.vector, w2w, w2w_raw)
         deal_scales(nc.vector, w2s, w2s_raw)
@@ -200,7 +200,9 @@ def tile_picked_heun_none_po_kernel(
             nc.sync.dma_start(out_rows[:, :, cols], result[:])
             weave(nc.scalar.copy if c < NCH - 1 else nc.vector.tensor_copy, rounded[:], result[:])
             nc.vector.quantize_mx(out=out_codes[:, cols].bitcast(FP8X4), scales=out_scales[:, cols], in_=rounded[:])
-            nc.sync.dma_start(out_words[:, cols], out_codes[:, cols].bitcast(I32))
+            if c % 2 == 1:
+                both = slice((c - 1) * CH, (c + 1) * CH)
+                nc.sync.dma_start(out_words[:, both], out_codes[:, both].bitcast(I32))
         for q in range(4):
             queue = nc.sync if q % 2 == 0 else nc.scalar
             queue.dma_start(out_2[0, 4 * q : 4 * q + 4, :].bitcast(I32), out_scales[32 * q : 32 * q + 4, :].bitcast(I32))

@@ -129,15 +129,17 @@ def tile_picked_heun_none_po_kernel(
         def velocity(name, windows, k, last_copy):
             woven = {}
 
-            def fetch(c):
-                tag = {2: f"{name}_late", 3: f"{name}_rows1"}.get(c, f"{name}_rows{c}")
-                rows = keep.tile([P, PACK, CH], BF16, name=f"{name}_rows{c}", tag=tag, align_bytes=64)
+            def fetch(first, n):
+                tag = {2: f"{name}_late", 3: f"{name}_rows0"}.get(first, f"{name}_rows{first}")
+                rows = keep.tile([P, PACK, n * CH], BF16, name=f"{name}_rows{first}", tag=tag, align_bytes=64)
                 for t in range(PACK):
                     nc.vector.tensor_copy(
-                        rows[:, t, :], windows[t][:].indirect(nb_sb[:, c * CH // 16 : (c + 1) * CH // 16])
+                        rows[:, t, :], windows[t][:].indirect(nb_sb[:, first * CH // 16 : (first + n) * CH // 16])
                     )
-                woven[c] = keep.tile([P, PACK * CH], BF16, name=f"{name}_woven{c}", align_bytes=64)
-                weave(last_copy if c == NCH - 1 else nc.scalar.copy, woven[c][:], rows[:])
+                for c in range(first, first + n):
+                    woven[c] = keep.tile([P, PACK * CH], BF16, name=f"{name}_woven{c}", align_bytes=64)
+                    piece = rows[:, :, (c - first) * CH : (c - first + 1) * CH]
+                    weave(last_copy if c == NCH - 1 else nc.scalar.copy, woven[c][:], piece)
 
             def multiply(c):
                 cols = slice(c * CH, (c + 1) * CH)
@@ -148,12 +150,11 @@ def tile_picked_heun_none_po_kernel(
                     product(acc[t][:, cols], w2w, w2s, t, codes[:], scales[:])
                     nc.scalar.activation(k[:, t, cols], acc[t][:, cols], ACT.Tanh)
 
-            fetch(0)
-            fetch(1)
-            fetch(2)
+            fetch(0, 2)
+            fetch(2, 1)
             multiply(0)
             multiply(1)
-            fetch(3)
+            fetch(3, 1)
             multiply(2)
             multiply(3)
 

@@ -1,6 +1,7 @@
 from contextlib import ExitStack
 
 import concourse.mybir as mybir
+from concourse.masks import make_identity
 
 K, T, S, H = 512, 2048, 512, 512
 FLOPS = 3 * 2 * 512 * 512 * 512
@@ -66,13 +67,16 @@ def tile_picked_heun_none_po_kernel(
         w2w_raw = keep.tile([P, 2 * H], U8, name="w2w_raw", align_bytes=64)
         w1s_raw = keep.tile([P, H], U8, name="w1s_raw", align_bytes=64)
         w2s_raw = keep.tile([P, H], U8, name="w2s_raw", align_bytes=64)
-        gain = keep.tile([P, PACK], F32, name="gain", tag="start_late", align_bytes=64)
-        half_gain = keep.tile([P, PACK], F32, name="half_gain", tag="end_late", align_bytes=64)
+        gain = keep.tile([P, PACK], F32, name="gain", tag="late1", align_bytes=64)
+        half_gain = keep.tile([P, PACK], F32, name="half_gain", tag="late2", align_bytes=64)
 
         nc.gpsimd.memset(xs[:, : T // 2].bitcast(I32), 0)
         nc.vector.memset(xs[:, T // 2 :].bitcast(I32), 0)
         nc.vector.memset(w1s_raw[:].bitcast(I32), 0)
         nc.vector.memset(w2s_raw[:].bitcast(I32), 0)
+
+        identity = keep.tile([P, P], F32, name="identity", align_bytes=64)
+        make_identity(nc, identity[:])
 
         x_view = x_words[0].rearrange("p n r -> p (n r)").bitcast(I32)
         nc.sync.dma_start(offs_sb[:], offs)
@@ -113,97 +117,190 @@ def tile_picked_heun_none_po_kernel(
                 stop=True,
             )
 
-        y_banks = [psum.tile([P, 2, S // 2], F32, name=f"y_bank{b}") for b in range(PACK)]
-        y = {(t, half): y_banks[2 * half + t % 2][:, t // 2, :] for t in range(PACK) for half in range(2)}
-        acc = [psum.tile([P, S], F32, name=f"acc{t}") for t in range(PACK)]
+        def turn(acc, block, start=False, stop=False):
+            nc.tensor.matmul(acc, block, identity[:], is_transpose=True, start=start, stop=stop)
+
+        banks = [psum.tile([P, S], F32, name=f"bank{b}") for b in range(8)]
+        HALF = S // 2
+        y = {
+            (t, half): banks[2 * half + t % 2][:, t // 2 * HALF : (t // 2 + 1) * HALF]
+            for t in range(PACK)
+            for half in range(2)
+        }
         gy = [keep.tile([P, S], F32, name=f"gy{t}") for t in range(PACK)]
         gh = [keep.tile([P, S], F32, name=f"gh{t}") for t in range(PACK)]
+        k = {v: keep.tile([P, PACK, S], F32, name=f"k{v}") for v in (1, 2)}
+        windows = {1: gy, 2: gh}
+        rows, woven, codes, scales, part, result, rounded = {}, {}, {}, {}, {}, {}, {}
 
-        for pair in range(0, PACK, 2):
-            for half in range(2):
-                cols = slice(half * S // 2, (half + 1) * S // 2)
-                for t in (pair, pair + 1):
-                    product(y[t, half], w1w, w1s, t, xqw[half][:], xqs[:, cols])
-                    nc.scalar.activation(gy[t][:, cols], y[t, half], ACT.Copy, scale=gain[:, t : t + 1])
+        def state(t, half):
+            cols = slice(half * HALF, (half + 1) * HALF)
+            product(y[t, half], w1w, w1s, t, xqw[half][:], xqs[:, cols])
+            nc.scalar.activation(gy[t][:, cols], y[t, half], ACT.Copy, scale=gain[:, t : t + 1])
 
-        def velocity(name, windows, k, last_copy):
-            woven = {}
+        four_y = keep.tile([P, PACK, HALF], F32, name="four_y", align_bytes=64)
 
-            def fetch(first, n):
-                tag = {2: f"{name}_late", 3: f"{name}_rows0"}.get(first, f"{name}_rows{first}")
-                rows = keep.tile([P, PACK, n * CH], BF16, name=f"{name}_rows{first}", tag=tag, align_bytes=64)
-                for t in range(PACK):
-                    nc.vector.tensor_copy(
-                        rows[:, t, :], windows[t][:].indirect(nb_sb[:, first * CH // 16 : (first + n) * CH // 16])
-                    )
-                for c in range(first, first + n):
-                    woven[c] = keep.tile([P, PACK * CH], BF16, name=f"{name}_woven{c}", align_bytes=64)
-                    piece = rows[:, :, (c - first) * CH : (c - first + 1) * CH]
-                    weave(last_copy if c == NCH - 1 else nc.scalar.copy, woven[c][:], piece)
+        def keep_state(odd):
+            pair = banks[2 + odd][:].rearrange("p (t s) -> p t s", t=2)
+            nc.scalar.activation(four_y[:, odd:PACK:2, :], pair, ACT.Copy, scale=4.0)
 
-            def multiply(c):
-                cols = slice(c * CH, (c + 1) * CH)
-                codes = keep.tile([P, CH], U32, name=f"{name}_codes{c}", align_bytes=64)
-                scales = keep.tile([P, CH], U8, name=f"{name}_scales{c}", align_bytes=64)
-                nc.vector.quantize_mx(out=codes[:].bitcast(FP8X4), scales=scales[:], in_=woven[c][:])
-                for t in range(PACK):
-                    product(acc[t][:, cols], w2w, w2s, t, codes[:], scales[:])
-                    nc.scalar.activation(k[:, t, cols], acc[t][:, cols], ACT.Tanh)
-
-            fetch(0, 2)
-            fetch(2, 1)
-            multiply(0)
-            multiply(1)
-            fetch(3, 1)
-            multiply(2)
-            multiply(3)
-
-        k1 = keep.tile([P, PACK, S], F32, name="k1")
-        k2 = keep.tile([P, PACK, S], F32, name="k2")
-        velocity("start", gy, k1, nc.scalar.copy)
-
-        def midpoint(c):
-            cols = slice(c * CH, (c + 1) * CH)
-            for t in range(PACK):
-                nc.vector.scalar_tensor_tensor(
-                    gh[t][:, cols], k1[:, t, cols], half_gain[:, t : t + 1], gy[t][:, cols], MULT, ADD
+        def fetch(v, c, ts=range(PACK), tag=None):
+            if (v, c) not in rows:
+                rows[v, c] = keep.tile([P, PACK, CH], BF16, name=f"rows{v}_{c}", tag=tag or f"rows{v}_{c}", align_bytes=64)
+            for t in ts:
+                nc.vector.tensor_copy(
+                    rows[v, c][:, t, :], windows[v][t][:].indirect(nb_sb[:, c * CH // 16 : (c + 1) * CH // 16])
                 )
 
-        def partial(half, tag):
-            cols = slice(half * S // 2, (half + 1) * S // 2)
-            part = keep.tile([P, PACK, S // 2], F32, name=f"part{half}", tag=tag, align_bytes=64)
-            for t in range(PACK):
-                nc.vector.scalar_tensor_tensor(part[:, t, :], k1[:, t, cols], 0.25, y[t, half], MULT, ADD)
-            return part
+        def interleave(v, c, copy, tag=None):
+            if (v, c) not in woven:
+                woven[v, c] = keep.tile([P, PACK * CH], BF16, name=f"woven{v}_{c}", tag=tag or f"woven{v}_{c}", align_bytes=64)
+            weave(copy, woven[v, c][:], rows[v, c][:])
 
-        midpoint(0)
-        part = partial(0, "part0")
-        for c in range(1, NCH):
-            midpoint(c)
-        velocity("end", gh, k2, nc.vector.tensor_copy)
+        def quantise(v, c):
+            codes[v, c] = keep.tile([P, CH], U32, name=f"codes{v}_{c}", align_bytes=64)
+            scales[v, c] = keep.tile([P, CH], U8, name=f"scales{v}_{c}", align_bytes=64)
+            nc.vector.quantize_mx(out=codes[v, c][:].bitcast(FP8X4), scales=scales[v, c][:], in_=woven[v, c][:])
+
+        def plain_product(v, c, t, bank, at):
+            product(banks[bank][:, at * CH : (at + 1) * CH], w2w, w2s, t, codes[v, c][:], scales[v, c][:])
+
+        def plain_tanh(v, c, t, bank, at, n=1):
+            near = slice(c * CH, (c + 1) * CH)
+            nc.scalar.activation(
+                k[v][:, t : t + n, near],
+                banks[bank][:, at * CH : (at + n) * CH].rearrange("p (t c) -> p t c", t=n),
+                ACT.Tanh,
+            )
+
+        def midpoint(c, t):
+            nc.vector.scalar_tensor_tensor(
+                gh[t][:, c * CH : (c + 1) * CH],
+                k[1][:, t, c * CH : (c + 1) * CH],
+                half_gain[:, t : t + 1],
+                gy[t][:, c * CH : (c + 1) * CH],
+                MULT,
+                ADD,
+            )
+
+        def open_partial(c):
+            near = slice(c % 2 * CH, (c % 2 + 1) * CH)
+            for t in range(PACK):
+                turn(banks[c][:, t * CH : (t + 1) * CH], four_y[:, t, near], start=(t == 0))
+
+        def close_partial(c):
+            cols = slice(c * CH, (c + 1) * CH)
+            for t in reversed(range(PACK)):
+                turn(banks[c][:, t * CH : (t + 1) * CH], k[1][:, t, cols], stop=(t == 0))
+            turned = keep.tile([P, PACK, P], F32, name=f"turned{c}", align_bytes=64)
+            nc.scalar.activation(turned[:].rearrange("p t c -> p (t c)"), banks[c][:], ACT.Copy, scale=0.25)
+            for t in range(PACK):
+                turn(banks[c - 2][:, t * CH : (t + 1) * CH], turned[:, t, :], start=(t == 0), stop=(t == PACK - 1))
+            part[c] = banks[c - 2][:].rearrange("p (t c) -> p t c", t=PACK)
+
+        def partial(c):
+            sums = keep.tile([P, PACK, CH], F32, name=f"part{c}", align_bytes=64)
+            part[c] = sums[:]
+            for odd in range(2):
+                pair = banks[odd][:].rearrange("p (t s) -> p t s", t=2)[:, :, c * CH : (c + 1) * CH]
+                nc.vector.scalar_tensor_tensor(
+                    part[c][:, odd:PACK:2, :], k[1][:, odd:PACK:2, c * CH : (c + 1) * CH], 0.25, pair, MULT, ADD
+                )
+
+        def multiply(v, c, into):
+            quantise(v, c)
+            n = PACK // len(into)
+            for t in range(PACK):
+                plain_product(v, c, t, into[t // n], t % n)
+                if t % n == n - 1:
+                    plain_tanh(v, c, t - n + 1, into[t // n], 0, n)
 
         out_rows = out_0.rearrange("(p t) s -> p t s", t=PACK)
         out_words = out_1[0].rearrange("p n r -> p (n r)").bitcast(I32)
         out_codes = keep.tile([P, S], U32, name="out_codes", align_bytes=64)
         out_scales = keep.tile([P, S], U8, name="out_scales", align_bytes=64)
-        for c in range(NCH):
+
+        def finish(c, tag=None):
             cols = slice(c * CH, (c + 1) * CH)
-            part_cols = slice(c % 2 * CH, (c % 2 + 1) * CH)
-            if c == 2:
-                part = partial(1, "end_late")
-            result = keep.tile([P, PACK, CH], F32, name=f"result{c}")
-            rounded = keep.tile([P, PACK * CH], BF16, name=f"rounded{c}", align_bytes=64)
+            result[c] = keep.tile([P, PACK, CH], F32, name=f"result{c}", tag=tag or f"result{c}", align_bytes=64)
             if c < NCH - 1:
-                nc.vector.scalar_tensor_tensor(result[:], k2[:, :, cols], 0.25, part[:, :, part_cols], MULT, ADD)
+                nc.vector.scalar_tensor_tensor(result[c][:], k[2][:, :, cols], 0.25, part[c], MULT, ADD)
             else:
                 for t in range(PACK):
-                    nc.vector.scalar_tensor_tensor(result[:, t, :], k2[:, t, cols], 0.25, part[:, t, part_cols], MULT, ADD)
-            nc.sync.dma_start(out_rows[:, :, cols], result[:])
-            weave(nc.scalar.copy if c < NCH - 1 else nc.vector.tensor_copy, rounded[:], result[:])
-            nc.vector.quantize_mx(out=out_codes[:, cols].bitcast(FP8X4), scales=out_scales[:, cols], in_=rounded[:])
-            if c % 2 == 1:
-                both = slice((c - 1) * CH, (c + 1) * CH)
-                nc.sync.dma_start(out_words[:, both], out_codes[:, both].bitcast(I32))
-        for q in range(4):
-            queue = nc.sync if q % 2 == 0 else nc.scalar
-            queue.dma_start(out_2[0, 4 * q : 4 * q + 4, :].bitcast(I32), out_scales[32 * q : 32 * q + 4, :].bitcast(I32))
+                    nc.vector.scalar_tensor_tensor(result[c][:, t, :], k[2][:, t, cols], 0.25, part[c][:, t, :], MULT, ADD)
+
+        def store(c):
+            nc.sync.dma_start(out_rows[:, :, c * CH : (c + 1) * CH], result[c][:])
+
+        def round_out(c, copy, tag=None):
+            rounded[c] = keep.tile([P, PACK * CH], BF16, name=f"rounded{c}", tag=tag or f"rounded{c}", align_bytes=64)
+            weave(copy, rounded[c][:], result[c][:])
+
+        def quantise_out(c):
+            cols = slice(c * CH, (c + 1) * CH)
+            nc.vector.quantize_mx(out=out_codes[:, cols].bitcast(FP8X4), scales=out_scales[:, cols], in_=rounded[c][:])
+
+        def store_words(c):
+            both = slice((c - 1) * CH, (c + 1) * CH)
+            nc.sync.dma_start(out_words[:, both], out_codes[:, both].bitcast(I32))
+
+        def store_scales():
+            for q in range(4):
+                queue = nc.sync if q % 2 == 0 else nc.scalar
+                queue.dma_start(out_2[0, 4 * q : 4 * q + 4, :].bitcast(I32), out_scales[32 * q : 32 * q + 4, :].bitcast(I32))
+
+        on_scalar, on_vector = nc.scalar.copy, nc.vector.tensor_copy
+
+        for pair in (0, 2):
+            for half in range(2):
+                state(pair, half)
+                state(pair + 1, half)
+        keep_state(0)
+        keep_state(1)
+        open_partial(2)
+        open_partial(3)
+        first = keep.tile([P, PACK, 2 * CH], BF16, name="rows1_1", align_bytes=64)
+        for t in range(PACK):
+            nc.vector.tensor_copy(first[:, t, :], gy[t][:].indirect(nb_sb[:, : 2 * CH // 16]))
+        for c in range(2):
+            rows[1, c] = first[:, :, c * CH : (c + 1) * CH]
+            interleave(1, c, on_scalar)
+        fetch(1, 2, tag="late1")
+        interleave(1, 2, on_scalar)
+        multiply(1, 0, (4, 5, 6, 7))
+        multiply(1, 1, (4,))
+        fetch(1, 3, tag="rows1_1")
+        interleave(1, 3, on_scalar)
+        multiply(1, 2, (5, 6))
+        multiply(1, 3, (7, 4, 5, 6))
+        for c in range(NCH):
+            for t in range(PACK):
+                midpoint(c, t)
+            if c < 2:
+                partial(c)
+        close_partial(2)
+        close_partial(3)
+        for c in range(2):
+            fetch(2, c, tag={1: "late2"}.get(c))
+            interleave(2, c, on_scalar)
+        multiply(2, 0, (4,))
+        fetch(2, 2, tag="rows2_0")
+        interleave(2, 2, on_scalar)
+        multiply(2, 1, (5,))
+        fetch(2, 3, tag="late2")
+        multiply(2, 2, (6, 7))
+        interleave(2, 3, on_vector, tag="rows2_0")
+        finish(0)
+        multiply(2, 3, (2, 3, 4, 5))
+        store(0)
+        round_out(0, on_scalar)
+        for c in range(1, NCH):
+            finish(c)
+            store(c)
+            quantise_out(c - 1)
+            if c == 2:
+                store_words(1)
+            round_out(c, on_scalar if c < NCH - 1 else on_vector)
+        quantise_out(3)
+        store_words(3)
+        store_scales()

@@ -67,7 +67,7 @@ def tile_picked_heun_none_po_kernel(
         w2w_raw = keep.tile([P, 2 * H], U8, name="w2w_raw", align_bytes=64)
         w1s_raw = keep.tile([P, H], U8, name="w1s_raw", align_bytes=64)
         w2s_raw = keep.tile([P, H], U8, name="w2s_raw", align_bytes=64)
-        gain = keep.tile([P, PACK], F32, name="gain", tag="late1", align_bytes=64)
+        gain = keep.tile([P, PACK], F32, name="gain", align_bytes=64)
         half_gain = keep.tile([P, PACK], F32, name="half_gain", tag="late2", align_bytes=64)
 
         nc.gpsimd.memset(xs[:, : T // 2].bitcast(I32), 0)
@@ -183,20 +183,22 @@ def tile_picked_heun_none_po_kernel(
                 ADD,
             )
 
-        def open_partial(c):
-            near = slice(c % 2 * CH, (c % 2 + 1) * CH)
+        def open_partial(c, bank, source):
             for t in range(PACK):
-                turn(banks[c][:, t * CH : (t + 1) * CH], four_y[:, t, near], start=(t == 0))
+                turn(banks[bank][:, t * CH : (t + 1) * CH], source[:, t, :], start=(t == 0))
 
-        def close_partial(c):
+        def close_partial(c, bank):
             cols = slice(c * CH, (c + 1) * CH)
             for t in reversed(range(PACK)):
-                turn(banks[c][:, t * CH : (t + 1) * CH], k[1][:, t, cols], stop=(t == 0))
+                turn(banks[bank][:, t * CH : (t + 1) * CH], k[1][:, t, cols], stop=(t == 0))
             turned = keep.tile([P, PACK, P], F32, name=f"turned{c}", align_bytes=64)
-            nc.scalar.activation(turned[:].rearrange("p t c -> p (t c)"), banks[c][:], ACT.Copy, scale=0.25)
+            nc.scalar.activation(turned[:].rearrange("p t c -> p (t c)"), banks[bank][:], ACT.Copy, scale=0.25)
+            return turned
+
+        def return_partial(c, bank, turned):
             for t in range(PACK):
-                turn(banks[c - 2][:, t * CH : (t + 1) * CH], turned[:, t, :], start=(t == 0), stop=(t == PACK - 1))
-            part[c] = banks[c - 2][:].rearrange("p (t c) -> p t c", t=PACK)
+                turn(banks[bank][:, t * CH : (t + 1) * CH], turned[:, t, :], start=(t == 0), stop=(t == PACK - 1))
+            part[c] = banks[bank][:].rearrange("p (t c) -> p t c", t=PACK)
 
         def partial(c):
             sums = keep.tile([P, PACK, CH], F32, name=f"part{c}", align_bytes=64)
@@ -257,29 +259,39 @@ def tile_picked_heun_none_po_kernel(
                 state(pair + 1, half)
         keep_state(0)
         keep_state(1)
-        open_partial(2)
-        open_partial(3)
-        first = keep.tile([P, PACK, 2 * CH], BF16, name="rows1_1", align_bytes=64)
+        open_partial(2, 2, four_y[:, :, :CH])
+        open_partial(3, 3, four_y[:, :, CH:])
+        shared = keep.tile([P, 3 * PACK * CH], BF16, name="shared", tag="w2s_raw", align_bytes=64)
+        first = shared[:, : 2 * PACK * CH].rearrange("p (t c) -> p t c", t=PACK)
+        rows[1, 2] = shared[:, 2 * PACK * CH :].rearrange("p (t c) -> p t c", t=PACK)
+        rows[1, 3] = shared[:, : PACK * CH].rearrange("p (t c) -> p t c", t=PACK)
         for t in range(PACK):
             nc.vector.tensor_copy(first[:, t, :], gy[t][:].indirect(nb_sb[:, : 2 * CH // 16]))
         for c in range(2):
             rows[1, c] = first[:, :, c * CH : (c + 1) * CH]
             interleave(1, c, on_scalar)
-        fetch(1, 2, tag="late1")
+        fetch(1, 2)
         interleave(1, 2, on_scalar)
         multiply(1, 0, (4, 5, 6, 7))
         multiply(1, 1, (4,))
-        fetch(1, 3, tag="rows1_1")
+        fetch(1, 3)
         interleave(1, 3, on_scalar)
         multiply(1, 2, (5, 6))
         multiply(1, 3, (7, 4, 5, 6))
         for c in range(NCH):
             for t in range(PACK):
                 midpoint(c, t)
-            if c < 2:
+            if c == 0:
                 partial(c)
-        close_partial(2)
-        close_partial(3)
+        second = keep.tile([P, PACK, CH], F32, name="second", tag="codes1_3", align_bytes=64)
+        for odd in range(2):
+            pair = banks[odd][:].rearrange("p (t s) -> p t s", t=2)[:, :, CH:]
+            nc.scalar.activation(second[:, odd:PACK:2, :], pair, ACT.Copy, scale=4.0)
+        turned = {c: close_partial(c, c) for c in (2, 3)}
+        open_partial(1, 7, second)
+        turned[1] = close_partial(1, 7)
+        for c, bank in ((2, 2), (3, 3), (1, 7)):
+            return_partial(c, bank, turned[c])
         for c in range(2):
             fetch(2, c, tag={1: "late2"}.get(c))
             interleave(2, c, on_scalar)
@@ -288,10 +300,10 @@ def tile_picked_heun_none_po_kernel(
         interleave(2, 2, on_scalar)
         multiply(2, 1, (5,))
         fetch(2, 3, tag="late2")
-        multiply(2, 2, (6, 7))
+        multiply(2, 2, (6, 0))
         interleave(2, 3, on_vector, tag="rows2_0")
         finish(0)
-        multiply(2, 3, (2, 3, 4, 5))
+        multiply(2, 3, (1, 4, 5, 6))
         store(0)
         round_out(0, on_scalar)
         for c in range(1, NCH):

@@ -187,12 +187,12 @@ def tile_picked_heun_none_po_kernel(
             for t in range(PACK):
                 turn(banks[bank][:, t * CH : (t + 1) * CH], source[:, t, :], start=(t == 0))
 
-        def close_partial(c, bank):
+        def close_partial(c, bank, scale=0.25):
             cols = slice(c * CH, (c + 1) * CH)
             for t in reversed(range(PACK)):
                 turn(banks[bank][:, t * CH : (t + 1) * CH], k[1][:, t, cols], stop=(t == 0))
             turned = keep.tile([P, PACK, P], F32, name=f"turned{c}", align_bytes=64)
-            nc.scalar.activation(turned[:].rearrange("p t c -> p (t c)"), banks[bank][:], ACT.Copy, scale=0.25)
+            nc.scalar.activation(turned[:].rearrange("p t c -> p (t c)"), banks[bank][:], ACT.Copy, scale=scale)
             return turned
 
         def return_partial(c, bank, turned):
@@ -200,22 +200,22 @@ def tile_picked_heun_none_po_kernel(
                 turn(banks[bank][:, t * CH : (t + 1) * CH], turned[:, t, :], start=(t == 0), stop=(t == PACK - 1))
             part[c] = banks[bank][:].rearrange("p (t c) -> p t c", t=PACK)
 
-        def partial(c):
-            sums = keep.tile([P, PACK, CH], F32, name=f"part{c}", align_bytes=64)
-            part[c] = sums[:]
-            for odd in range(2):
-                pair = banks[odd][:].rearrange("p (t s) -> p t s", t=2)[:, :, c * CH : (c + 1) * CH]
-                nc.vector.scalar_tensor_tensor(
-                    part[c][:, odd:PACK:2, :], k[1][:, odd:PACK:2, c * CH : (c + 1) * CH], 0.25, pair, MULT, ADD
-                )
+        def partial(c, odd, tag=None):
+            part[c, odd] = keep.tile([P, 2, CH], F32, name=f"part{c}_{odd}", tag=tag or f"part{c}_{odd}", align_bytes=64)
+            pair = banks[odd][:].rearrange("p (t s) -> p t s", t=2)[:, :, c * CH : (c + 1) * CH]
+            nc.vector.scalar_tensor_tensor(
+                part[c, odd][:], k[1][:, odd:PACK:2, c * CH : (c + 1) * CH], 0.25, pair, MULT, ADD
+            )
 
-        def multiply(v, c, into):
-            quantise(v, c)
-            n = PACK // len(into)
-            for t in range(PACK):
-                plain_product(v, c, t, into[t // n], t % n)
-                if t % n == n - 1:
-                    plain_tanh(v, c, t - n + 1, into[t // n], 0, n)
+        def multiply(v, c, into, planes):
+            if (v, c) not in codes:
+                quantise(v, c)
+            for t, bank in enumerate(into):
+                plain_product(v, c, t, bank, into[:t].count(bank))
+                if bank not in into[t + 1 :]:
+                    first_plane = into.index(bank)
+                    for u in range(first_plane, t + 1, planes):
+                        plain_tanh(v, c, u, bank, u - first_plane, min(planes, t + 1 - u))
 
         out_rows = out_0.rearrange("(p t) s -> p t s", t=PACK)
         out_words = out_1[0].rearrange("p n r -> p (n r)").bitcast(I32)
@@ -225,11 +225,12 @@ def tile_picked_heun_none_po_kernel(
         def finish(c, tag=None):
             cols = slice(c * CH, (c + 1) * CH)
             result[c] = keep.tile([P, PACK, CH], F32, name=f"result{c}", tag=tag or f"result{c}", align_bytes=64)
-            if c < NCH - 1:
-                nc.vector.scalar_tensor_tensor(result[c][:], k[2][:, :, cols], 0.25, part[c], MULT, ADD)
+            if c != 1:
+                for pair in (slice(0, 2), slice(2, 4)):
+                    nc.vector.scalar_tensor_tensor(result[c][:, pair, :], k[2][:, pair, cols], 0.25, part[c][:, pair, :], MULT, ADD)
             else:
                 for t in range(PACK):
-                    nc.vector.scalar_tensor_tensor(result[c][:, t, :], k[2][:, t, cols], 0.25, part[c][:, t, :], MULT, ADD)
+                    nc.vector.scalar_tensor_tensor(result[c][:, t, :], k[2][:, t, cols], 0.25, part[c, t % 2][:, t // 2, :], MULT, ADD)
 
         def store(c):
             nc.sync.dma_start(out_rows[:, :, c * CH : (c + 1) * CH], result[c][:])
@@ -259,60 +260,92 @@ def tile_picked_heun_none_po_kernel(
                 state(pair + 1, half)
         keep_state(0)
         keep_state(1)
+        second = keep.tile([P, PACK, CH], F32, name="second", align_bytes=64)
+
+        def keep_second(odd):
+            pair = banks[odd][:].rearrange("p (t s) -> p t s", t=2)[:, :, :CH]
+            nc.scalar.activation(second[:, odd:PACK:2, :], pair, ACT.Copy, scale=4.0)
+
+        keep_second(0)
         open_partial(2, 2, four_y[:, :, :CH])
         open_partial(3, 3, four_y[:, :, CH:])
         shared = keep.tile([P, 3 * PACK * CH], BF16, name="shared", tag="w2s_raw", align_bytes=64)
         first = shared[:, : 2 * PACK * CH].rearrange("p (t c) -> p t c", t=PACK)
-        rows[1, 2] = shared[:, 2 * PACK * CH :].rearrange("p (t c) -> p t c", t=PACK)
-        rows[1, 3] = shared[:, : PACK * CH].rearrange("p (t c) -> p t c", t=PACK)
+        rows[1, 3] = shared[:, 2 * PACK * CH :].rearrange("p (t c) -> p t c", t=PACK)
+        rows[1, 0] = shared[:, : PACK * CH].rearrange("p (t c) -> p t c", t=PACK)
         for t in range(PACK):
-            nc.vector.tensor_copy(first[:, t, :], gy[t][:].indirect(nb_sb[:, : 2 * CH // 16]))
-        for c in range(2):
-            rows[1, c] = first[:, :, c * CH : (c + 1) * CH]
+            nc.vector.tensor_copy(first[:, t, :], gy[t][:].indirect(nb_sb[:, CH // 16 : 3 * CH // 16]))
+        for c in (1, 2):
+            rows[1, c] = first[:, :, (c - 1) * CH : c * CH]
             interleave(1, c, on_scalar)
-        fetch(1, 2)
-        interleave(1, 2, on_scalar)
-        multiply(1, 0, (4, 5, 6, 7))
-        multiply(1, 1, (4,))
         fetch(1, 3)
         interleave(1, 3, on_scalar)
-        multiply(1, 2, (5, 6))
-        multiply(1, 3, (7, 4, 5, 6))
-        for c in range(NCH):
+        keep_second(1)
+        multiply(1, 1, (4, 4, 5, 5), 2)
+        quantise(1, 2)
+        fetch(1, 0)
+        interleave(1, 0, on_scalar)
+        multiply(1, 2, (6, 6, 6, 6), 2)
+        multiply(1, 3, (7, 7, 7, 7), 2)
+        multiply(1, 0, (4, 5, 6, 6), 1)
+        for c in (1, 2, 3, 0):
             for t in range(PACK):
                 midpoint(c, t)
-            if c == 0:
-                partial(c)
-        second = keep.tile([P, PACK, CH], F32, name="second", tag="codes1_3", align_bytes=64)
-        for odd in range(2):
-            pair = banks[odd][:].rearrange("p (t s) -> p t s", t=2)[:, :, CH:]
-            nc.scalar.activation(second[:, odd:PACK:2, :], pair, ACT.Copy, scale=4.0)
-        turned = {c: close_partial(c, c) for c in (2, 3)}
-        open_partial(1, 7, second)
-        turned[1] = close_partial(1, 7)
-        for c, bank in ((2, 2), (3, 3), (1, 7)):
-            return_partial(c, bank, turned[c])
-        for c in range(2):
-            fetch(2, c, tag={1: "late2"}.get(c))
-            interleave(2, c, on_scalar)
-        multiply(2, 0, (4,))
-        fetch(2, 2, tag="rows2_0")
+            if c == 1:
+                partial(1, 0)
+        turned = {2: close_partial(2, 2, 1.0), 3: close_partial(3, 3)}
+        fetch(2, 2)
         interleave(2, 2, on_scalar)
-        multiply(2, 1, (5,))
+        open_partial(0, 7, second)
+        turned[0] = close_partial(0, 7)
+        for t in range(PACK):
+            turn(banks[2][:, t * CH : (t + 1) * CH], turned[2][:, t, :], start=(t == 0))
+        return_partial(3, 3, turned[3])
         fetch(2, 3, tag="late2")
-        multiply(2, 2, (6, 0))
-        interleave(2, 3, on_vector, tag="rows2_0")
+        interleave(2, 3, on_scalar)
+        quantise(2, 2)
+        k2_turned = keep.tile([P, PACK, P], F32, name="k2_turned", align_bytes=64)
+        for u in range(2):
+            nc.tensor.matmul_mx(
+                out=banks[4 + u][:, :HALF],
+                lhsT=codes[2, 2][:].bitcast(FP8X4),
+                lhsT_scale=scales[2, 2][:],
+                rhs=w2w[:, 2 * HALF * u : 2 * HALF * (u + 1)].bitcast(FP4X4),
+                rhs_scale=w2s[:, HALF * u : HALF * (u + 1)],
+                start=True,
+                stop=True,
+            )
+            nc.scalar.activation(
+                k2_turned[:, 2 * u : 2 * u + 2, :].rearrange("p t c -> p (t c)"), banks[4 + u][:, :HALF], ACT.Tanh
+            )
+        return_partial(0, 7, turned[0])
+        fetch(2, 0, tag="rows2_2")
+        interleave(2, 0, on_scalar, tag="codes2_2")
+        for t in range(PACK):
+            turn(banks[2][:, t * CH : (t + 1) * CH], k2_turned[:, t, :], stop=(t == PACK - 1))
+        result[2] = keep.tile([P, PACK, CH], F32, name="result2", align_bytes=64)
+        nc.scalar.activation(result[2][:].rearrange("p t c -> p (t c)"), banks[2][:], ACT.Copy, scale=0.25)
+        multiply(2, 3, (5, 5, 5, 5), 2)
+        store(2)
+        fetch(2, 1, tag="late2")
+        multiply(2, 0, (6, 6, 0, 0), 2)
+        interleave(2, 1, on_vector, tag="rows2_2")
+        partial(1, 1, tag="codes2_2")
+        multiply(2, 1, (4, 5, 1, 6), 1)
+        finish(3)
+        store(3)
+        round_out(2, on_vector, tag="rows2_2")
         finish(0)
-        multiply(2, 3, (1, 4, 5, 6))
         store(0)
+        finish(1)
+        store(1)
+        round_out(3, on_scalar)
         round_out(0, on_scalar)
-        for c in range(1, NCH):
-            finish(c)
-            store(c)
-            quantise_out(c - 1)
-            if c == 2:
-                store_words(1)
-            round_out(c, on_scalar if c < NCH - 1 else on_vector)
+        round_out(1, on_vector)
+        quantise_out(2)
         quantise_out(3)
         store_words(3)
+        quantise_out(0)
+        quantise_out(1)
+        store_words(1)
         store_scales()

@@ -146,7 +146,7 @@ def tile_picked_heun_none_po_kernel(
 
         def fetch(v, c, ts=range(PACK), tag=None):
             if (v, c) not in rows:
-                rows[v, c] = keep.tile([P, PACK, CH], BF16, name=f"rows{v}_{c}", tag=tag or f"rows{v}_{c}", align_bytes=64)
+                rows[v, c] = keep.tile([P, PACK, CH], F32, name=f"rows{v}_{c}", tag=tag or f"rows{v}_{c}", align_bytes=64)
             for t in ts:
                 nc.vector.tensor_copy(
                     rows[v, c][:, t, :], windows[v][t][:].indirect(nb_sb[:, c * CH // 16 : (c + 1) * CH // 16])
@@ -269,7 +269,7 @@ def tile_picked_heun_none_po_kernel(
         keep_second(0)
         open_partial(2, 2, four_y[:, :, :CH])
         open_partial(3, 3, four_y[:, :, CH:])
-        shared = keep.tile([P, 3 * PACK * CH], BF16, name="shared", tag="w2s_raw", align_bytes=64)
+        shared = keep.tile([P, 3 * PACK * CH], F32, name="shared", tag="w2s_raw", align_bytes=64)
         first = shared[:, : 2 * PACK * CH].rearrange("p (t c) -> p t c", t=PACK)
         rows[1, 3] = shared[:, 2 * PACK * CH :].rearrange("p (t c) -> p t c", t=PACK)
         rows[1, 0] = shared[:, : PACK * CH].rearrange("p (t c) -> p t c", t=PACK)

@@ -3,7 +3,7 @@ from contextlib import ExitStack
 import concourse.mybir as mybir
 from concourse.masks import make_identity
 
-K, T, S, H = 512, 2048, 512, 512
+T, S, H = 2048, 512, 512
 FLOPS = 3 * 2 * 512 * 512 * 512
 
 F32 = mybir.dt.float32
@@ -19,35 +19,33 @@ ADD = mybir.AluOpType.add
 ACT = mybir.ActivationFunctionType
 
 P = 128
-PACK = 4
+PLANES = 4
 CH = 128
-NCH = S // CH
-X_FIRST = 1536
+HALF = S // 2
+PER_COLUMN = 16
+X_FIRST = 3 * T // 4
 
 
-def load_scale_rows(queue, plane, scales):
+def chunk(c):
+    return slice(c * CH, (c + 1) * CH)
+
+
+def load_scale_rows(nc, tile, scales):
     for r in range(4):
-        queue.dma_start(plane[r:P:32, :].bitcast(I32), scales[0, r:16:4, :].bitcast(I32))
+        nc.sync.dma_start(tile[r:P:32, :].bitcast(I32), scales[0, r:16:4, :].bitcast(I32))
 
 
-def deal_words(eng, dealt, raw):
-    eng.tensor_copy(
-        dealt[:].rearrange("p (t m b) -> p t m b", t=PACK, b=2),
-        raw[:].rearrange("p (m t b) -> p t m b", t=PACK, b=2),
+def deal(nc, dealt, raw):
+    nc.vector.tensor_copy(
+        dealt.rearrange("p (t m) -> p t m", t=PLANES),
+        raw.rearrange("p (m t) -> p t m", t=PLANES),
     )
 
 
-def deal_scales(eng, dealt, raw):
-    eng.tensor_copy(
-        dealt[:].rearrange("p (t m) -> p t m", t=PACK),
-        raw[:].rearrange("p (m t) -> p t m", t=PACK),
-    )
-
-
-def weave(copy, woven, rows):
+def weave(copy, woven, planes):
     copy(
-        woven.rearrange("p (c i t) -> p c t i", i=4, t=PACK),
-        rows.rearrange("p t (c i) -> p c t i", i=4),
+        woven.rearrange("p (c i t) -> p c t i", i=4, t=PLANES),
+        planes.rearrange("p t (c i) -> p c t i", i=4),
     )
 
 
@@ -59,293 +57,269 @@ def tile_picked_heun_none_po_kernel(
         keep = ctx.enter_context(tc.tile_pool(name="keep", bufs=1))
         psum = ctx.enter_context(tc.psum_pool(name="psum", bufs=1))
 
-        offs_sb = keep.tile([P, S // 16], U16, name="offs_sb")
-        nb_sb = keep.tile([P, S // 16], U16, name="nb_sb")
-        xw = keep.tile([P, T], U32, name="xw", align_bytes=64)
-        xs = keep.tile([P, T], U8, name="xs", align_bytes=64)
-        w1w_raw = keep.tile([P, 2 * H], U8, name="w1w_raw", align_bytes=64)
-        w2w_raw = keep.tile([P, 2 * H], U8, name="w2w_raw", align_bytes=64)
-        w1s_raw = keep.tile([P, H], U8, name="w1s_raw", align_bytes=64)
-        w2s_raw = keep.tile([P, H], U8, name="w2s_raw", align_bytes=64)
-        gain = keep.tile([P, PACK], F32, name="gain", align_bytes=64)
-        half_gain = keep.tile([P, PACK], F32, name="half_gain", tag="late2", align_bytes=64)
+        def sbuf(name, shape, dtype, after=None):
+            return keep.tile(shape, dtype, name=name, tag=after or name, align_bytes=64)
+
+        offs_sb = keep.tile([P, S // PER_COLUMN], U16, name="offs_sb")
+        nb_sb = keep.tile([P, S // PER_COLUMN], U16, name="nb_sb")
+        xw = sbuf("xw", [P, T], U32)
+        xs = sbuf("xs", [P, T], U8)
+        w1w_raw = sbuf("w1w_raw", [P, 2 * H], U8)
+        w2w_raw = sbuf("w2w_raw", [P, 2 * H], U8)
+        w1s_raw = sbuf("w1s_raw", [P, H], U8)
+        w2s_raw = sbuf("w2s_raw", [P, H], U8)
+        gain = sbuf("gain", [P, PLANES], F32)
+        half_gain = sbuf("half_gain", [P, PLANES], F32)
 
         nc.gpsimd.memset(xs[:, : T // 2].bitcast(I32), 0)
         nc.vector.memset(xs[:, T // 2 :].bitcast(I32), 0)
         nc.vector.memset(w1s_raw[:].bitcast(I32), 0)
         nc.vector.memset(w2s_raw[:].bitcast(I32), 0)
 
-        identity = keep.tile([P, P], F32, name="identity", align_bytes=64)
+        identity = sbuf("identity", [P, P], F32)
         make_identity(nc, identity[:])
 
         x_view = x_words[0].rearrange("p n r -> p (n r)").bitcast(I32)
         nc.sync.dma_start(offs_sb[:], offs)
         nc.sync.dma_start(w1w_raw[:].bitcast(I32), w1_words[0].bitcast(I32))
-        load_scale_rows(nc.sync, xs, x_scales)
+        load_scale_rows(nc, xs, x_scales)
         nc.sync.dma_start(xw[:, :X_FIRST].bitcast(I32), x_view[:, :X_FIRST])
-        load_scale_rows(nc.sync, w1s_raw, w1_scales)
+        load_scale_rows(nc, w1s_raw, w1_scales)
         nc.sync.dma_start(xw[:, X_FIRST:].bitcast(I32), x_view[:, X_FIRST:])
-        nc.sync.dma_start(gain[:], gn.rearrange("(p t) o -> p (t o)", t=PACK))
+        nc.sync.dma_start(gain[:], gn.rearrange("(p t) o -> p (t o)", t=PLANES))
         nc.sync.dma_start(nb_sb[:], nb)
         nc.sync.dma_start(w2w_raw[:].bitcast(I32), w2_words[0].bitcast(I32))
-        load_scale_rows(nc.sync, w2s_raw, w2_scales)
+        load_scale_rows(nc, w2s_raw, w2_scales)
 
-        w1w = keep.tile([P, 2 * H], U8, name="w1w", align_bytes=64)
-        w2w = keep.tile([P, 2 * H], U8, name="w2w", align_bytes=64)
-        w1s = keep.tile([P, H], U8, name="w1s", align_bytes=64)
-        w2s = keep.tile([P, H], U8, name="w2s", align_bytes=64)
-        xqw = [keep.tile([P, S // 2], U32, name=f"xqw{half}", align_bytes=64) for half in range(2)]
-        xqs = keep.tile([P, S], U8, name="xqs", align_bytes=64)
+        w1w = sbuf("w1w", [P, 2 * H], U8)
+        w2w = sbuf("w2w", [P, 2 * H], U8)
+        w1s = sbuf("w1s", [P, H], U8)
+        w2s = sbuf("w2s", [P, H], U8)
+        xqw = [sbuf(f"xqw{half}", [P, HALF], U32) for half in range(2)]
+        xqs = sbuf("xqs", [P, S], U8)
 
         nc.scalar.activation(half_gain[:], gain[:], ACT.Copy, scale=0.5)
-        deal_words(nc.vector, w1w, w1w_raw)
+        deal(nc, w1w[:].bitcast(U16), w1w_raw[:].bitcast(U16))
         nc.vector.tensor_copy(xqs[:], xs[:].indirect(offs_sb[:]))
-        deal_scales(nc.vector, w1s, w1s_raw)
-        nc.vector.tensor_copy(xqw[0][:], xw[:].indirect(offs_sb[:, : S // 32]))
-        nc.vector.tensor_copy(xqw[1][:], xw[:].indirect(offs_sb[:, S // 32 :]))
-        deal_words(nc.vector, w2w, w2w_raw)
-        deal_scales(nc.vector, w2s, w2s_raw)
+        deal(nc, w1s[:], w1s_raw[:])
+        for half in range(2):
+            entries = slice(half * HALF // PER_COLUMN, (half + 1) * HALF // PER_COLUMN)
+            nc.vector.tensor_copy(xqw[half][:], xw[:].indirect(offs_sb[:, entries]))
+        deal(nc, w2w[:].bitcast(U16), w2w_raw[:].bitcast(U16))
+        deal(nc, w2s[:], w2s_raw[:])
 
-        def product(acc, words, scales, t, codes, code_scales):
+        banks = [psum.tile([P, S], F32, name=f"bank{b}") for b in range(8)]
+        gy = [keep.tile([P, S], F32, name=f"gy{t}") for t in range(PLANES)]
+        gh = [keep.tile([P, S], F32, name=f"gh{t}") for t in range(PLANES)]
+        windows = {1: gy, 2: gh}
+        k = {v: keep.tile([P, PLANES, S], F32, name=f"k{v}") for v in (1, 2)}
+        rows, woven, codes, scales, result, rounded = {}, {}, {}, {}, {}, {}
+        on_scalar, on_vector = nc.scalar.copy, nc.vector.tensor_copy
+
+        def product(acc, words, word_scales, t, moving, moving_scales):
             nc.tensor.matmul_mx(
                 out=acc,
                 lhsT=words[:, 2 * P * t : 2 * P * (t + 1)].bitcast(FP4X4),
-                lhsT_scale=scales[:, P * t : P * (t + 1)],
-                rhs=codes.bitcast(FP8X4),
-                rhs_scale=code_scales,
+                lhsT_scale=word_scales[:, P * t : P * (t + 1)],
+                rhs=moving.bitcast(FP8X4),
+                rhs_scale=moving_scales,
                 start=True,
                 stop=True,
             )
 
-        def turn(acc, block, start=False, stop=False):
-            nc.tensor.matmul(acc, block, identity[:], is_transpose=True, start=start, stop=stop)
-
-        banks = [psum.tile([P, S], F32, name=f"bank{b}") for b in range(8)]
-        HALF = S // 2
-        y = {
-            (t, half): banks[2 * half + t % 2][:, t // 2 * HALF : (t // 2 + 1) * HALF]
-            for t in range(PACK)
-            for half in range(2)
-        }
-        gy = [keep.tile([P, S], F32, name=f"gy{t}") for t in range(PACK)]
-        gh = [keep.tile([P, S], F32, name=f"gh{t}") for t in range(PACK)]
-        k = {v: keep.tile([P, PACK, S], F32, name=f"k{v}") for v in (1, 2)}
-        windows = {1: gy, 2: gh}
-        rows, woven, codes, scales, part, result, rounded = {}, {}, {}, {}, {}, {}, {}
+        def state_planes(half, odd):
+            return banks[2 * half + odd][:].rearrange("p (t s) -> p t s", t=2)
 
         def state(t, half):
             cols = slice(half * HALF, (half + 1) * HALF)
-            product(y[t, half], w1w, w1s, t, xqw[half][:], xqs[:, cols])
-            nc.scalar.activation(gy[t][:, cols], y[t, half], ACT.Copy, scale=gain[:, t : t + 1])
+            acc = state_planes(half, t % 2)[:, t // 2, :]
+            product(acc, w1w, w1s, t, xqw[half][:], xqs[:, cols])
+            nc.scalar.activation(gy[t][:, cols], acc, ACT.Copy, scale=gain[:, t : t + 1])
 
-        four_y = keep.tile([P, PACK, HALF], F32, name="four_y", align_bytes=64)
+        def keep_state(tile, half, odd):
+            width = tile[:].shape[2]
+            nc.scalar.activation(tile[:, odd:PLANES:2, :], state_planes(half, odd)[:, :, :width], ACT.Copy, scale=4.0)
 
-        def keep_state(odd):
-            pair = banks[2 + odd][:].rearrange("p (t s) -> p t s", t=2)
-            nc.scalar.activation(four_y[:, odd:PACK:2, :], pair, ACT.Copy, scale=4.0)
+        def gather(into, v, first, last):
+            entries = nb_sb[:, first * CH // PER_COLUMN : last * CH // PER_COLUMN]
+            for t in range(PLANES):
+                nc.vector.tensor_copy(into[:, t, :], windows[v][t][:].indirect(entries))
 
-        def fetch(v, c, ts=range(PACK), tag=None):
-            if (v, c) not in rows:
-                rows[v, c] = keep.tile([P, PACK, CH], F32, name=f"rows{v}_{c}", tag=tag or f"rows{v}_{c}", align_bytes=64)
-            for t in ts:
-                nc.vector.tensor_copy(
-                    rows[v, c][:, t, :], windows[v][t][:].indirect(nb_sb[:, c * CH // 16 : (c + 1) * CH // 16])
-                )
+        def fetch(v, c, after=None):
+            rows[v, c] = sbuf(f"rows{v}_{c}", [P, PLANES, CH], F32, after)[:]
+            gather(rows[v, c], v, c, c + 1)
 
-        def interleave(v, c, copy, tag=None):
-            if (v, c) not in woven:
-                woven[v, c] = keep.tile([P, PACK * CH], BF16, name=f"woven{v}_{c}", tag=tag or f"woven{v}_{c}", align_bytes=64)
-            weave(copy, woven[v, c][:], rows[v, c][:])
+        def interleave(v, c, copy, after=None):
+            woven[v, c] = sbuf(f"woven{v}_{c}", [P, PLANES * CH], BF16, after)
+            weave(copy, woven[v, c][:], rows[v, c])
 
         def quantise(v, c):
-            codes[v, c] = keep.tile([P, CH], U32, name=f"codes{v}_{c}", align_bytes=64)
-            scales[v, c] = keep.tile([P, CH], U8, name=f"scales{v}_{c}", align_bytes=64)
+            codes[v, c] = sbuf(f"codes{v}_{c}", [P, CH], U32)
+            scales[v, c] = sbuf(f"scales{v}_{c}", [P, CH], U8)
             nc.vector.quantize_mx(out=codes[v, c][:].bitcast(FP8X4), scales=scales[v, c][:], in_=woven[v, c][:])
 
-        def plain_product(v, c, t, bank, at):
-            product(banks[bank][:, at * CH : (at + 1) * CH], w2w, w2s, t, codes[v, c][:], scales[v, c][:])
-
-        def plain_tanh(v, c, t, bank, at, n=1):
-            near = slice(c * CH, (c + 1) * CH)
-            nc.scalar.activation(
-                k[v][:, t : t + n, near],
-                banks[bank][:, at * CH : (at + n) * CH].rearrange("p (t c) -> p t c", t=n),
-                ACT.Tanh,
-            )
-
-        def midpoint(c, t):
-            nc.vector.scalar_tensor_tensor(
-                gh[t][:, c * CH : (c + 1) * CH],
-                k[1][:, t, c * CH : (c + 1) * CH],
-                half_gain[:, t : t + 1],
-                gy[t][:, c * CH : (c + 1) * CH],
-                MULT,
-                ADD,
-            )
-
-        def open_partial(c, bank, source):
-            for t in range(PACK):
-                turn(banks[bank][:, t * CH : (t + 1) * CH], source[:, t, :], start=(t == 0))
-
-        def close_partial(c, bank, scale=0.25):
-            cols = slice(c * CH, (c + 1) * CH)
-            for t in reversed(range(PACK)):
-                turn(banks[bank][:, t * CH : (t + 1) * CH], k[1][:, t, cols], stop=(t == 0))
-            turned = keep.tile([P, PACK, P], F32, name=f"turned{c}", align_bytes=64)
-            nc.scalar.activation(turned[:].rearrange("p t c -> p (t c)"), banks[bank][:], ACT.Copy, scale=scale)
-            return turned
-
-        def return_partial(c, bank, turned):
-            for t in range(PACK):
-                turn(banks[bank][:, t * CH : (t + 1) * CH], turned[:, t, :], start=(t == 0), stop=(t == PACK - 1))
-            part[c] = banks[bank][:].rearrange("p (t c) -> p t c", t=PACK)
-
-        def partial(c, odd, tag=None):
-            part[c, odd] = keep.tile([P, 2, CH], F32, name=f"part{c}_{odd}", tag=tag or f"part{c}_{odd}", align_bytes=64)
-            pair = banks[odd][:].rearrange("p (t s) -> p t s", t=2)[:, :, c * CH : (c + 1) * CH]
-            nc.vector.scalar_tensor_tensor(
-                part[c, odd][:], k[1][:, odd:PACK:2, c * CH : (c + 1) * CH], 0.25, pair, MULT, ADD
-            )
-
-        def multiply(v, c, into, planes):
-            if (v, c) not in codes:
-                quantise(v, c)
+        def velocity(v, c, into, step):
             for t, bank in enumerate(into):
-                plain_product(v, c, t, bank, into[:t].count(bank))
+                first = into.index(bank)
+                product(banks[bank][:, chunk(t - first)], w2w, w2s, t, codes[v, c][:], scales[v, c][:])
                 if bank not in into[t + 1 :]:
-                    first_plane = into.index(bank)
-                    for u in range(first_plane, t + 1, planes):
-                        plain_tanh(v, c, u, bank, u - first_plane, min(planes, t + 1 - u))
+                    for u in range(first, t + 1, step):
+                        acc = banks[bank][:, (u - first) * CH : (u - first + step) * CH]
+                        nc.scalar.activation(
+                            k[v][:, u : u + step, chunk(c)], acc.rearrange("p (t c) -> p t c", t=step), ACT.Tanh
+                        )
 
-        out_rows = out_0.rearrange("(p t) s -> p t s", t=PACK)
+        def midpoint(c):
+            for t in range(PLANES):
+                nc.vector.scalar_tensor_tensor(
+                    gh[t][:, chunk(c)], k[1][:, t, chunk(c)], half_gain[:, t : t + 1], gy[t][:, chunk(c)], MULT, ADD
+                )
+
+        def turn(bank, planes, order=range(PLANES), start=False, stop=False):
+            for t in order:
+                nc.tensor.matmul(
+                    banks[bank][:, chunk(t)],
+                    planes[:, t, :],
+                    identity[:],
+                    is_transpose=True,
+                    start=start and t == order[0],
+                    stop=stop and t == order[-1],
+                )
+
+        def empty(name, bank, scale):
+            tile = sbuf(name, [P, PLANES, CH], F32)
+            nc.scalar.activation(tile[:].rearrange("p t c -> p (t c)"), banks[bank][:], ACT.Copy, scale=scale)
+            return tile
+
+        def add_first_velocity(c, bank, scale):
+            turn(bank, k[1][:, :, chunk(c)], order=range(PLANES - 1, -1, -1), stop=True)
+            return empty(f"turned{c}", bank, scale)
+
+        def partial(c, odd, after=None):
+            tile = sbuf(f"part{c}_{odd}", [P, 2, CH], F32, after)
+            nc.vector.scalar_tensor_tensor(
+                tile[:], k[1][:, odd:PLANES:2, chunk(c)], 0.25, state_planes(0, odd)[:, :, chunk(c)], MULT, ADD
+            )
+            return tile
+
+        out_rows = out_0.rearrange("(p t) s -> p t s", t=PLANES)
         out_words = out_1[0].rearrange("p n r -> p (n r)").bitcast(I32)
-        out_codes = keep.tile([P, S], U32, name="out_codes", align_bytes=64)
-        out_scales = keep.tile([P, S], U8, name="out_scales", align_bytes=64)
-
-        def finish(c, tag=None):
-            cols = slice(c * CH, (c + 1) * CH)
-            result[c] = keep.tile([P, PACK, CH], F32, name=f"result{c}", tag=tag or f"result{c}", align_bytes=64)
-            if c != 1:
-                for pair in (slice(0, 2), slice(2, 4)):
-                    nc.vector.scalar_tensor_tensor(result[c][:, pair, :], k[2][:, pair, cols], 0.25, part[c][:, pair, :], MULT, ADD)
-            else:
-                for t in range(PACK):
-                    nc.vector.scalar_tensor_tensor(result[c][:, t, :], k[2][:, t, cols], 0.25, part[c, t % 2][:, t // 2, :], MULT, ADD)
+        out_codes = sbuf("out_codes", [P, S], U32)
+        out_scales = sbuf("out_scales", [P, S], U8)
 
         def store(c):
-            nc.sync.dma_start(out_rows[:, :, c * CH : (c + 1) * CH], result[c][:])
+            nc.sync.dma_start(out_rows[:, :, chunk(c)], result[c][:])
 
-        def round_out(c, copy, tag=None):
-            rounded[c] = keep.tile([P, PACK * CH], BF16, name=f"rounded{c}", tag=tag or f"rounded{c}", align_bytes=64)
+        def finish(c, parts):
+            result[c] = sbuf(f"result{c}", [P, PLANES, CH], F32)
+            for planes, part in parts:
+                nc.vector.scalar_tensor_tensor(result[c][:, planes, :], k[2][:, planes, chunk(c)], 0.25, part, MULT, ADD)
+            store(c)
+
+        def pairs_of(bank):
+            planes = banks[bank][:].rearrange("p (t c) -> p t c", t=PLANES)
+            return [(pair, planes[:, pair, :]) for pair in (slice(0, 2), slice(2, 4))]
+
+        def round_out(c, copy, after=None):
+            rounded[c] = sbuf(f"rounded{c}", [P, PLANES * CH], BF16, after)
             weave(copy, rounded[c][:], result[c][:])
 
-        def quantise_out(c):
-            cols = slice(c * CH, (c + 1) * CH)
-            nc.vector.quantize_mx(out=out_codes[:, cols].bitcast(FP8X4), scales=out_scales[:, cols], in_=rounded[c][:])
+        def quantise_out(half):
+            for c in (2 * half, 2 * half + 1):
+                nc.vector.quantize_mx(
+                    out=out_codes[:, chunk(c)].bitcast(FP8X4), scales=out_scales[:, chunk(c)], in_=rounded[c][:]
+                )
+            cols = slice(half * HALF, (half + 1) * HALF)
+            nc.sync.dma_start(out_words[:, cols], out_codes[:, cols].bitcast(I32))
 
-        def store_words(c):
-            both = slice((c - 1) * CH, (c + 1) * CH)
-            nc.sync.dma_start(out_words[:, both], out_codes[:, both].bitcast(I32))
-
-        def store_scales():
-            for q in range(4):
-                queue = nc.sync if q % 2 == 0 else nc.scalar
-                queue.dma_start(out_2[0, 4 * q : 4 * q + 4, :].bitcast(I32), out_scales[32 * q : 32 * q + 4, :].bitcast(I32))
-
-        on_scalar, on_vector = nc.scalar.copy, nc.vector.tensor_copy
-
+        four_y_high = sbuf("four_y_high", [P, PLANES, HALF], F32)
         for pair in (0, 2):
             for half in range(2):
                 state(pair, half)
                 state(pair + 1, half)
-        keep_state(0)
-        keep_state(1)
-        second = keep.tile([P, PACK, CH], F32, name="second", align_bytes=64)
+        for odd in range(2):
+            keep_state(four_y_high, 1, odd)
+        four_y_0 = sbuf("four_y_0", [P, PLANES, CH], F32)
+        keep_state(four_y_0, 0, 0)
+        for c in (2, 3):
+            turn(c, four_y_high[:, :, chunk(c - 2)], start=True)
 
-        def keep_second(odd):
-            pair = banks[odd][:].rearrange("p (t s) -> p t s", t=2)[:, :, :CH]
-            nc.scalar.activation(second[:, odd:PACK:2, :], pair, ACT.Copy, scale=4.0)
-
-        keep_second(0)
-        open_partial(2, 2, four_y[:, :, :CH])
-        open_partial(3, 3, four_y[:, :, CH:])
-        shared = keep.tile([P, 3 * PACK * CH], F32, name="shared", tag="w2s_raw", align_bytes=64)
-        first = shared[:, : 2 * PACK * CH].rearrange("p (t c) -> p t c", t=PACK)
-        rows[1, 3] = shared[:, 2 * PACK * CH :].rearrange("p (t c) -> p t c", t=PACK)
-        rows[1, 0] = shared[:, : PACK * CH].rearrange("p (t c) -> p t c", t=PACK)
-        for t in range(PACK):
-            nc.vector.tensor_copy(first[:, t, :], gy[t][:].indirect(nb_sb[:, CH // 16 : 3 * CH // 16]))
+        first_rows = sbuf("first_rows", [P, 3 * PLANES * CH], F32, after="w2s_raw")
+        both = first_rows[:, : 2 * PLANES * CH].rearrange("p (t c) -> p t c", t=PLANES)
+        rows[1, 3] = first_rows[:, 2 * PLANES * CH :].rearrange("p (t c) -> p t c", t=PLANES)
+        rows[1, 0] = first_rows[:, : PLANES * CH].rearrange("p (t c) -> p t c", t=PLANES)
+        gather(both, 1, 1, 3)
         for c in (1, 2):
-            rows[1, c] = first[:, :, (c - 1) * CH : c * CH]
+            rows[1, c] = both[:, :, chunk(c - 1)]
             interleave(1, c, on_scalar)
-        fetch(1, 3)
+        gather(rows[1, 3], 1, 3, 4)
         interleave(1, 3, on_scalar)
-        keep_second(1)
-        multiply(1, 1, (4, 4, 5, 5), 2)
+        keep_state(four_y_0, 0, 1)
+        quantise(1, 1)
+        velocity(1, 1, (4, 4, 5, 5), 2)
         quantise(1, 2)
-        fetch(1, 0)
+        gather(rows[1, 0], 1, 0, 1)
         interleave(1, 0, on_scalar)
-        multiply(1, 2, (6, 6, 6, 6), 2)
-        multiply(1, 3, (7, 7, 7, 7), 2)
-        multiply(1, 0, (4, 5, 6, 6), 1)
-        for c in (1, 2, 3, 0):
-            for t in range(PACK):
-                midpoint(c, t)
-            if c == 1:
-                partial(1, 0)
-        turned = {2: close_partial(2, 2, 1.0), 3: close_partial(3, 3)}
+        velocity(1, 2, (6, 6, 6, 6), 2)
+        quantise(1, 3)
+        velocity(1, 3, (7, 7, 7, 7), 2)
+        quantise(1, 0)
+        velocity(1, 0, (4, 5, 6, 6), 1)
+        midpoint(1)
+        part_even = partial(1, 0)
+        for c in (2, 3, 0):
+            midpoint(c)
+
+        turned = {2: add_first_velocity(2, 2, 1.0), 3: add_first_velocity(3, 3, 0.25)}
         fetch(2, 2)
         interleave(2, 2, on_scalar)
-        open_partial(0, 7, second)
-        turned[0] = close_partial(0, 7)
-        for t in range(PACK):
-            turn(banks[2][:, t * CH : (t + 1) * CH], turned[2][:, t, :], start=(t == 0))
-        return_partial(3, 3, turned[3])
-        fetch(2, 3, tag="late2")
+        turn(7, four_y_0, start=True)
+        turned[0] = add_first_velocity(0, 7, 0.25)
+        turn(2, turned[2], start=True)
+        turn(3, turned[3], start=True, stop=True)
+        fetch(2, 3, after="half_gain")
         interleave(2, 3, on_scalar)
         quantise(2, 2)
-        k2_turned = keep.tile([P, PACK, P], F32, name="k2_turned", align_bytes=64)
-        for u in range(2):
+        k2_turned = sbuf("k2_turned", [P, PLANES, P], F32)
+        for pair in range(2):
+            acc = banks[4 + pair][:, :HALF]
             nc.tensor.matmul_mx(
-                out=banks[4 + u][:, :HALF],
+                out=acc,
                 lhsT=codes[2, 2][:].bitcast(FP8X4),
                 lhsT_scale=scales[2, 2][:],
-                rhs=w2w[:, 2 * HALF * u : 2 * HALF * (u + 1)].bitcast(FP4X4),
-                rhs_scale=w2s[:, HALF * u : HALF * (u + 1)],
+                rhs=w2w[:, 2 * HALF * pair : 2 * HALF * (pair + 1)].bitcast(FP4X4),
+                rhs_scale=w2s[:, HALF * pair : HALF * (pair + 1)],
                 start=True,
                 stop=True,
             )
             nc.scalar.activation(
-                k2_turned[:, 2 * u : 2 * u + 2, :].rearrange("p t c -> p (t c)"), banks[4 + u][:, :HALF], ACT.Tanh
+                k2_turned[:, 2 * pair : 2 * pair + 2, :].rearrange("p t c -> p (t c)"), acc, ACT.Tanh
             )
-        return_partial(0, 7, turned[0])
-        fetch(2, 0, tag="rows2_2")
-        interleave(2, 0, on_scalar, tag="codes2_2")
-        for t in range(PACK):
-            turn(banks[2][:, t * CH : (t + 1) * CH], k2_turned[:, t, :], stop=(t == PACK - 1))
-        result[2] = keep.tile([P, PACK, CH], F32, name="result2", align_bytes=64)
-        nc.scalar.activation(result[2][:].rearrange("p t c -> p (t c)"), banks[2][:], ACT.Copy, scale=0.25)
-        multiply(2, 3, (5, 5, 5, 5), 2)
+        turn(7, turned[0], start=True, stop=True)
+        fetch(2, 0, after="rows2_2")
+        interleave(2, 0, on_scalar, after="codes2_2")
+        turn(2, k2_turned, stop=True)
+        result[2] = empty("result2", 2, 0.25)
+        quantise(2, 3)
+        velocity(2, 3, (5, 5, 5, 5), 2)
         store(2)
-        fetch(2, 1, tag="late2")
-        multiply(2, 0, (6, 6, 0, 0), 2)
-        interleave(2, 1, on_vector, tag="rows2_2")
-        partial(1, 1, tag="codes2_2")
-        multiply(2, 1, (4, 5, 1, 6), 1)
-        finish(3)
-        store(3)
-        round_out(2, on_vector, tag="rows2_2")
-        finish(0)
-        store(0)
-        finish(1)
-        store(1)
+        fetch(2, 1, after="half_gain")
+        quantise(2, 0)
+        velocity(2, 0, (6, 6, 0, 0), 2)
+        interleave(2, 1, on_vector, after="rows2_2")
+        part_odd = partial(1, 1, after="codes2_2")
+        quantise(2, 1)
+        velocity(2, 1, (4, 5, 1, 6), 1)
+
+        finish(3, pairs_of(3))
+        round_out(2, on_vector, after="rows2_2")
+        finish(0, pairs_of(7))
+        finish(1, [(t, (part_even, part_odd)[t % 2][:, t // 2, :]) for t in range(PLANES)])
         round_out(3, on_scalar)
         round_out(0, on_scalar)
         round_out(1, on_vector)
-        quantise_out(2)
-        quantise_out(3)
-        store_words(3)
-        quantise_out(0)
         quantise_out(1)
-        store_words(1)
-        store_scales()
+        quantise_out(0)
+        for q in range(4):
+            queue = nc.sync if q % 2 == 0 else nc.scalar
+            queue.dma_start(out_2[0, 4 * q : 4 * q + 4, :].bitcast(I32), out_scales[32 * q : 32 * q + 4, :].bitcast(I32))

@@ -242,7 +242,8 @@ def tile_picked_heun_none_po_kernel(
         four_y_0 = sbuf("four_y_0", [P, PLANES, CH], F32)
         keep_state(four_y_0, 0, 0)
         for c in (2, 3):
-            turn(c, four_y_high[:, :, chunk(c - 2)], start=True)
+            turn(c, four_y_high[:, :, chunk(c - 2)], order=(0, 2, 1, 3), start=True)
+        turn(7, four_y_0, order=(0, 2), start=True)
 
         first_rows = sbuf("first_rows", [P, 3 * PLANES * CH], F32, after="w2s_raw")
         both = first_rows[:, : 2 * PLANES * CH].rearrange("p (t c) -> p t c", t=PLANES)
@@ -262,9 +263,9 @@ def tile_picked_heun_none_po_kernel(
         interleave(1, 0, on_scalar)
         velocity(1, 2, (6, 6, 6, 6), 2)
         quantise(1, 3)
-        velocity(1, 3, (7, 7, 7, 7), 2)
+        velocity(1, 3, (4, 4, 4, 4), 2)
         quantise(1, 0)
-        velocity(1, 0, (4, 5, 6, 6), 1)
+        velocity(1, 0, (5, 5, 6, 6), 1)
         midpoint(1)
         part_even = partial(1, 0)
         for c in (2, 3, 0):
@@ -273,8 +274,9 @@ def tile_picked_heun_none_po_kernel(
         turned = {2: add_first_velocity(2, 2, 1.0), 3: add_first_velocity(3, 3, 0.25)}
         fetch(2, 2)
         interleave(2, 2, on_scalar)
-        turn(7, four_y_0, start=True)
-        turned[0] = add_first_velocity(0, 7, 0.25)
+        turn(7, k[1][:, :, chunk(0)], order=(3, 2, 1, 0))
+        turn(7, four_y_0, order=(1, 3), stop=True)
+        turned[0] = empty("turned0", 7, 0.25)
         turn(2, turned[2], start=True)
         turn(3, turned[3], start=True, stop=True)
         fetch(2, 3, after="half_gain")
@@ -309,10 +311,10 @@ def tile_picked_heun_none_po_kernel(
         interleave(2, 1, on_vector, after="rows2_2")
         part_odd = partial(1, 1, after="codes2_2")
         quantise(2, 1)
-        velocity(2, 1, (4, 5, 1, 6), 1)
+        velocity(2, 1, (4, 1, 5, 6), 1)
 
+        round_out(2, on_vector)
         finish(3, pairs_of(3))
-        round_out(2, on_vector, after="rows2_2")
         finish(0, pairs_of(7))
         finish(1, [(t, (part_even, part_odd)[t % 2][:, t // 2, :]) for t in range(PLANES)])
         round_out(3, on_scalar)

@@ -311,14 +311,17 @@ def tile_picked_heun_none_po_kernel(
         interleave(2, 1, on_vector, after="rows2_2")
         part_odd = partial(1, 1, after="codes2_2")
         quantise(2, 1)
-        velocity(2, 1, (4, 1, 5, 6), 1)
+        velocity(2, 1, (4, 1, 2, 5), 1)
 
         round_out(2, on_vector)
         finish(3, pairs_of(3))
         finish(0, pairs_of(7))
         finish(1, [(t, (part_even, part_odd)[t % 2][:, t // 2, :]) for t in range(PLANES)])
         round_out(3, on_scalar)
-        round_out(0, on_scalar)
+        rounded[0] = sbuf("rounded0", [P, PLANES * CH], BF16)
+        cut = 3 * CH // 4
+        weave(on_scalar, rounded[0][:, : PLANES * cut], result[0][:, :, :cut])
+        weave(on_vector, rounded[0][:, PLANES * cut :], result[0][:, :, cut:])
         round_out(1, on_vector)
         quantise_out(1)
         quantise_out(0)

@@ -23,7 +23,9 @@ PLANES = 4
 CH = 128
 HALF = S // 2
 PER_COLUMN = 16
-X_FIRST = 3 * T // 4
+ROWS_END = 2 * PLANES * CH * 4
+SCALE_ROWS = 16
+PARKED = P - SCALE_ROWS
 
 
 def chunk(c):
@@ -55,6 +57,7 @@ def tile_picked_heun_none_po_kernel(
     nc = tc.nc
     with ExitStack() as ctx:
         keep = ctx.enter_context(tc.tile_pool(name="keep", bufs=1))
+        laid = ctx.enter_context(tc.tile_pool(name="laid", bufs=1))
         psum = ctx.enter_context(tc.psum_pool(name="psum", bufs=1))
 
         def sbuf(name, shape, dtype, after=None):
@@ -66,47 +69,48 @@ def tile_picked_heun_none_po_kernel(
         xs = sbuf("xs", [P, T], U8)
         w1w_raw = sbuf("w1w_raw", [P, 2 * H], U8)
         w2w_raw = sbuf("w2w_raw", [P, 2 * H], U8)
-        w1s_raw = sbuf("w1s_raw", [P, H], U8)
-        w2s_raw = sbuf("w2s_raw", [P, H], U8)
-        gain = sbuf("gain", [P, PLANES], F32)
+        ws_raw = laid.tile([P, H], U8, name="ws_raw", offset=ROWS_END - H // 2)
+        xqs = sbuf("xqs", [P, S], U8)
+        gain = laid.tile([P, PLANES], F32, name="gain", offset=ROWS_END + H // 2)
         half_gain = sbuf("half_gain", [P, PLANES], F32)
 
-        nc.gpsimd.memset(xs[:, : T // 2].bitcast(I32), 0)
-        nc.vector.memset(xs[:, T // 2 :].bitcast(I32), 0)
-        nc.vector.memset(w1s_raw[:].bitcast(I32), 0)
-        nc.vector.memset(w2s_raw[:].bitcast(I32), 0)
+        nc.gpsimd.memset(ws_raw[:].bitcast(I32), 0)
+        nc.vector.memset(xs[:PARKED, :].bitcast(I32), 0)
+        nc.vector.memset(xqs[:].bitcast(I32), 0)
 
         identity = sbuf("identity", [P, P], F32)
         make_identity(nc, identity[:])
 
         x_view = x_words[0].rearrange("p n r -> p (n r)").bitcast(I32)
         nc.sync.dma_start(offs_sb[:], offs)
+        nc.sync.dma_start(xs[PARKED:, :].bitcast(I32), x_scales[0].bitcast(I32))
         nc.sync.dma_start(w1w_raw[:].bitcast(I32), w1_words[0].bitcast(I32))
-        load_scale_rows(nc, xs, x_scales)
-        nc.sync.dma_start(xw[:, :X_FIRST].bitcast(I32), x_view[:, :X_FIRST])
-        load_scale_rows(nc, w1s_raw, w1_scales)
-        nc.sync.dma_start(xw[:, X_FIRST:].bitcast(I32), x_view[:, X_FIRST:])
+        load_scale_rows(nc, ws_raw, w1_scales)
+        nc.sync.dma_start(xw[:].bitcast(I32), x_view)
         nc.sync.dma_start(gain[:], gn.rearrange("(p t) o -> p (t o)", t=PLANES))
         nc.sync.dma_start(nb_sb[:], nb)
         nc.sync.dma_start(w2w_raw[:].bitcast(I32), w2_words[0].bitcast(I32))
-        load_scale_rows(nc, w2s_raw, w2_scales)
 
         w1w = sbuf("w1w", [P, 2 * H], U8)
         w2w = sbuf("w2w", [P, 2 * H], U8)
         w1s = sbuf("w1s", [P, H], U8)
         w2s = sbuf("w2s", [P, H], U8)
         xqw = [sbuf(f"xqw{half}", [P, HALF], U32) for half in range(2)]
-        xqs = sbuf("xqs", [P, S], U8)
+        parked = sbuf("parked", [P, S], U8)
 
         nc.scalar.activation(half_gain[:], gain[:], ACT.Copy, scale=0.5)
         deal(nc, w1w[:].bitcast(U16), w1w_raw[:].bitcast(U16))
-        nc.vector.tensor_copy(xqs[:], xs[:].indirect(offs_sb[:]))
-        deal(nc, w1s[:], w1s_raw[:])
+        nc.vector.tensor_copy(parked[:], xs[:].indirect(offs_sb[:]))
+        for q in range(4):
+            rows_q = slice(PARKED + 4 * q, PARKED + 4 * q + 4)
+            nc.sync.dma_start(xqs[32 * q : 32 * q + 4, :].bitcast(I32), parked[rows_q, :].bitcast(I32))
+        deal(nc, w1s[:], ws_raw[:])
+        load_scale_rows(nc, ws_raw, w2_scales)
         for half in range(2):
             entries = slice(half * HALF // PER_COLUMN, (half + 1) * HALF // PER_COLUMN)
             nc.vector.tensor_copy(xqw[half][:], xw[:].indirect(offs_sb[:, entries]))
         deal(nc, w2w[:].bitcast(U16), w2w_raw[:].bitcast(U16))
-        deal(nc, w2s[:], w2s_raw[:])
+        deal(nc, w2s[:], ws_raw[:])
 
         banks = [psum.tile([P, S], F32, name=f"bank{b}") for b in range(8)]
         gy = [keep.tile([P, S], F32, name=f"gy{t}") for t in range(PLANES)]
@@ -245,9 +249,9 @@ def tile_picked_heun_none_po_kernel(
             turn(c, four_y_high[:, :, chunk(c - 2)], order=(0, 2, 1, 3), start=True)
         turn(7, four_y_0, order=(0, 2), start=True)
 
-        first_rows = sbuf("first_rows", [P, 3 * PLANES * CH], F32, after="w2s_raw")
-        both = first_rows[:, : 2 * PLANES * CH].rearrange("p (t c) -> p t c", t=PLANES)
-        rows[1, 3] = first_rows[:, 2 * PLANES * CH :].rearrange("p (t c) -> p t c", t=PLANES)
+        first_rows = laid.tile([P, 2 * PLANES * CH], F32, name="first_rows", offset=0)
+        both = first_rows[:].rearrange("p (t c) -> p t c", t=PLANES)
+        rows[1, 3] = laid.tile([P, PLANES, CH], F32, name="rows1_3", offset=ROWS_END)[:]
         rows[1, 0] = first_rows[:, : PLANES * CH].rearrange("p (t c) -> p t c", t=PLANES)
         gather(both, 1, 1, 3)
         for c in (1, 2):

@@ -23,7 +23,6 @@ PLANES = 4
 CH = 128
 HALF = S // 2
 PER_COLUMN = 16
-ROWS_END = 2 * PLANES * CH * 4
 SCALE_ROWS = 16
 PARKED = P - SCALE_ROWS
 
@@ -32,9 +31,15 @@ def chunk(c):
     return slice(c * CH, (c + 1) * CH)
 
 
-def load_scale_rows(nc, tile, scales):
+def load_scale_rows(queues, tile, scales):
     for r in range(4):
-        nc.sync.dma_start(tile[r:P:32, :].bitcast(I32), scales[0, r:16:4, :].bitcast(I32))
+        queues[r % len(queues)].dma_start(tile[r:P:32, :].bitcast(I32), scales[0, r:16:4, :].bitcast(I32))
+
+
+def unpark(nc, tile, parked):
+    for q in range(4):
+        rows = slice(PARKED + 4 * q, PARKED + 4 * q + 4)
+        nc.sync.dma_start(tile[32 * q : 32 * q + 4, :].bitcast(I32), parked[rows, :].bitcast(I32))
 
 
 def deal(nc, dealt, raw):
@@ -57,7 +62,6 @@ def tile_picked_heun_none_po_kernel(
     nc = tc.nc
     with ExitStack() as ctx:
         keep = ctx.enter_context(tc.tile_pool(name="keep", bufs=1))
-        laid = ctx.enter_context(tc.tile_pool(name="laid", bufs=1))
         psum = ctx.enter_context(tc.psum_pool(name="psum", bufs=1))
 
         def sbuf(name, shape, dtype, after=None):
@@ -69,48 +73,50 @@ def tile_picked_heun_none_po_kernel(
         xs = sbuf("xs", [P, T], U8)
         w1w_raw = sbuf("w1w_raw", [P, 2 * H], U8)
         w2w_raw = sbuf("w2w_raw", [P, 2 * H], U8)
-        ws_raw = laid.tile([P, H], U8, name="ws_raw", offset=ROWS_END - H // 2)
+        w1s_raw = sbuf("w1s_raw", [P, H], U8)
+        w2s_raw = sbuf("w2s_raw", [P, H], U8)
         xqs = sbuf("xqs", [P, S], U8)
-        gain = laid.tile([P, PLANES], F32, name="gain", offset=ROWS_END + H // 2)
+        w2s = sbuf("w2s", [P, H], U8)
+        gain = sbuf("gain", [P, PLANES], F32)
         half_gain = sbuf("half_gain", [P, PLANES], F32)
 
-        nc.gpsimd.memset(ws_raw[:].bitcast(I32), 0)
+        nc.gpsimd.memset(w1s_raw[:].bitcast(I32), 0)
         nc.vector.memset(xs[:PARKED, :].bitcast(I32), 0)
         nc.vector.memset(xqs[:].bitcast(I32), 0)
-
-        identity = sbuf("identity", [P, P], F32)
-        make_identity(nc, identity[:])
+        nc.vector.memset(w2s_raw[:PARKED, :].bitcast(I32), 0)
+        nc.vector.memset(w2s[:].bitcast(I32), 0)
+        nc.gpsimd.dma_start(gain[:], gn.rearrange("(p t) o -> p (t o)", t=PLANES))
 
         x_view = x_words[0].rearrange("p n r -> p (n r)").bitcast(I32)
         nc.sync.dma_start(offs_sb[:], offs)
         nc.sync.dma_start(xs[PARKED:, :].bitcast(I32), x_scales[0].bitcast(I32))
         nc.sync.dma_start(w1w_raw[:].bitcast(I32), w1_words[0].bitcast(I32))
-        load_scale_rows(nc, ws_raw, w1_scales)
+        load_scale_rows((nc.sync, nc.scalar), w1s_raw, w1_scales)
         nc.sync.dma_start(xw[:].bitcast(I32), x_view)
-        nc.sync.dma_start(gain[:], gn.rearrange("(p t) o -> p (t o)", t=PLANES))
+        nc.sync.dma_start(w2s_raw[PARKED:, :].bitcast(I32), w2_scales[0].bitcast(I32))
         nc.sync.dma_start(nb_sb[:], nb)
         nc.sync.dma_start(w2w_raw[:].bitcast(I32), w2_words[0].bitcast(I32))
 
         w1w = sbuf("w1w", [P, 2 * H], U8)
         w2w = sbuf("w2w", [P, 2 * H], U8)
         w1s = sbuf("w1s", [P, H], U8)
-        w2s = sbuf("w2s", [P, H], U8)
         xqw = [sbuf(f"xqw{half}", [P, HALF], U32) for half in range(2)]
         parked = sbuf("parked", [P, S], U8)
+        w2s_parked = sbuf("w2s_parked", [P, H], U8)
 
         nc.scalar.activation(half_gain[:], gain[:], ACT.Copy, scale=0.5)
-        deal(nc, w1w[:].bitcast(U16), w1w_raw[:].bitcast(U16))
         nc.vector.tensor_copy(parked[:], xs[:].indirect(offs_sb[:]))
-        for q in range(4):
-            rows_q = slice(PARKED + 4 * q, PARKED + 4 * q + 4)
-            nc.sync.dma_start(xqs[32 * q : 32 * q + 4, :].bitcast(I32), parked[rows_q, :].bitcast(I32))
-        deal(nc, w1s[:], ws_raw[:])
-        load_scale_rows(nc, ws_raw, w2_scales)
+        deal(nc, w1w[:].bitcast(U16), w1w_raw[:].bitcast(U16))
+        unpark(nc, xqs, parked)
+        deal(nc, w1s[:], w1s_raw[:])
+        identity = sbuf("identity", [P, P], F32, after="w1w_raw")
+        make_identity(nc, identity[:])
         for half in range(2):
             entries = slice(half * HALF // PER_COLUMN, (half + 1) * HALF // PER_COLUMN)
             nc.vector.tensor_copy(xqw[half][:], xw[:].indirect(offs_sb[:, entries]))
+        deal(nc, w2s_parked[:], w2s_raw[:])
+        unpark(nc, w2s, w2s_parked)
         deal(nc, w2w[:].bitcast(U16), w2w_raw[:].bitcast(U16))
-        deal(nc, w2s[:], ws_raw[:])
 
         banks = [psum.tile([P, S], F32, name=f"bank{b}") for b in range(8)]
         gy = [keep.tile([P, S], F32, name=f"gy{t}") for t in range(PLANES)]
@@ -119,6 +125,9 @@ def tile_picked_heun_none_po_kernel(
         k = {v: keep.tile([P, PLANES, S], F32, name=f"k{v}") for v in (1, 2)}
         rows, woven, codes, scales, result, rounded = {}, {}, {}, {}, {}, {}
         on_scalar, on_vector = nc.scalar.copy, nc.vector.tensor_copy
+
+        def on_gpsimd(out, in_):
+            nc.gpsimd.tensor_scalar(out, in_, 1.0, -0.0, MULT, ADD)
 
         def product(acc, words, word_scales, t, moving, moving_scales):
             nc.tensor.matmul_mx(
@@ -209,7 +218,6 @@ def tile_picked_heun_none_po_kernel(
         out_rows = out_0.rearrange("(p t) s -> p t s", t=PLANES)
         out_words = out_1[0].rearrange("p n r -> p (n r)").bitcast(I32)
         out_codes = sbuf("out_codes", [P, S], U32)
-        out_scales = sbuf("out_scales", [P, S], U8)
 
         def store(c):
             nc.sync.dma_start(out_rows[:, :, chunk(c)], result[c][:])
@@ -249,9 +257,9 @@ def tile_picked_heun_none_po_kernel(
             turn(c, four_y_high[:, :, chunk(c - 2)], order=(0, 2, 1, 3), start=True)
         turn(7, four_y_0, order=(0, 2), start=True)
 
-        first_rows = laid.tile([P, 2 * PLANES * CH], F32, name="first_rows", offset=0)
+        first_rows = sbuf("first_rows", [P, 2 * PLANES * CH], F32)
         both = first_rows[:].rearrange("p (t c) -> p t c", t=PLANES)
-        rows[1, 3] = laid.tile([P, PLANES, CH], F32, name="rows1_3", offset=ROWS_END)[:]
+        rows[1, 3] = sbuf("rows1_3", [P, PLANES, CH], F32, after="gain")[:]
         rows[1, 0] = first_rows[:, : PLANES * CH].rearrange("p (t c) -> p t c", t=PLANES)
         gather(both, 1, 1, 3)
         for c in (1, 2):
@@ -317,10 +325,12 @@ def tile_picked_heun_none_po_kernel(
         quantise(2, 1)
         velocity(2, 1, (4, 1, 2, 5), 1)
 
-        round_out(2, on_vector)
+        rounded[2] = sbuf("rounded2", [P, PLANES * CH], BF16, after="rows2_2")
+        on_gpsimd(rounded[2][:].rearrange("p (c t) -> p c t", t=PLANES), result[2][:].rearrange("p t c -> p c t"))
         finish(3, pairs_of(3))
         finish(0, pairs_of(7))
         finish(1, [(t, (part_even, part_odd)[t % 2][:, t // 2, :]) for t in range(PLANES)])
+        out_scales = sbuf("out_scales", [P, S], U8, after="part1_0")
         round_out(3, on_scalar)
         rounded[0] = sbuf("rounded0", [P, PLANES * CH], BF16)
         cut = 3 * CH // 4

@@ -80,7 +80,7 @@ def tile_picked_heun_none_po_kernel(
         gain = sbuf("gain", [P, PLANES], F32)
         half_gain = sbuf("half_gain", [P, PLANES], F32)
 
-        nc.gpsimd.memset(w1s_raw[:].bitcast(I32), 0)
+        nc.gpsimd.memset(w1s_raw[:].bitcast(F32), 0.0)
         nc.vector.memset(xs[:PARKED, :].bitcast(I32), 0)
         nc.vector.memset(xqs[:].bitcast(I32), 0)
         nc.vector.memset(w2s_raw[:PARKED, :].bitcast(I32), 0)
@@ -109,7 +109,7 @@ def tile_picked_heun_none_po_kernel(
         deal(nc, w1w[:].bitcast(U16), w1w_raw[:].bitcast(U16))
         unpark(nc, xqs, parked)
         deal(nc, w1s[:], w1s_raw[:])
-        identity = sbuf("identity", [P, P], F32, after="w1w_raw")
+        identity = sbuf("identity", [P, P], F32, after="xs")
         make_identity(nc, identity[:])
         for half in range(2):
             entries = slice(half * HALF // PER_COLUMN, (half + 1) * HALF // PER_COLUMN)
@@ -122,7 +122,7 @@ def tile_picked_heun_none_po_kernel(
         gy = [keep.tile([P, S], F32, name=f"gy{t}") for t in range(PLANES)]
         gh = [keep.tile([P, S], F32, name=f"gh{t}") for t in range(PLANES)]
         windows = {1: gy, 2: gh}
-        k = {v: keep.tile([P, PLANES, S], F32, name=f"k{v}") for v in (1, 2)}
+        k = {(v, c): sbuf(f"k{v}_{c}", [P, PLANES, CH], F32) for v in (1, 2) for c in range(S // CH) if (v, c) != (2, 2)}
         rows, woven, codes, scales, result, rounded = {}, {}, {}, {}, {}, {}
         on_scalar, on_vector = nc.scalar.copy, nc.vector.tensor_copy
 
@@ -149,13 +149,14 @@ def tile_picked_heun_none_po_kernel(
             product(acc, w1w, w1s, t, xqw[half][:], xqs[:, cols])
             nc.scalar.activation(gy[t][:, cols], acc, ACT.Copy, scale=gain[:, t : t + 1])
 
-        def keep_state(tile, half, odd):
-            width = tile[:].shape[2]
-            nc.scalar.activation(tile[:, odd:PLANES:2, :], state_planes(half, odd)[:, :, :width], ACT.Copy, scale=4.0)
+        def keep_state(tile, half, odd, width=HALF):
+            nc.scalar.activation(
+                tile[:, odd:PLANES:2, :width], state_planes(half, odd)[:, :, :width], ACT.Copy, scale=4.0
+            )
 
-        def gather(into, v, first, last):
+        def gather(into, v, first, last, order=range(PLANES)):
             entries = nb_sb[:, first * CH // PER_COLUMN : last * CH // PER_COLUMN]
-            for t in range(PLANES):
+            for t in order:
                 nc.vector.tensor_copy(into[:, t, :], windows[v][t][:].indirect(entries))
 
         def fetch(v, c, after=None):
@@ -179,13 +180,13 @@ def tile_picked_heun_none_po_kernel(
                     for u in range(first, t + 1, step):
                         acc = banks[bank][:, (u - first) * CH : (u - first + step) * CH]
                         nc.scalar.activation(
-                            k[v][:, u : u + step, chunk(c)], acc.rearrange("p (t c) -> p t c", t=step), ACT.Tanh
+                            k[v, c][:, u : u + step, :], acc.rearrange("p (t c) -> p t c", t=step), ACT.Tanh
                         )
 
         def midpoint(c):
             for t in range(PLANES):
                 nc.vector.scalar_tensor_tensor(
-                    gh[t][:, chunk(c)], k[1][:, t, chunk(c)], half_gain[:, t : t + 1], gy[t][:, chunk(c)], MULT, ADD
+                    gh[t][:, chunk(c)], k[1, c][:, t, :], half_gain[:, t : t + 1], gy[t][:, chunk(c)], MULT, ADD
                 )
 
         def turn(bank, planes, order=range(PLANES), start=False, stop=False):
@@ -205,13 +206,13 @@ def tile_picked_heun_none_po_kernel(
             return tile
 
         def add_first_velocity(c, bank, scale):
-            turn(bank, k[1][:, :, chunk(c)], order=range(PLANES - 1, -1, -1), stop=True)
+            turn(bank, k[1, c], order=range(PLANES - 1, -1, -1), stop=True)
             return empty(f"turned{c}", bank, scale)
 
         def partial(c, odd, after=None):
             tile = sbuf(f"part{c}_{odd}", [P, 2, CH], F32, after)
             nc.vector.scalar_tensor_tensor(
-                tile[:], k[1][:, odd:PLANES:2, chunk(c)], 0.25, state_planes(0, odd)[:, :, chunk(c)], MULT, ADD
+                tile[:], k[1, c][:, odd:PLANES:2, :], 0.25, state_planes(0, odd)[:, :, chunk(c)], MULT, ADD
             )
             return tile
 
@@ -222,10 +223,13 @@ def tile_picked_heun_none_po_kernel(
         def store(c):
             nc.sync.dma_start(out_rows[:, :, chunk(c)], result[c][:])
 
+        def add_last(c, parts):
+            for planes, part in parts:
+                nc.vector.scalar_tensor_tensor(result[c][:, planes, :], k[2, c][:, planes, :], 0.25, part, MULT, ADD)
+
         def finish(c, parts):
             result[c] = sbuf(f"result{c}", [P, PLANES, CH], F32)
-            for planes, part in parts:
-                nc.vector.scalar_tensor_tensor(result[c][:, planes, :], k[2][:, planes, chunk(c)], 0.25, part, MULT, ADD)
+            add_last(c, parts)
             store(c)
 
         def pairs_of(bank):
@@ -252,10 +256,11 @@ def tile_picked_heun_none_po_kernel(
         for odd in range(2):
             keep_state(four_y_high, 1, odd)
         four_y_0 = sbuf("four_y_0", [P, PLANES, CH], F32)
-        keep_state(four_y_0, 0, 0)
+        for odd in range(2):
+            keep_state(four_y_0, 0, odd, CH)
         for c in (2, 3):
             turn(c, four_y_high[:, :, chunk(c - 2)], order=(0, 2, 1, 3), start=True)
-        turn(7, four_y_0, order=(0, 2), start=True)
+        turn(7, four_y_0, order=(0, 2, 1, 3), start=True)
 
         first_rows = sbuf("first_rows", [P, 2 * PLANES * CH], F32)
         both = first_rows[:].rearrange("p (t c) -> p t c", t=PLANES)
@@ -267,33 +272,32 @@ def tile_picked_heun_none_po_kernel(
             interleave(1, c, on_scalar)
         gather(rows[1, 3], 1, 3, 4)
         interleave(1, 3, on_scalar)
-        keep_state(four_y_0, 0, 1)
         quantise(1, 1)
         velocity(1, 1, (4, 4, 5, 5), 2)
+        gather(rows[1, 0], 1, 0, 1, order=(0, 2))
         quantise(1, 2)
-        gather(rows[1, 0], 1, 0, 1)
-        interleave(1, 0, on_scalar)
+        gather(rows[1, 0], 1, 0, 1, order=(1, 3))
+        interleave(1, 0, on_scalar, after="codes1_1")
         velocity(1, 2, (6, 6, 6, 6), 2)
         quantise(1, 3)
         velocity(1, 3, (4, 4, 4, 4), 2)
-        quantise(1, 0)
-        velocity(1, 0, (5, 5, 6, 6), 1)
         midpoint(1)
         part_even = partial(1, 0)
+        quantise(1, 0)
+        velocity(1, 0, (5, 5, 6, 6), 1)
         for c in (2, 3, 0):
             midpoint(c)
 
         turned = {2: add_first_velocity(2, 2, 1.0), 3: add_first_velocity(3, 3, 0.25)}
         fetch(2, 2)
-        interleave(2, 2, on_scalar)
-        turn(7, k[1][:, :, chunk(0)], order=(3, 2, 1, 0))
-        turn(7, four_y_0, order=(1, 3), stop=True)
-        turned[0] = empty("turned0", 7, 0.25)
+        turned[0] = add_first_velocity(0, 7, 0.25)
+        interleave(2, 2, on_scalar, after="k1_0")
         turn(2, turned[2], start=True)
         turn(3, turned[3], start=True, stop=True)
+        turn(7, turned[0], start=True, stop=True)
         fetch(2, 3, after="half_gain")
-        interleave(2, 3, on_scalar)
         quantise(2, 2)
+        interleave(2, 3, on_scalar, after="k1_0")
         k2_turned = sbuf("k2_turned", [P, PLANES, P], F32)
         for pair in range(2):
             acc = banks[4 + pair][:, :HALF]
@@ -309,7 +313,6 @@ def tile_picked_heun_none_po_kernel(
             nc.scalar.activation(
                 k2_turned[:, 2 * pair : 2 * pair + 2, :].rearrange("p t c -> p (t c)"), acc, ACT.Tanh
             )
-        turn(7, turned[0], start=True, stop=True)
         fetch(2, 0, after="rows2_2")
         interleave(2, 0, on_scalar, after="codes2_2")
         turn(2, k2_turned, stop=True)

@@ -23,6 +23,7 @@ PLANES = 4
 CH = 128
 HALF = S // 2
 PER_COLUMN = 16
+X_FIRST = T // 2
 SCALE_ROWS = 16
 PARKED = P - SCALE_ROWS
 
@@ -72,7 +73,6 @@ def tile_picked_heun_none_po_kernel(
         xw = sbuf("xw", [P, T], U32)
         xs = sbuf("xs", [P, T], U8)
         w1w_raw = sbuf("w1w_raw", [P, 2 * H], U8)
-        w2w_raw = sbuf("w2w_raw", [P, 2 * H], U8)
         w1s_raw = sbuf("w1s_raw", [P, H], U8)
         w2s_raw = sbuf("w2s_raw", [P, H], U8)
         xqs = sbuf("xqs", [P, S], U8)
@@ -91,11 +91,11 @@ def tile_picked_heun_none_po_kernel(
         nc.sync.dma_start(offs_sb[:], offs)
         nc.sync.dma_start(xs[PARKED:, :].bitcast(I32), x_scales[0].bitcast(I32))
         nc.sync.dma_start(w1w_raw[:].bitcast(I32), w1_words[0].bitcast(I32))
-        load_scale_rows((nc.sync, nc.scalar), w1s_raw, w1_scales)
-        nc.sync.dma_start(xw[:].bitcast(I32), x_view)
+        nc.sync.dma_start(xw[:, :X_FIRST].bitcast(I32), x_view[:, :X_FIRST])
+        load_scale_rows((nc.sync,), w1s_raw, w1_scales)
+        nc.sync.dma_start(xw[:, X_FIRST:].bitcast(I32), x_view[:, X_FIRST:])
         nc.sync.dma_start(w2s_raw[PARKED:, :].bitcast(I32), w2_scales[0].bitcast(I32))
         nc.sync.dma_start(nb_sb[:], nb)
-        nc.sync.dma_start(w2w_raw[:].bitcast(I32), w2_words[0].bitcast(I32))
 
         w1w = sbuf("w1w", [P, 2 * H], U8)
         w2w = sbuf("w2w", [P, 2 * H], U8)
@@ -108,6 +108,8 @@ def tile_picked_heun_none_po_kernel(
         nc.vector.tensor_copy(parked[:], xs[:].indirect(offs_sb[:]))
         deal(nc, w1w[:].bitcast(U16), w1w_raw[:].bitcast(U16))
         unpark(nc, xqs, parked)
+        w2w_raw = sbuf("w2w_raw", [P, 2 * H], U8, after="w1w_raw")
+        nc.sync.dma_start(w2w_raw[:].bitcast(I32), w2_words[0].bitcast(I32))
         deal(nc, w1s[:], w1s_raw[:])
         identity = sbuf("identity", [P, P], F32, after="xs")
         make_identity(nc, identity[:])

@@ -23,24 +23,23 @@ PLANES = 4
 CH = 128
 HALF = S // 2
 PER_COLUMN = 16
+PARKED = P - 16
 X_FIRST = T // 2
-SCALE_ROWS = 16
-PARKED = P - SCALE_ROWS
 
 
 def chunk(c):
     return slice(c * CH, (c + 1) * CH)
 
 
-def load_scale_rows(queues, tile, scales):
+def load_scale_rows(nc, tile, scales):
     for r in range(4):
-        queues[r % len(queues)].dma_start(tile[r:P:32, :].bitcast(I32), scales[0, r:16:4, :].bitcast(I32))
+        nc.sync.dma_start(tile[r:P:32, :].bitcast(I32), scales[0, r:16:4, :].bitcast(I32))
 
 
 def unpark(nc, tile, parked):
     for q in range(4):
-        rows = slice(PARKED + 4 * q, PARKED + 4 * q + 4)
-        nc.sync.dma_start(tile[32 * q : 32 * q + 4, :].bitcast(I32), parked[rows, :].bitcast(I32))
+        source = parked[PARKED + 4 * q : PARKED + 4 * q + 4, :]
+        nc.sync.dma_start(tile[32 * q : 32 * q + 4, :].bitcast(I32), source.bitcast(I32))
 
 
 def deal(nc, dealt, raw):
@@ -92,7 +91,7 @@ def tile_picked_heun_none_po_kernel(
         nc.sync.dma_start(xs[PARKED:, :].bitcast(I32), x_scales[0].bitcast(I32))
         nc.sync.dma_start(w1w_raw[:].bitcast(I32), w1_words[0].bitcast(I32))
         nc.sync.dma_start(xw[:, :X_FIRST].bitcast(I32), x_view[:, :X_FIRST])
-        load_scale_rows((nc.sync,), w1s_raw, w1_scales)
+        load_scale_rows(nc, w1s_raw, w1_scales)
         nc.sync.dma_start(xw[:, X_FIRST:].bitcast(I32), x_view[:, X_FIRST:])
         nc.sync.dma_start(w2s_raw[PARKED:, :].bitcast(I32), w2_scales[0].bitcast(I32))
         nc.sync.dma_start(nb_sb[:], nb)
@@ -101,13 +100,13 @@ def tile_picked_heun_none_po_kernel(
         w2w = sbuf("w2w", [P, 2 * H], U8)
         w1s = sbuf("w1s", [P, H], U8)
         xqw = [sbuf(f"xqw{half}", [P, HALF], U32) for half in range(2)]
-        parked = sbuf("parked", [P, S], U8)
+        xqs_parked = sbuf("parked", [P, S], U8)
         w2s_parked = sbuf("w2s_parked", [P, H], U8)
 
         nc.scalar.activation(half_gain[:], gain[:], ACT.Copy, scale=0.5)
-        nc.vector.tensor_copy(parked[:], xs[:].indirect(offs_sb[:]))
+        nc.vector.tensor_copy(xqs_parked[:], xs[:].indirect(offs_sb[:]))
         deal(nc, w1w[:].bitcast(U16), w1w_raw[:].bitcast(U16))
-        unpark(nc, xqs, parked)
+        unpark(nc, xqs, xqs_parked)
         w2w_raw = sbuf("w2w_raw", [P, 2 * H], U8, after="w1w_raw")
         nc.sync.dma_start(w2w_raw[:].bitcast(I32), w2_words[0].bitcast(I32))
         deal(nc, w1s[:], w1s_raw[:])
@@ -124,12 +123,10 @@ def tile_picked_heun_none_po_kernel(
         gy = [keep.tile([P, S], F32, name=f"gy{t}") for t in range(PLANES)]
         gh = [keep.tile([P, S], F32, name=f"gh{t}") for t in range(PLANES)]
         windows = {1: gy, 2: gh}
-        k = {(v, c): sbuf(f"k{v}_{c}", [P, PLANES, CH], F32) for v in (1, 2) for c in range(S // CH) if (v, c) != (2, 2)}
+        plain = [(v, c) for v in (1, 2) for c in range(S // CH) if (v, c) != (2, 2)]
+        k = {(v, c): sbuf(f"k{v}_{c}", [P, PLANES, CH], F32) for v, c in plain}
         rows, woven, codes, scales, result, rounded = {}, {}, {}, {}, {}, {}
         on_scalar, on_vector = nc.scalar.copy, nc.vector.tensor_copy
-
-        def on_gpsimd(out, in_):
-            nc.gpsimd.tensor_scalar(out, in_, 1.0, -0.0, MULT, ADD)
 
         def product(acc, words, word_scales, t, moving, moving_scales):
             nc.tensor.matmul_mx(
@@ -225,13 +222,10 @@ def tile_picked_heun_none_po_kernel(
         def store(c):
             nc.sync.dma_start(out_rows[:, :, chunk(c)], result[c][:])
 
-        def add_last(c, parts):
-            for planes, part in parts:
-                nc.vector.scalar_tensor_tensor(result[c][:, planes, :], k[2, c][:, planes, :], 0.25, part, MULT, ADD)
-
         def finish(c, parts):
             result[c] = sbuf(f"result{c}", [P, PLANES, CH], F32)
-            add_last(c, parts)
+            for planes, part in parts:
+                nc.vector.scalar_tensor_tensor(result[c][:, planes, :], k[2, c][:, planes, :], 0.25, part, MULT, ADD)
             store(c)
 
         def pairs_of(bank):
@@ -244,9 +238,11 @@ def tile_picked_heun_none_po_kernel(
 
         def quantise_out(half):
             for c in (2 * half, 2 * half + 1):
-                nc.vector.quantize_mx(
-                    out=out_codes[:, chunk(c)].bitcast(FP8X4), scales=out_scales[:, chunk(c)], in_=rounded[c][:]
-                )
+                pieces = (early, rounded[c]) if c == 2 else (rounded[c],)
+                for i, piece in enumerate(pieces):
+                    width = CH // len(pieces)
+                    at = slice(c * CH + i * width, c * CH + (i + 1) * width)
+                    nc.vector.quantize_mx(out=out_codes[:, at].bitcast(FP8X4), scales=out_scales[:, at], in_=piece[:])
             cols = slice(half * HALF, (half + 1) * HALF)
             nc.sync.dma_start(out_words[:, cols], out_codes[:, cols].bitcast(I32))
 
@@ -319,6 +315,12 @@ def tile_picked_heun_none_po_kernel(
         interleave(2, 0, on_scalar, after="codes2_2")
         turn(2, k2_turned, stop=True)
         result[2] = empty("result2", 2, 0.25)
+        early = sbuf("rounded2_early", [P, PLANES * CH // 2], BF16)
+        weave(
+            lambda out, in_: nc.scalar.activation(out, in_, ACT.Copy, scale=0.25),
+            early[:],
+            banks[2][:].rearrange("p (t c) -> p t c", t=PLANES)[:, :, : CH // 2],
+        )
         quantise(2, 3)
         velocity(2, 3, (5, 5, 5, 5), 2)
         store(2)
@@ -330,8 +332,15 @@ def tile_picked_heun_none_po_kernel(
         quantise(2, 1)
         velocity(2, 1, (4, 1, 2, 5), 1)
 
-        rounded[2] = sbuf("rounded2", [P, PLANES * CH], BF16, after="rows2_2")
-        on_gpsimd(rounded[2][:].rearrange("p (c t) -> p c t", t=PLANES), result[2][:].rearrange("p t c -> p c t"))
+        rounded[2] = sbuf("rounded2", [P, PLANES * CH // 2], BF16, after="rows2_2")
+        nc.gpsimd.tensor_scalar(
+            rounded[2][:].rearrange("p (c t) -> p c t", t=PLANES),
+            result[2][:, :, CH // 2 :].rearrange("p t c -> p c t"),
+            1.0,
+            -0.0,
+            MULT,
+            ADD,
+        )
         finish(3, pairs_of(3))
         finish(0, pairs_of(7))
         finish(1, [(t, (part_even, part_odd)[t % 2][:, t // 2, :]) for t in range(PLANES)])
@@ -346,4 +355,5 @@ def tile_picked_heun_none_po_kernel(
         quantise_out(0)
         for q in range(4):
             queue = nc.sync if q % 2 == 0 else nc.scalar
-            queue.dma_start(out_2[0, 4 * q : 4 * q + 4, :].bitcast(I32), out_scales[32 * q : 32 * q + 4, :].bitcast(I32))
+            live = out_scales[32 * q : 32 * q + 4, :]
+            queue.dma_start(out_2[0, 4 * q : 4 * q + 4, :].bitcast(I32), live.bitcast(I32))

@@ -1,7 +1,6 @@
 from contextlib import ExitStack
 
 import concourse.mybir as mybir
-from concourse.masks import make_identity
 
 T, S, H = 2048, 512, 512
 FLOPS = 3 * 2 * 512 * 512 * 512
@@ -77,7 +76,7 @@ def tile_picked_heun_none_po_kernel(
         xqs = sbuf("xqs", [P, S], U8)
         w2s = sbuf("w2s", [P, H], U8)
         gain = sbuf("gain", [P, PLANES], F32)
-        half_gain = sbuf("half_gain", [P, PLANES], F32)
+        half_gain = [sbuf(f"half_gain{pair}", [P, 2], F32) for pair in range(2)]
 
         nc.gpsimd.memset(w1s_raw[:].bitcast(F32), 0.0)
         nc.vector.memset(xs[:PARKED, :].bitcast(I32), 0)
@@ -103,15 +102,14 @@ def tile_picked_heun_none_po_kernel(
         xqs_parked = sbuf("parked", [P, S], U8)
         w2s_parked = sbuf("w2s_parked", [P, H], U8)
 
-        nc.scalar.activation(half_gain[:], gain[:], ACT.Copy, scale=0.5)
+        for pair in range(2):
+            nc.scalar.activation(half_gain[pair][:], gain[:, 2 * pair : 2 * pair + 2], ACT.Copy, scale=0.5)
         nc.vector.tensor_copy(xqs_parked[:], xs[:].indirect(offs_sb[:]))
         deal(nc, w1w[:].bitcast(U16), w1w_raw[:].bitcast(U16))
         unpark(nc, xqs, xqs_parked)
         w2w_raw = sbuf("w2w_raw", [P, 2 * H], U8, after="w1w_raw")
         nc.sync.dma_start(w2w_raw[:].bitcast(I32), w2_words[0].bitcast(I32))
         deal(nc, w1s[:], w1s_raw[:])
-        identity = sbuf("identity", [P, P], F32, after="xs")
-        make_identity(nc, identity[:])
         for half in range(2):
             entries = slice(half * HALF // PER_COLUMN, (half + 1) * HALF // PER_COLUMN)
             nc.vector.tensor_copy(xqw[half][:], xw[:].indirect(offs_sb[:, entries]))
@@ -123,10 +121,13 @@ def tile_picked_heun_none_po_kernel(
         gy = [keep.tile([P, S], F32, name=f"gy{t}") for t in range(PLANES)]
         gh = [keep.tile([P, S], F32, name=f"gh{t}") for t in range(PLANES)]
         windows = {1: gy, 2: gh}
-        plain = [(v, c) for v in (1, 2) for c in range(S // CH) if (v, c) != (2, 2)]
-        k = {(v, c): sbuf(f"k{v}_{c}", [P, PLANES, CH], F32) for v, c in plain}
-        rows, woven, codes, scales, result, rounded = {}, {}, {}, {}, {}, {}
-        on_scalar, on_vector = nc.scalar.copy, nc.vector.tensor_copy
+        woven, codes, scales, result, rounded = {}, {}, {}, {}, {}
+        k = {v: sbuf(f"k{v}", [P, PLANES, S], F32) for v in (1, 2)}
+
+        def on_scalar(out, in_):
+            nc.scalar.activation(out, in_, ACT.Copy)
+
+        on_vector = nc.vector.tensor_copy
 
         def product(acc, words, word_scales, t, moving, moving_scales):
             nc.tensor.matmul_mx(
@@ -148,211 +149,161 @@ def tile_picked_heun_none_po_kernel(
             product(acc, w1w, w1s, t, xqw[half][:], xqs[:, cols])
             nc.scalar.activation(gy[t][:, cols], acc, ACT.Copy, scale=gain[:, t : t + 1])
 
-        def keep_state(tile, half, odd, width=HALF):
-            nc.scalar.activation(
-                tile[:, odd:PLANES:2, :width], state_planes(half, odd)[:, :, :width], ACT.Copy, scale=4.0
-            )
+        rows = {v: sbuf(f"rows{v}", [P, PLANES, S], F32) for v in (1, 2)}
 
-        def gather(into, v, first, last, order=range(PLANES)):
+        def gather(v, first, last, planes, copy):
             entries = nb_sb[:, first * CH // PER_COLUMN : last * CH // PER_COLUMN]
-            for t in order:
-                nc.vector.tensor_copy(into[:, t, :], windows[v][t][:].indirect(entries))
+            for t in planes:
+                copy(rows[v][:, t, first * CH : last * CH], windows[v][t][:].indirect(entries))
 
-        def fetch(v, c, after=None):
-            rows[v, c] = sbuf(f"rows{v}_{c}", [P, PLANES, CH], F32, after)[:]
-            gather(rows[v, c], v, c, c + 1)
-
-        def interleave(v, c, copy, after=None):
+        def interleave(v, c, after=None):
             woven[v, c] = sbuf(f"woven{v}_{c}", [P, PLANES * CH], BF16, after)
-            weave(copy, woven[v, c][:], rows[v, c])
+            weave(on_vector, woven[v, c][:], rows[v][:, :, chunk(c)])
 
-        def quantise(v, c):
-            codes[v, c] = sbuf(f"codes{v}_{c}", [P, CH], U32)
+        def quantise(v, c, after=None):
+            codes[v, c] = sbuf(f"codes{v}_{c}", [P, CH], U32, after)
             scales[v, c] = sbuf(f"scales{v}_{c}", [P, CH], U8)
             nc.vector.quantize_mx(out=codes[v, c][:].bitcast(FP8X4), scales=scales[v, c][:], in_=woven[v, c][:])
 
-        def velocity(v, c, into, step):
+        def passes(v, c, into):
             for t, bank in enumerate(into):
-                first = into.index(bank)
-                product(banks[bank][:, chunk(t - first)], w2w, w2s, t, codes[v, c][:], scales[v, c][:])
-                if bank not in into[t + 1 :]:
-                    for u in range(first, t + 1, step):
-                        acc = banks[bank][:, (u - first) * CH : (u - first + step) * CH]
-                        nc.scalar.activation(
-                            k[v, c][:, u : u + step, :], acc.rearrange("p (t c) -> p t c", t=step), ACT.Tanh
-                        )
+                product(banks[bank][:, chunk(t)], w2w, w2s, t, codes[v, c][:], scales[v, c][:])
 
-        def midpoint(c):
-            for t in range(PLANES):
-                nc.vector.scalar_tensor_tensor(
-                    gh[t][:, chunk(c)], k[1, c][:, t, :], half_gain[:, t : t + 1], gy[t][:, chunk(c)], MULT, ADD
-                )
+        def velocity(v, c, bank, planes):
+            acc = banks[bank][:].rearrange("p (t c) -> p t c", t=PLANES)
+            nc.scalar.activation(k[v][:, planes, chunk(c)], acc[:, planes, :], ACT.Tanh)
 
-        def turn(bank, planes, order=range(PLANES), start=False, stop=False):
-            for t in order:
-                nc.tensor.matmul(
-                    banks[bank][:, chunk(t)],
-                    planes[:, t, :],
-                    identity[:],
-                    is_transpose=True,
-                    start=start and t == order[0],
-                    stop=stop and t == order[-1],
-                )
+        def midpoint(first, last, planes):
+            cols = slice(first * CH, last * CH)
+            for t in planes:
+                factor = half_gain[t // 2][:, t % 2 : t % 2 + 1]
+                nc.vector.scalar_tensor_tensor(gh[t][:, cols], k[1][:, t, cols], factor, gy[t][:, cols], MULT, ADD)
 
-        def empty(name, bank, scale):
-            tile = sbuf(name, [P, PLANES, CH], F32)
-            nc.scalar.activation(tile[:].rearrange("p t c -> p (t c)"), banks[bank][:], ACT.Copy, scale=scale)
-            return tile
-
-        def add_first_velocity(c, bank, scale):
-            turn(bank, k[1, c], order=range(PLANES - 1, -1, -1), stop=True)
-            return empty(f"turned{c}", bank, scale)
-
-        def partial(c, odd, after=None):
-            tile = sbuf(f"part{c}_{odd}", [P, 2, CH], F32, after)
-            nc.vector.scalar_tensor_tensor(
-                tile[:], k[1, c][:, odd:PLANES:2, :], 0.25, state_planes(0, odd)[:, :, chunk(c)], MULT, ADD
-            )
-            return tile
+        def partial(c, odd):
+            y = state_planes(c // 2, odd)[:, :, chunk(c % 2)]
+            planes = slice(odd, PLANES, 2)
+            nc.vector.scalar_tensor_tensor(part[:, planes, chunk(c)], k[1][:, planes, chunk(c)], 0.25, y, MULT, ADD)
 
         out_rows = out_0.rearrange("(p t) s -> p t s", t=PLANES)
         out_words = out_1[0].rearrange("p n r -> p (n r)").bitcast(I32)
         out_codes = sbuf("out_codes", [P, S], U32)
+        out_scales = sbuf("out_scales", [P, S], U8)
+
+        def finish(c, planes, after=None):
+            if c not in result:
+                result[c] = sbuf(f"result{c}", [P, PLANES, CH], F32, after)
+            nc.vector.scalar_tensor_tensor(
+                result[c][:, planes, :], k[2][:, planes, chunk(c)], 0.25, part[:, planes, chunk(c)], MULT, ADD
+            )
 
         def store(c):
             nc.sync.dma_start(out_rows[:, :, chunk(c)], result[c][:])
-
-        def finish(c, parts):
-            result[c] = sbuf(f"result{c}", [P, PLANES, CH], F32)
-            for planes, part in parts:
-                nc.vector.scalar_tensor_tensor(result[c][:, planes, :], k[2, c][:, planes, :], 0.25, part, MULT, ADD)
-            store(c)
-
-        def pairs_of(bank):
-            planes = banks[bank][:].rearrange("p (t c) -> p t c", t=PLANES)
-            return [(pair, planes[:, pair, :]) for pair in (slice(0, 2), slice(2, 4))]
 
         def round_out(c, copy, after=None):
             rounded[c] = sbuf(f"rounded{c}", [P, PLANES * CH], BF16, after)
             weave(copy, rounded[c][:], result[c][:])
 
-        def quantise_out(half):
-            for c in (2 * half, 2 * half + 1):
-                pieces = (early, rounded[c]) if c == 2 else (rounded[c],)
-                for i, piece in enumerate(pieces):
-                    width = CH // len(pieces)
-                    at = slice(c * CH + i * width, c * CH + (i + 1) * width)
-                    nc.vector.quantize_mx(out=out_codes[:, at].bitcast(FP8X4), scales=out_scales[:, at], in_=piece[:])
+        def quantise_out(c):
+            nc.vector.quantize_mx(
+                out=out_codes[:, chunk(c)].bitcast(FP8X4), scales=out_scales[:, chunk(c)], in_=rounded[c][:]
+            )
+
+        def store_codes(half):
             cols = slice(half * HALF, (half + 1) * HALF)
             nc.sync.dma_start(out_words[:, cols], out_codes[:, cols].bitcast(I32))
 
-        four_y_high = sbuf("four_y_high", [P, PLANES, HALF], F32)
+        every = slice(0, PLANES)
+        low, high = slice(0, 2), slice(2, 4)
+
         for pair in (0, 2):
             for half in range(2):
                 state(pair, half)
                 state(pair + 1, half)
-        for odd in range(2):
-            keep_state(four_y_high, 1, odd)
-        four_y_0 = sbuf("four_y_0", [P, PLANES, CH], F32)
-        for odd in range(2):
-            keep_state(four_y_0, 0, odd, CH)
+
+        for t in (0, 1):
+            gather(1, 0, 2, (t,), on_vector)
+            gather(1, 2, 4, (t,), on_vector)
+        for t in (2, 3):
+            gather(1, 0, 1, (t,), on_scalar)
+            gather(1, 1, 2, (t,), on_scalar)
         for c in (2, 3):
-            turn(c, four_y_high[:, :, chunk(c - 2)], order=(0, 2, 1, 3), start=True)
-        turn(7, four_y_0, order=(0, 2, 1, 3), start=True)
-
-        first_rows = sbuf("first_rows", [P, 2 * PLANES * CH], F32)
-        both = first_rows[:].rearrange("p (t c) -> p t c", t=PLANES)
-        rows[1, 3] = sbuf("rows1_3", [P, PLANES, CH], F32, after="gain")[:]
-        rows[1, 0] = first_rows[:, : PLANES * CH].rearrange("p (t c) -> p t c", t=PLANES)
-        gather(both, 1, 1, 3)
-        for c in (1, 2):
-            rows[1, c] = both[:, :, chunk(c - 1)]
-            interleave(1, c, on_scalar)
-        gather(rows[1, 3], 1, 3, 4)
-        interleave(1, 3, on_scalar)
-        quantise(1, 1)
-        velocity(1, 1, (4, 4, 5, 5), 2)
-        gather(rows[1, 0], 1, 0, 1, order=(0, 2))
-        quantise(1, 2)
-        gather(rows[1, 0], 1, 0, 1, order=(1, 3))
-        interleave(1, 0, on_scalar, after="codes1_1")
-        velocity(1, 2, (6, 6, 6, 6), 2)
-        quantise(1, 3)
-        velocity(1, 3, (4, 4, 4, 4), 2)
-        midpoint(1)
-        part_even = partial(1, 0)
+            gather(1, c, c + 1, (2, 3), on_scalar)
+        interleave(1, 0)
+        interleave(1, 1)
         quantise(1, 0)
-        velocity(1, 0, (5, 5, 6, 6), 1)
-        for c in (2, 3, 0):
-            midpoint(c)
+        passes(1, 0, (4, 4, 5, 5))
+        velocity(1, 0, 4, low)
+        velocity(1, 0, 5, high)
+        interleave(1, 2)
+        quantise(1, 1)
+        passes(1, 1, (6, 6, 7, 7))
+        velocity(1, 1, 6, low)
+        velocity(1, 1, 7, high)
+        quantise(1, 2)
+        passes(1, 2, (4, 4, 5, 5))
+        velocity(1, 2, 4, low)
+        velocity(1, 2, 5, high)
+        interleave(1, 3, after="codes1_0")
+        midpoint(0, 1, (0, 1))
+        quantise(1, 3)
+        passes(1, 3, (6, 6, 7, 7))
+        velocity(1, 3, 6, low)
+        velocity(1, 3, 7, high)
+        midpoint(0, 1, (2, 3))
+        midpoint(1, 2, range(PLANES))
+        midpoint(2, 3, (0, 1))
+        midpoint(2, 3, (2,))
+        midpoint(3, 4, (0, 1))
+        midpoint(2, 3, (3,))
+        midpoint(3, 4, (2, 3))
 
-        turned = {2: add_first_velocity(2, 2, 1.0), 3: add_first_velocity(3, 3, 0.25)}
-        fetch(2, 2)
-        turned[0] = add_first_velocity(0, 7, 0.25)
-        interleave(2, 2, on_scalar, after="k1_0")
-        turn(2, turned[2], start=True)
-        turn(3, turned[3], start=True, stop=True)
-        turn(7, turned[0], start=True, stop=True)
-        fetch(2, 3, after="half_gain")
-        quantise(2, 2)
-        interleave(2, 3, on_scalar, after="k1_0")
-        k2_turned = sbuf("k2_turned", [P, PLANES, P], F32)
-        for pair in range(2):
-            acc = banks[4 + pair][:, :HALF]
-            nc.tensor.matmul_mx(
-                out=acc,
-                lhsT=codes[2, 2][:].bitcast(FP8X4),
-                lhsT_scale=scales[2, 2][:],
-                rhs=w2w[:, 2 * HALF * pair : 2 * HALF * (pair + 1)].bitcast(FP4X4),
-                rhs_scale=w2s[:, HALF * pair : HALF * (pair + 1)],
-                start=True,
-                stop=True,
-            )
-            nc.scalar.activation(
-                k2_turned[:, 2 * pair : 2 * pair + 2, :].rearrange("p t c -> p (t c)"), acc, ACT.Tanh
-            )
-        fetch(2, 0, after="rows2_2")
-        interleave(2, 0, on_scalar, after="codes2_2")
-        turn(2, k2_turned, stop=True)
-        result[2] = empty("result2", 2, 0.25)
-        early = sbuf("rounded2_early", [P, PLANES * CH // 2], BF16)
-        weave(
-            lambda out, in_: nc.scalar.activation(out, in_, ACT.Copy, scale=0.25),
-            early[:],
-            banks[2][:].rearrange("p (t c) -> p t c", t=PLANES)[:, :, : CH // 2],
-        )
-        quantise(2, 3)
-        velocity(2, 3, (5, 5, 5, 5), 2)
-        store(2)
-        fetch(2, 1, after="half_gain")
+        part = sbuf("part", [P, PLANES, S], F32, after="half_gain0")
+        gather(2, 0, 2, (0, 1, 2), on_scalar)
+        gather(2, 2, 3, (0, 1, 2), on_scalar)
+        gather(2, 3, 4, range(PLANES), on_scalar)
+        partial(0, 0)
+        gather(2, 0, 3, (3,), on_vector)
+        partial(0, 1)
+        interleave(2, 0)
+        interleave(2, 1)
         quantise(2, 0)
-        velocity(2, 0, (6, 6, 0, 0), 2)
-        interleave(2, 1, on_vector, after="rows2_2")
-        part_odd = partial(1, 1, after="codes2_2")
+        passes(2, 0, (4, 4, 4, 4))
+        velocity(2, 0, 4, every)
+        partial(1, 0)
         quantise(2, 1)
-        velocity(2, 1, (4, 1, 2, 5), 1)
-
-        rounded[2] = sbuf("rounded2", [P, PLANES * CH // 2], BF16, after="rows2_2")
-        nc.gpsimd.tensor_scalar(
-            rounded[2][:].rearrange("p (c t) -> p c t", t=PLANES),
-            result[2][:, :, CH // 2 :].rearrange("p t c -> p c t"),
-            1.0,
-            -0.0,
-            MULT,
-            ADD,
-        )
-        finish(3, pairs_of(3))
-        finish(0, pairs_of(7))
-        finish(1, [(t, (part_even, part_odd)[t % 2][:, t // 2, :]) for t in range(PLANES)])
-        out_scales = sbuf("out_scales", [P, S], U8, after="part1_0")
-        round_out(3, on_scalar)
-        rounded[0] = sbuf("rounded0", [P, PLANES * CH], BF16)
-        cut = 3 * CH // 4
-        weave(on_scalar, rounded[0][:, : PLANES * cut], result[0][:, :, :cut])
-        weave(on_vector, rounded[0][:, PLANES * cut :], result[0][:, :, cut:])
-        round_out(1, on_vector)
-        quantise_out(1)
+        passes(2, 1, (5, 5, 5, 5))
+        velocity(2, 1, 5, every)
+        interleave(2, 2)
+        partial(1, 1)
+        quantise(2, 2)
+        passes(2, 2, (6, 6, 6, 6))
+        velocity(2, 2, 6, every)
+        partial(2, 0)
+        partial(2, 1)
+        interleave(2, 3)
+        partial(3, 0)
+        quantise(2, 3)
+        last = (7, 0, 1, 4)
+        passes(2, 3, last)
+        partial(3, 1)
+        for t in range(PLANES):
+            velocity(2, 3, last[t], slice(t, t + 1))
+        for c in range(3):
+            finish(c, every)
+            store(c)
+        finish(3, low)
+        finish(3, high)
+        store(3)
+        round_out(0, on_scalar, after="codes2_3")
+        round_out(1, on_scalar)
+        round_out(2, on_scalar)
         quantise_out(0)
+        round_out(3, on_vector)
+        quantise_out(1)
+        store_codes(0)
+        quantise_out(2)
+        quantise_out(3)
+        store_codes(1)
         for q in range(4):
             queue = nc.sync if q % 2 == 0 else nc.scalar
             live = out_scales[32 * q : 32 * q + 4, :]

@@ -21,6 +21,7 @@ P = 128
 PLANES = 4
 CH = 128
 HALF = S // 2
+SLOT = 4 * PLANES * CH
 PER_COLUMN = 16
 PARKED = P - 16
 X_FIRST = T // 2
@@ -61,14 +62,22 @@ def tile_picked_heun_none_po_kernel(
     nc = tc.nc
     with ExitStack() as ctx:
         keep = ctx.enter_context(tc.tile_pool(name="keep", bufs=1))
+        slots = ctx.enter_context(tc.tile_pool(name="slots", bufs=1))
         psum = ctx.enter_context(tc.psum_pool(name="psum", bufs=1))
 
-        def sbuf(name, shape, dtype, after=None):
-            return keep.tile(shape, dtype, name=name, tag=after or name, align_bytes=64)
+        places, fresh = {}, []
+
+        def sbuf(name, shape, dtype, after=None, at=0, room=1):
+            if after:
+                places[name] = places[after] + at
+            else:
+                places[name] = SLOT * len(fresh)
+                fresh.extend([name] * room)
+            return slots.tile(shape, dtype, name=name, offset=places[name], align_bytes=64)
 
         offs_sb = keep.tile([P, S // PER_COLUMN], U16, name="offs_sb")
         nb_sb = keep.tile([P, S // PER_COLUMN], U16, name="nb_sb")
-        xw = sbuf("xw", [P, T], U32)
+        xw = keep.tile([P, T], U32, name="xw")
         xs = sbuf("xs", [P, T], U8)
         w1w_raw = sbuf("w1w_raw", [P, 2 * H], U8)
         w1s_raw = sbuf("w1s_raw", [P, H], U8)
@@ -121,8 +130,8 @@ def tile_picked_heun_none_po_kernel(
         gy = [keep.tile([P, S], F32, name=f"gy{t}") for t in range(PLANES)]
         gh = [keep.tile([P, S], F32, name=f"gh{t}") for t in range(PLANES)]
         windows = {1: gy, 2: gh}
-        woven, codes, scales, result, rounded = {}, {}, {}, {}, {}
-        k = {v: sbuf(f"k{v}", [P, PLANES, S], F32) for v in (1, 2)}
+        woven, codes, scales, part, result, rounded = {}, {}, {}, {}, {}, {}
+        k = {(v, c): sbuf(f"k{v}_{c}", [P, PLANES, CH], F32) for v in (1, 2) for c in range(S // CH)}
 
         def on_scalar(out, in_):
             nc.scalar.activation(out, in_, ACT.Copy)
@@ -149,55 +158,59 @@ def tile_picked_heun_none_po_kernel(
             product(acc, w1w, w1s, t, xqw[half][:], xqs[:, cols])
             nc.scalar.activation(gy[t][:, cols], acc, ACT.Copy, scale=gain[:, t : t + 1])
 
-        rows = {v: sbuf(f"rows{v}", [P, PLANES, S], F32) for v in (1, 2)}
+        rows = {}
 
-        def gather(v, first, last, planes, copy):
-            entries = nb_sb[:, first * CH // PER_COLUMN : last * CH // PER_COLUMN]
+        def rows_for(v, c, after=None, at=0, room=1):
+            rows[v, c] = sbuf(f"rows{v}_{c}", [P, PLANES, CH], F32, after, at, room)
+
+        def gather(v, c, planes, copy):
+            entries = nb_sb[:, c * CH // PER_COLUMN : (c + 1) * CH // PER_COLUMN]
             for t in planes:
-                copy(rows[v][:, t, first * CH : last * CH], windows[v][t][:].indirect(entries))
+                copy(rows[v, c][:, t, :], windows[v][t][:].indirect(entries))
 
-        def interleave(v, c, after=None):
-            woven[v, c] = sbuf(f"woven{v}_{c}", [P, PLANES * CH], BF16, after)
-            weave(on_vector, woven[v, c][:], rows[v][:, :, chunk(c)])
+        def interleave(v, c, after=None, at=0, copy=on_vector):
+            woven[v, c] = sbuf(f"woven{v}_{c}", [P, PLANES * CH], BF16, after, at)
+            weave(copy, woven[v, c][:], rows[v, c][:])
 
-        def quantise(v, c, after=None):
-            codes[v, c] = sbuf(f"codes{v}_{c}", [P, CH], U32, after)
+        def quantise(v, c, after=None, at=0):
+            codes[v, c] = sbuf(f"codes{v}_{c}", [P, CH], U32, after, at)
             scales[v, c] = sbuf(f"scales{v}_{c}", [P, CH], U8)
             nc.vector.quantize_mx(out=codes[v, c][:].bitcast(FP8X4), scales=scales[v, c][:], in_=woven[v, c][:])
 
-        def passes(v, c, into):
-            for t, bank in enumerate(into):
-                product(banks[bank][:, chunk(t)], w2w, w2s, t, codes[v, c][:], scales[v, c][:])
+        def passes(v, c, into, order=range(PLANES)):
+            for t in order:
+                product(banks[into[t]][:, chunk(t)], w2w, w2s, t, codes[v, c][:], scales[v, c][:])
 
         def velocity(v, c, bank, planes):
             acc = banks[bank][:].rearrange("p (t c) -> p t c", t=PLANES)
-            nc.scalar.activation(k[v][:, planes, chunk(c)], acc[:, planes, :], ACT.Tanh)
+            nc.scalar.activation(k[v, c][:, planes, :], acc[:, planes, :], ACT.Tanh)
 
-        def midpoint(first, last, planes):
-            cols = slice(first * CH, last * CH)
+        def midpoint(c, planes):
             for t in planes:
                 factor = half_gain[t // 2][:, t % 2 : t % 2 + 1]
-                nc.vector.scalar_tensor_tensor(gh[t][:, cols], k[1][:, t, cols], factor, gy[t][:, cols], MULT, ADD)
+                nc.vector.scalar_tensor_tensor(
+                    gh[t][:, chunk(c)], k[1, c][:, t, :], factor, gy[t][:, chunk(c)], MULT, ADD
+                )
 
-        def partial(c, odd):
+        def partial(c, odd, after=None):
+            part[c, odd] = sbuf(f"part{c}_{odd}", [P, 2, CH], F32, after)
             y = state_planes(c // 2, odd)[:, :, chunk(c % 2)]
-            planes = slice(odd, PLANES, 2)
-            nc.vector.scalar_tensor_tensor(part[:, planes, chunk(c)], k[1][:, planes, chunk(c)], 0.25, y, MULT, ADD)
+            nc.vector.scalar_tensor_tensor(part[c, odd][:], k[1, c][:, odd:PLANES:2, :], 0.25, y, MULT, ADD)
 
         out_rows = out_0.rearrange("(p t) s -> p t s", t=PLANES)
         out_words = out_1[0].rearrange("p n r -> p (n r)").bitcast(I32)
         out_codes = sbuf("out_codes", [P, S], U32)
-        out_scales = sbuf("out_scales", [P, S], U8)
 
-        def finish(c, planes, after=None):
+        def finish(c, odd, after=None):
             if c not in result:
                 result[c] = sbuf(f"result{c}", [P, PLANES, CH], F32, after)
+            planes = slice(odd, PLANES, 2)
             nc.vector.scalar_tensor_tensor(
-                result[c][:, planes, :], k[2][:, planes, chunk(c)], 0.25, part[:, planes, chunk(c)], MULT, ADD
+                result[c][:, planes, :], k[2, c][:, planes, :], 0.25, part[c, odd][:], MULT, ADD
             )
 
-        def store(c):
-            nc.sync.dma_start(out_rows[:, :, chunk(c)], result[c][:])
+        def store(c, planes):
+            nc.sync.dma_start(out_rows[:, planes, chunk(c)], result[c][:, planes, :])
 
         def round_out(c, copy, after=None):
             rounded[c] = sbuf(f"rounded{c}", [P, PLANES * CH], BF16, after)
@@ -208,33 +221,33 @@ def tile_picked_heun_none_po_kernel(
                 out=out_codes[:, chunk(c)].bitcast(FP8X4), scales=out_scales[:, chunk(c)], in_=rounded[c][:]
             )
 
-        def store_codes(half):
-            cols = slice(half * HALF, (half + 1) * HALF)
+        def store_codes(first, last):
+            cols = slice(first * CH, last * CH)
             nc.sync.dma_start(out_words[:, cols], out_codes[:, cols].bitcast(I32))
 
         every = slice(0, PLANES)
         low, high = slice(0, 2), slice(2, 4)
+        even, odd = slice(0, PLANES, 2), slice(1, PLANES, 2)
 
         for pair in (0, 2):
             for half in range(2):
                 state(pair, half)
                 state(pair + 1, half)
 
-        for t in (0, 1):
-            gather(1, 0, 2, (t,), on_vector)
-            gather(1, 2, 4, (t,), on_vector)
-        for t in (2, 3):
-            gather(1, 0, 1, (t,), on_scalar)
-            gather(1, 1, 2, (t,), on_scalar)
+        for c in range(4):
+            rows_for(1, c)
+        for t in range(PLANES):
+            gather(1, 0, (t,), on_vector)
+            gather(1, 1, (t,), on_vector)
         for c in (2, 3):
-            gather(1, c, c + 1, (2, 3), on_scalar)
+            gather(1, c, range(PLANES), on_scalar)
         interleave(1, 0)
         interleave(1, 1)
         quantise(1, 0)
         passes(1, 0, (4, 4, 5, 5))
         velocity(1, 0, 4, low)
         velocity(1, 0, 5, high)
-        interleave(1, 2)
+        interleave(1, 2, after="rows1_0")
         quantise(1, 1)
         passes(1, 1, (6, 6, 7, 7))
         velocity(1, 1, 6, low)
@@ -243,67 +256,76 @@ def tile_picked_heun_none_po_kernel(
         passes(1, 2, (4, 4, 5, 5))
         velocity(1, 2, 4, low)
         velocity(1, 2, 5, high)
-        interleave(1, 3, after="codes1_0")
-        midpoint(0, 1, (0, 1))
+        interleave(1, 3, after="woven1_1")
+        midpoint(0, (0, 1))
         quantise(1, 3)
         passes(1, 3, (6, 6, 7, 7))
         velocity(1, 3, 6, low)
         velocity(1, 3, 7, high)
-        midpoint(0, 1, (2, 3))
-        midpoint(1, 2, range(PLANES))
-        midpoint(2, 3, (0, 1))
-        midpoint(2, 3, (2,))
-        midpoint(3, 4, (0, 1))
-        midpoint(2, 3, (3,))
-        midpoint(3, 4, (2, 3))
+        midpoint(0, (2, 3))
+        for c in (1, 2, 3):
+            midpoint(c, range(PLANES))
 
-        part = sbuf("part", [P, PLANES, S], F32, after="half_gain0")
-        gather(2, 0, 2, (0, 1, 2), on_scalar)
-        gather(2, 2, 3, (0, 1, 2), on_scalar)
-        gather(2, 3, 4, range(PLANES), on_scalar)
-        partial(0, 0)
-        gather(2, 0, 3, (3,), on_vector)
-        partial(0, 1)
-        interleave(2, 0)
-        interleave(2, 1)
-        quantise(2, 0)
-        passes(2, 0, (4, 4, 4, 4))
-        velocity(2, 0, 4, every)
-        partial(1, 0)
-        quantise(2, 1)
-        passes(2, 1, (5, 5, 5, 5))
-        velocity(2, 1, 5, every)
-        interleave(2, 2)
-        partial(1, 1)
-        quantise(2, 2)
-        passes(2, 2, (6, 6, 6, 6))
-        velocity(2, 2, 6, every)
-        partial(2, 0)
-        partial(2, 1)
-        interleave(2, 3)
-        partial(3, 0)
-        quantise(2, 3)
-        last = (7, 0, 1, 4)
-        passes(2, 3, last)
-        partial(3, 1)
-        for t in range(PLANES):
-            velocity(2, 3, last[t], slice(t, t + 1))
         for c in range(3):
-            finish(c, every)
-            store(c)
-        finish(3, low)
-        finish(3, high)
-        store(3)
-        round_out(0, on_scalar, after="codes2_3")
-        round_out(1, on_scalar)
+            rows_for(2, c, room=2)
+        gather(2, 0, range(PLANES), on_scalar)
+        for c in (1, 2):
+            gather(2, c, (1, 2, 3), on_scalar)
+            gather(2, c, (0,), on_vector)
+        partial(0, 0, after="half_gain0")
+        partial(0, 1, after="half_gain1")
+        interleave(2, 0)
+        partial(1, 0, after="k1_0")
+        quantise(2, 0, after="rows2_1", at=SLOT)
+        passes(2, 0, (4, 4, 5, 5))
+        velocity(2, 0, 4, low)
+        velocity(2, 0, 5, high)
+        partial(1, 1, after="rows2_0")
+        interleave(2, 1, after="rows2_0", at=SLOT // 2)
+        partial(2, 0, after="k1_1")
+        quantise(2, 1)
+        passes(2, 1, (6, 6, 6, 6))
+        rows_for(2, 3, after="rows2_1", at=SLOT // 2)
+        gather(2, 3, (1, 2, 3), on_scalar)
+        velocity(2, 1, 6, every)
+        interleave(2, 2, after="rows2_1")
+        gather(2, 3, (0,), on_vector)
+        quantise(2, 2)
+        passes(2, 2, (7, 7, 7, 7))
+        velocity(2, 2, 7, every)
+        finish(0, 0, after="rows2_2")
+        finish(0, 1)
+        store(0, every)
+        round_out(0, on_scalar, after="codes2_2")
+        partial(2, 1, after="woven2_2")
+        interleave(2, 3)
+        partial(3, 0, after="k1_2")
+        quantise(2, 3)
+        last = (4, 5, 0, 1)
+        passes(2, 3, last, order=(0, 2, 1, 3))
+        for t in (0, 2, 1, 3):
+            velocity(2, 3, last[t], slice(t, t + 1))
+        finish(1, 0, after="rows2_3")
+        finish(1, 1)
+        store(1, every)
+        round_out(1, on_scalar, after="codes2_3")
+        partial(3, 1, after="woven2_3")
+        finish(2, 0, after="k2_1")
+        finish(2, 1)
+        store(2, every)
         round_out(2, on_scalar)
+        out_scales = sbuf("out_scales", [P, S], U8, after="k1_3")
         quantise_out(0)
-        round_out(3, on_vector)
+        finish(3, 0)
+        store(3, even)
+        finish(3, 1)
+        store(3, odd)
         quantise_out(1)
-        store_codes(0)
+        store_codes(0, 2)
+        round_out(3, on_vector)
         quantise_out(2)
         quantise_out(3)
-        store_codes(1)
+        store_codes(2, 4)
         for q in range(4):
             queue = nc.sync if q % 2 == 0 else nc.scalar
             live = out_scales[32 * q : 32 * q + 4, :]

@@ -22,6 +22,7 @@ PLANES = 4
 CH = 128
 HALF = S // 2
 SLOT = 4 * PLANES * CH
+EVEN_FIRST = (0, 2, 1, 3)
 PER_COLUMN = 16
 PARKED = P - 16
 X_FIRST = T // 2
@@ -85,7 +86,7 @@ def tile_picked_heun_none_po_kernel(
         xqs = sbuf("xqs", [P, S], U8)
         w2s = sbuf("w2s", [P, H], U8)
         gain = sbuf("gain", [P, PLANES], F32)
-        half_gain = [sbuf(f"half_gain{pair}", [P, 2], F32) for pair in range(2)]
+        half_gain = [sbuf(f"half_gain{odd}", [P, 2], F32) for odd in range(2)]
 
         nc.gpsimd.memset(w1s_raw[:].bitcast(F32), 0.0)
         nc.vector.memset(xs[:PARKED, :].bitcast(I32), 0)
@@ -111,8 +112,8 @@ def tile_picked_heun_none_po_kernel(
         xqs_parked = sbuf("parked", [P, S], U8)
         w2s_parked = sbuf("w2s_parked", [P, H], U8)
 
-        for pair in range(2):
-            nc.scalar.activation(half_gain[pair][:], gain[:, 2 * pair : 2 * pair + 2], ACT.Copy, scale=0.5)
+        for odd in range(2):
+            nc.scalar.activation(half_gain[odd][:], gain[:, odd:PLANES:2], ACT.Copy, scale=0.5)
         nc.vector.tensor_copy(xqs_parked[:], xs[:].indirect(offs_sb[:]))
         deal(nc, w1w[:].bitcast(U16), w1w_raw[:].bitcast(U16))
         unpark(nc, xqs, xqs_parked)
@@ -131,12 +132,16 @@ def tile_picked_heun_none_po_kernel(
         gh = [keep.tile([P, S], F32, name=f"gh{t}") for t in range(PLANES)]
         windows = {1: gy, 2: gh}
         woven, codes, scales, part, result, rounded = {}, {}, {}, {}, {}, {}
-        k = {(v, c): sbuf(f"k{v}_{c}", [P, PLANES, CH], F32) for v in (1, 2) for c in range(S // CH)}
+        k1 = {(c, odd): sbuf(f"k1_{c}_{odd}", [P, 2, CH], F32) for c in range(S // CH) for odd in range(2)}
+        k2 = [sbuf(f"k2_{c}", [P, PLANES, CH], F32) for c in range(S // CH)]
 
         def on_scalar(out, in_):
             nc.scalar.activation(out, in_, ACT.Copy)
 
         on_vector = nc.vector.tensor_copy
+
+        def on_gpsimd(out, in_):
+            nc.gpsimd.tensor_scalar(out, in_, 1.0, -0.0, MULT, ADD)
 
         def product(acc, words, word_scales, t, moving, moving_scales):
             nc.tensor.matmul_mx(
@@ -160,53 +165,65 @@ def tile_picked_heun_none_po_kernel(
 
         rows = {}
 
-        def rows_for(v, c, after=None, at=0, room=1):
-            rows[v, c] = sbuf(f"rows{v}_{c}", [P, PLANES, CH], F32, after, at, room)
+        def rows_for(v, first, last):
+            count = last - first
+            tile = sbuf(f"rows{v}_{first}", [P, PLANES, count * CH], F32, room=count)
+            for c in range(first, last):
+                rows[v, c] = (tile[:], first)
 
-        def gather(v, c, planes, copy):
-            entries = nb_sb[:, c * CH // PER_COLUMN : (c + 1) * CH // PER_COLUMN]
+        def gather(v, first, last, planes, copy):
+            entries = nb_sb[:, first * CH // PER_COLUMN : last * CH // PER_COLUMN]
+            tile, start = rows[v, first]
             for t in planes:
-                copy(rows[v, c][:, t, :], windows[v][t][:].indirect(entries))
+                copy(tile[:, t, (first - start) * CH : (last - start) * CH], windows[v][t][:].indirect(entries))
 
         def interleave(v, c, after=None, at=0, copy=on_vector):
             woven[v, c] = sbuf(f"woven{v}_{c}", [P, PLANES * CH], BF16, after, at)
-            weave(copy, woven[v, c][:], rows[v, c][:])
+            tile, start = rows[v, c]
+            weave(copy, woven[v, c][:], tile[:, :, chunk(c - start)])
 
         def quantise(v, c, after=None, at=0):
             codes[v, c] = sbuf(f"codes{v}_{c}", [P, CH], U32, after, at)
             scales[v, c] = sbuf(f"scales{v}_{c}", [P, CH], U8)
             nc.vector.quantize_mx(out=codes[v, c][:].bitcast(FP8X4), scales=scales[v, c][:], in_=woven[v, c][:])
 
-        def passes(v, c, into, order=range(PLANES)):
-            for t in order:
+        def passes(v, c, into):
+            for t in EVEN_FIRST:
                 product(banks[into[t]][:, chunk(t)], w2w, w2s, t, codes[v, c][:], scales[v, c][:])
 
-        def velocity(v, c, bank, planes):
+        def tanh(out, bank, planes):
             acc = banks[bank][:].rearrange("p (t c) -> p t c", t=PLANES)
-            nc.scalar.activation(k[v, c][:, planes, :], acc[:, planes, :], ACT.Tanh)
+            nc.scalar.activation(out, acc[:, planes, :], ACT.Tanh)
+
+        def first_velocity(c, even_bank, odd_bank):
+            passes(1, c, (even_bank, odd_bank) * 2)
+            tanh(k1[c, 0][:], even_bank, even)
+            tanh(k1[c, 1][:], odd_bank, odd)
+
+        def second_velocity(c, bank, planes):
+            tanh(k2[c][:, planes, :], bank, planes)
 
         def midpoint(c, planes):
             for t in planes:
-                factor = half_gain[t // 2][:, t % 2 : t % 2 + 1]
+                factor = half_gain[t % 2][:, t // 2 : t // 2 + 1]
                 nc.vector.scalar_tensor_tensor(
-                    gh[t][:, chunk(c)], k[1, c][:, t, :], factor, gy[t][:, chunk(c)], MULT, ADD
+                    gh[t][:, chunk(c)], k1[c, t % 2][:, t // 2, :], factor, gy[t][:, chunk(c)], MULT, ADD
                 )
 
-        def partial(c, odd, after=None):
-            part[c, odd] = sbuf(f"part{c}_{odd}", [P, 2, CH], F32, after)
-            y = state_planes(c // 2, odd)[:, :, chunk(c % 2)]
-            nc.vector.scalar_tensor_tensor(part[c, odd][:], k[1, c][:, odd:PLANES:2, :], 0.25, y, MULT, ADD)
+        def partial(c, planes, after=None, at=0):
+            tile = part[c, planes.start] = sbuf(f"part{c}_{planes.start}", [P, 2, CH], F32, after, at)
+            y = state_planes(c // 2, planes.start)[:, :, chunk(c % 2)]
+            nc.vector.scalar_tensor_tensor(tile[:], k1[c, planes.start][:], 0.25, y, MULT, ADD)
 
         out_rows = out_0.rearrange("(p t) s -> p t s", t=PLANES)
         out_words = out_1[0].rearrange("p n r -> p (n r)").bitcast(I32)
         out_codes = sbuf("out_codes", [P, S], U32)
 
-        def finish(c, odd, after=None):
+        def finish(c, planes, after=None, at=0):
             if c not in result:
-                result[c] = sbuf(f"result{c}", [P, PLANES, CH], F32, after)
-            planes = slice(odd, PLANES, 2)
+                result[c] = sbuf(f"result{c}", [P, PLANES, CH], F32, after, at)
             nc.vector.scalar_tensor_tensor(
-                result[c][:, planes, :], k[2, c][:, planes, :], 0.25, part[c, odd][:], MULT, ADD
+                result[c][:, planes, :], k2[c][:, planes, :], 0.25, part[c, planes.start][:], MULT, ADD
             )
 
         def store(c, planes):
@@ -225,104 +242,95 @@ def tile_picked_heun_none_po_kernel(
             cols = slice(first * CH, last * CH)
             nc.sync.dma_start(out_words[:, cols], out_codes[:, cols].bitcast(I32))
 
-        every = slice(0, PLANES)
-        low, high = slice(0, 2), slice(2, 4)
-        even, odd = slice(0, PLANES, 2), slice(1, PLANES, 2)
+        every, even, odd = slice(0, PLANES), slice(0, PLANES, 2), slice(1, PLANES, 2)
 
         for pair in (0, 2):
             for half in range(2):
                 state(pair, half)
                 state(pair + 1, half)
 
-        for c in range(4):
-            rows_for(1, c)
+        rows_for(1, 0, 1)
+        rows_for(1, 1, 2)
+        rows_for(1, 2, 4)
         for t in range(PLANES):
-            gather(1, 0, (t,), on_vector)
-            gather(1, 1, (t,), on_vector)
-        for c in (2, 3):
-            gather(1, c, range(PLANES), on_scalar)
+            gather(1, 0, 1, (t,), on_vector)
+            gather(1, 1, 2, (t,), on_vector)
+        gather(1, 2, 4, (0, 1, 2), on_scalar)
+        gather(1, 2, 3, (3,), on_scalar)
+        gather(1, 3, 4, (3,), on_scalar)
         interleave(1, 0)
         interleave(1, 1)
         quantise(1, 0)
-        passes(1, 0, (4, 4, 5, 5))
-        velocity(1, 0, 4, low)
-        velocity(1, 0, 5, high)
-        interleave(1, 2, after="rows1_0")
+        first_velocity(0, 4, 5)
         quantise(1, 1)
-        passes(1, 1, (6, 6, 7, 7))
-        velocity(1, 1, 6, low)
-        velocity(1, 1, 7, high)
+        first_velocity(1, 6, 7)
+        interleave(1, 2, after="rows1_1")
+        interleave(1, 3, after="rows1_1", at=SLOT // 2)
         quantise(1, 2)
-        passes(1, 2, (4, 4, 5, 5))
-        velocity(1, 2, 4, low)
-        velocity(1, 2, 5, high)
-        interleave(1, 3, after="woven1_1")
-        midpoint(0, (0, 1))
+        first_velocity(2, 4, 5)
+        midpoint(0, EVEN_FIRST[:1])
         quantise(1, 3)
-        passes(1, 3, (6, 6, 7, 7))
-        velocity(1, 3, 6, low)
-        velocity(1, 3, 7, high)
-        midpoint(0, (2, 3))
+        first_velocity(3, 6, 7)
+        midpoint(0, EVEN_FIRST[1:])
         for c in (1, 2, 3):
-            midpoint(c, range(PLANES))
+            midpoint(c, EVEN_FIRST)
 
-        for c in range(3):
-            rows_for(2, c, room=2)
-        gather(2, 0, range(PLANES), on_scalar)
-        for c in (1, 2):
-            gather(2, c, (1, 2, 3), on_scalar)
-            gather(2, c, (0,), on_vector)
-        partial(0, 0, after="half_gain0")
-        partial(0, 1, after="half_gain1")
+        rows_for(2, 0, 1)
+        later = sbuf("rows2_1", [P, (3 * PLANES - 1) * CH], F32, room=3)
+        rows[2, 1] = rows[2, 2] = (later[:, : 2 * PLANES * CH].rearrange("p (t c) -> p t c", t=PLANES), 1)
+        rows[2, 3] = (later[:, (2 * PLANES - 1) * CH :].rearrange("p (t c) -> p t c", t=PLANES), 3)
+        gather(2, 0, 1, EVEN_FIRST, on_vector)
+        gather(2, 1, 3, EVEN_FIRST, on_scalar)
+        gather(2, 3, 4, (1, 2, 3), on_scalar)
+        partial(0, even, after="half_gain1")
         interleave(2, 0)
-        partial(1, 0, after="k1_0")
-        quantise(2, 0, after="rows2_1", at=SLOT)
-        passes(2, 0, (4, 4, 5, 5))
-        velocity(2, 0, 4, low)
-        velocity(2, 0, 5, high)
-        partial(1, 1, after="rows2_0")
+        partial(0, odd, after="k1_0_0")
+        quantise(2, 0)
+        passes(2, 0, (4, 5, 4, 5))
+        second_velocity(0, 4, even)
+        second_velocity(0, 5, odd)
+        partial(1, even, after="rows2_0")
         interleave(2, 1, after="rows2_0", at=SLOT // 2)
-        partial(2, 0, after="k1_1")
+        interleave(2, 2, after="k1_0_1")
+        gather(2, 3, 4, (0,), on_scalar)
         quantise(2, 1)
         passes(2, 1, (6, 6, 6, 6))
-        rows_for(2, 3, after="rows2_1", at=SLOT // 2)
-        gather(2, 3, (1, 2, 3), on_scalar)
-        velocity(2, 1, 6, every)
-        interleave(2, 2, after="rows2_1")
-        gather(2, 3, (0,), on_vector)
+        second_velocity(1, 6, every)
+        partial(1, odd, after="codes2_0")
         quantise(2, 2)
         passes(2, 2, (7, 7, 7, 7))
-        velocity(2, 2, 7, every)
-        finish(0, 0, after="rows2_2")
-        finish(0, 1)
+        second_velocity(2, 7, every)
+        partial(2, even, after="woven2_1")
+        partial(2, odd, after="k1_1_1")
+        finish(0, even, after="woven2_2")
+        interleave(2, 3)
+        finish(0, odd)
         store(0, every)
         round_out(0, on_scalar, after="codes2_2")
-        partial(2, 1, after="woven2_2")
-        interleave(2, 3)
-        partial(3, 0, after="k1_2")
         quantise(2, 3)
         last = (4, 5, 0, 1)
-        passes(2, 3, last, order=(0, 2, 1, 3))
-        for t in (0, 2, 1, 3):
-            velocity(2, 3, last[t], slice(t, t + 1))
-        finish(1, 0, after="rows2_3")
-        finish(1, 1)
+        passes(2, 3, last)
+        for t in EVEN_FIRST:
+            second_velocity(3, last[t], slice(t, t + 1))
+        finish(1, even, after="rows2_1")
+        finish(1, odd)
         store(1, every)
         round_out(1, on_scalar, after="codes2_3")
-        partial(3, 1, after="woven2_3")
-        finish(2, 0, after="k2_1")
-        finish(2, 1)
+        partial(3, even, after="woven2_3")
+        finish(2, even, after="k2_1")
+        finish(2, odd)
         store(2, every)
         round_out(2, on_scalar)
-        out_scales = sbuf("out_scales", [P, S], U8, after="k1_3")
-        quantise_out(0)
-        finish(3, 0)
+        partial(3, odd, after="k1_3_0")
+        out_scales = sbuf("out_scales", [P, S], U8, after="k1_3_1")
+        finish(3, even)
         store(3, even)
-        finish(3, 1)
+        finish(3, odd)
         store(3, odd)
+        quantise_out(0)
+        round_out(3, on_vector)
         quantise_out(1)
         store_codes(0, 2)
-        round_out(3, on_vector)
         quantise_out(2)
         quantise_out(3)
         store_codes(2, 4)

@@ -86,7 +86,7 @@ def tile_picked_heun_none_po_kernel(
         xqs = sbuf("xqs", [P, S], U8)
         w2s = sbuf("w2s", [P, H], U8)
         gain = sbuf("gain", [P, PLANES], F32)
-        half_gain = [sbuf(f"half_gain{odd}", [P, 2], F32) for odd in range(2)]
+        half_gain = sbuf("half_gain", [P, PLANES], F32)
 
         nc.gpsimd.memset(w1s_raw[:].bitcast(F32), 0.0)
         nc.vector.memset(xs[:PARKED, :].bitcast(I32), 0)
@@ -112,8 +112,7 @@ def tile_picked_heun_none_po_kernel(
         xqs_parked = sbuf("parked", [P, S], U8)
         w2s_parked = sbuf("w2s_parked", [P, H], U8)
 
-        for odd in range(2):
-            nc.scalar.activation(half_gain[odd][:], gain[:, odd:PLANES:2], ACT.Copy, scale=0.5)
+        nc.scalar.activation(half_gain[:], gain[:], ACT.Copy, scale=0.5)
         nc.vector.tensor_copy(xqs_parked[:], xs[:].indirect(offs_sb[:]))
         deal(nc, w1w[:].bitcast(U16), w1w_raw[:].bitcast(U16))
         unpark(nc, xqs, xqs_parked)
@@ -128,7 +127,7 @@ def tile_picked_heun_none_po_kernel(
         deal(nc, w2w[:].bitcast(U16), w2w_raw[:].bitcast(U16))
 
         banks = [psum.tile([P, S], F32, name=f"bank{b}") for b in range(8)]
-        gy = [keep.tile([P, S], F32, name=f"gy{t}") for t in range(PLANES)]
+        gy = [sbuf(f"gy{t}", [P, S], F32) for t in range(PLANES)]
         gh = [keep.tile([P, S], F32, name=f"gh{t}") for t in range(PLANES)]
         windows = {1: gy, 2: gh}
         woven, codes, scales, part, result, rounded = {}, {}, {}, {}, {}, {}
@@ -140,8 +139,6 @@ def tile_picked_heun_none_po_kernel(
 
         on_vector = nc.vector.tensor_copy
 
-        def on_gpsimd(out, in_):
-            nc.gpsimd.tensor_scalar(out, in_, 1.0, -0.0, MULT, ADD)
 
         def product(acc, words, word_scales, t, moving, moving_scales):
             nc.tensor.matmul_mx(
@@ -165,27 +162,22 @@ def tile_picked_heun_none_po_kernel(
 
         rows = {}
 
-        def rows_for(v, first, last):
-            count = last - first
-            tile = sbuf(f"rows{v}_{first}", [P, PLANES, count * CH], F32, room=count)
-            for c in range(first, last):
-                rows[v, c] = (tile[:], first)
+        def rows_for(v, c, after=None):
+            rows[v, c] = sbuf(f"rows{v}_{c}", [P, PLANES, CH], F32, after)[:]
 
-        def gather(v, first, last, planes, copy):
-            entries = nb_sb[:, first * CH // PER_COLUMN : last * CH // PER_COLUMN]
-            tile, start = rows[v, first]
+        def gather(v, c, planes, copy):
+            entries = nb_sb[:, c * CH // PER_COLUMN : (c + 1) * CH // PER_COLUMN]
             for t in planes:
-                copy(tile[:, t, (first - start) * CH : (last - start) * CH], windows[v][t][:].indirect(entries))
+                copy(rows[v, c][:, t, :], windows[v][t][:].indirect(entries))
 
-        def interleave(v, c, after=None, at=0, copy=on_vector):
-            woven[v, c] = sbuf(f"woven{v}_{c}", [P, PLANES * CH], BF16, after, at)
-            tile, start = rows[v, c]
-            weave(copy, woven[v, c][:], tile[:, :, chunk(c - start)])
+        def interleave(v, c, after=None, at=0):
+            woven[v, c] = sbuf(f"woven{v}_{c}", [P, PLANES * CH], BF16, after, at)[:]
+            weave(on_vector, woven[v, c], rows[v, c])
 
         def quantise(v, c, after=None, at=0):
             codes[v, c] = sbuf(f"codes{v}_{c}", [P, CH], U32, after, at)
             scales[v, c] = sbuf(f"scales{v}_{c}", [P, CH], U8)
-            nc.vector.quantize_mx(out=codes[v, c][:].bitcast(FP8X4), scales=scales[v, c][:], in_=woven[v, c][:])
+            nc.vector.quantize_mx(out=codes[v, c][:].bitcast(FP8X4), scales=scales[v, c][:], in_=woven[v, c])
 
         def passes(v, c, into):
             for t in EVEN_FIRST:
@@ -205,7 +197,7 @@ def tile_picked_heun_none_po_kernel(
 
         def midpoint(c, planes):
             for t in planes:
-                factor = half_gain[t % 2][:, t // 2 : t // 2 + 1]
+                factor = half_gain[:, t : t + 1]
                 nc.vector.scalar_tensor_tensor(
                     gh[t][:, chunk(c)], k1[c, t % 2][:, t // 2, :], factor, gy[t][:, chunk(c)], MULT, ADD
                 )
@@ -249,80 +241,91 @@ def tile_picked_heun_none_po_kernel(
                 state(pair, half)
                 state(pair + 1, half)
 
-        rows_for(1, 0, 1)
-        rows_for(1, 1, 2)
-        rows_for(1, 2, 4)
-        for t in range(PLANES):
-            gather(1, 0, 1, (t,), on_vector)
-            gather(1, 1, 2, (t,), on_vector)
-        gather(1, 2, 4, (0, 1, 2), on_scalar)
-        gather(1, 2, 3, (3,), on_scalar)
-        gather(1, 3, 4, (3,), on_scalar)
+        shared = sbuf("rows1_shared", [P, 2 * PLANES * CH], F32, room=2)
+        for c, start in ((0, 0), (1, PLANES * CH), (3, CH)):
+            rows[1, c] = shared[:, start : start + PLANES * CH].rearrange("p (t c) -> p t c", t=PLANES)
+        rows_for(1, 2)
+        for t in (0, 1):
+            gather(1, 0, (t,), on_vector)
+            gather(1, 1, (t,), on_vector)
+        gather(1, 0, (2, 3), on_vector)
+        gather(1, 1, (3,), on_vector)
+        gather(1, 1, (2,), on_scalar)
+        gather(1, 2, range(PLANES), on_scalar)
         interleave(1, 0)
         interleave(1, 1)
+        gather(1, 3, (1, 2), on_scalar)
         quantise(1, 0)
         first_velocity(0, 4, 5)
+        gather(1, 3, (0,), on_vector)
         quantise(1, 1)
         first_velocity(1, 6, 7)
-        interleave(1, 2, after="rows1_1")
-        interleave(1, 3, after="rows1_1", at=SLOT // 2)
+        woven[1, 2] = shared[:, (PLANES + 1) * CH : (PLANES + 3) * CH].bitcast(BF16)
+        weave(on_vector, woven[1, 2], rows[1, 2])
+        gather(1, 3, (3,), on_vector)
         quantise(1, 2)
         first_velocity(2, 4, 5)
-        midpoint(0, EVEN_FIRST[:1])
+        interleave(1, 3, after="rows1_2")
+        midpoint(0, EVEN_FIRST[:2])
         quantise(1, 3)
         first_velocity(3, 6, 7)
-        midpoint(0, EVEN_FIRST[1:])
-        for c in (1, 2, 3):
-            midpoint(c, EVEN_FIRST)
+        midpoint(0, EVEN_FIRST[2:])
+        midpoint(1, EVEN_FIRST)
+        midpoint(2, EVEN_FIRST[:3])
+        midpoint(3, EVEN_FIRST[:2])
+        midpoint(2, EVEN_FIRST[3:])
+        midpoint(3, EVEN_FIRST[2:])
 
-        rows_for(2, 0, 1)
-        later = sbuf("rows2_1", [P, (3 * PLANES - 1) * CH], F32, room=3)
-        rows[2, 1] = rows[2, 2] = (later[:, : 2 * PLANES * CH].rearrange("p (t c) -> p t c", t=PLANES), 1)
-        rows[2, 3] = (later[:, (2 * PLANES - 1) * CH :].rearrange("p (t c) -> p t c", t=PLANES), 3)
-        gather(2, 0, 1, EVEN_FIRST, on_vector)
-        gather(2, 1, 3, EVEN_FIRST, on_scalar)
-        gather(2, 3, 4, (1, 2, 3), on_scalar)
-        partial(0, even, after="half_gain1")
+        rows_for(2, 0)
+        rows_for(2, 1)
+        gather(2, 0, (0, 2), on_scalar)
+        gather(2, 0, (1, 3), on_vector)
+        gather(2, 1, EVEN_FIRST, on_scalar)
+        partial(0, even, after="gy3")
         interleave(2, 0)
+        rows_for(2, 2, after="rows2_0")
+        gather(2, 2, (0, 2), on_scalar)
         partial(0, odd, after="k1_0_0")
         quantise(2, 0)
         passes(2, 0, (4, 5, 4, 5))
         second_velocity(0, 4, even)
         second_velocity(0, 5, odd)
-        partial(1, even, after="rows2_0")
-        interleave(2, 1, after="rows2_0", at=SLOT // 2)
-        interleave(2, 2, after="k1_0_1")
-        gather(2, 3, 4, (0,), on_scalar)
+        rows_for(2, 3, after="codes2_0")
+        gather(2, 3, EVEN_FIRST, on_scalar)
+        gather(2, 2, (1, 3), on_vector)
+        partial(1, even, after="k1_0_1")
+        interleave(2, 1, after="woven2_0")
+        partial(1, odd, after="k1_1_0")
         quantise(2, 1)
         passes(2, 1, (6, 6, 6, 6))
         second_velocity(1, 6, every)
-        partial(1, odd, after="codes2_0")
+        interleave(2, 2, after="rows2_1")
+        partial(2, even, after="rows2_1", at=SLOT // 2)
         quantise(2, 2)
         passes(2, 2, (7, 7, 7, 7))
         second_velocity(2, 7, every)
-        partial(2, even, after="woven2_1")
-        partial(2, odd, after="k1_1_1")
-        finish(0, even, after="woven2_2")
-        interleave(2, 3)
+        finish(0, even, after="rows2_2")
         finish(0, odd)
         store(0, every)
         round_out(0, on_scalar, after="codes2_2")
+        partial(2, odd, after="woven2_2")
+        interleave(2, 3)
+        partial(3, even, after="k1_2_1")
         quantise(2, 3)
         last = (4, 5, 0, 1)
         passes(2, 3, last)
         for t in EVEN_FIRST:
             second_velocity(3, last[t], slice(t, t + 1))
-        finish(1, even, after="rows2_1")
+        finish(1, even, after="rows2_3")
         finish(1, odd)
         store(1, every)
         round_out(1, on_scalar, after="codes2_3")
-        partial(3, even, after="woven2_3")
-        finish(2, even, after="k2_1")
+        finish(2, even, after="woven2_3")
         finish(2, odd)
         store(2, every)
         round_out(2, on_scalar)
-        partial(3, odd, after="k1_3_0")
-        out_scales = sbuf("out_scales", [P, S], U8, after="k1_3_1")
+        partial(3, odd, after="k2_1")
+        out_scales = sbuf("out_scales", [P, S], U8, after="part3_0")
         finish(3, even)
         store(3, even)
         finish(3, odd)

@@ -162,8 +162,8 @@ def tile_picked_heun_none_po_kernel(
 
         rows = {}
 
-        def rows_for(v, c, after=None):
-            rows[v, c] = sbuf(f"rows{v}_{c}", [P, PLANES, CH], F32, after)[:]
+        def rows_for(v, c, after=None, at=0, room=1):
+            rows[v, c] = sbuf(f"rows{v}_{c}", [P, PLANES, CH], F32, after, at, room)[:]
 
         def gather(v, c, planes, copy):
             entries = nb_sb[:, c * CH // PER_COLUMN : (c + 1) * CH // PER_COLUMN]
@@ -179,8 +179,8 @@ def tile_picked_heun_none_po_kernel(
             scales[v, c] = sbuf(f"scales{v}_{c}", [P, CH], U8)
             nc.vector.quantize_mx(out=codes[v, c][:].bitcast(FP8X4), scales=scales[v, c][:], in_=woven[v, c])
 
-        def passes(v, c, into):
-            for t in EVEN_FIRST:
+        def passes(v, c, into, order=EVEN_FIRST):
+            for t in order:
                 product(banks[into[t]][:, chunk(t)], w2w, w2s, t, codes[v, c][:], scales[v, c][:])
 
         def tanh(out, bank, planes):
@@ -244,7 +244,7 @@ def tile_picked_heun_none_po_kernel(
         shared = sbuf("rows1_shared", [P, 2 * PLANES * CH], F32, room=2)
         for c, start in ((0, 0), (1, PLANES * CH), (3, CH)):
             rows[1, c] = shared[:, start : start + PLANES * CH].rearrange("p (t c) -> p t c", t=PLANES)
-        rows_for(1, 2)
+        rows_for(1, 2, after="gain")
         for t in (0, 1):
             gather(1, 0, (t,), on_vector)
             gather(1, 1, (t,), on_vector)
@@ -268,39 +268,43 @@ def tile_picked_heun_none_po_kernel(
         interleave(1, 3, after="rows1_2")
         midpoint(0, EVEN_FIRST[:2])
         quantise(1, 3)
-        first_velocity(3, 6, 7)
+        passes(1, 3, (6, 4, 7, 5))
+        for t, bank in zip(EVEN_FIRST, (6, 7, 4, 5)):
+            tanh(k1[3, t % 2][:, t // 2 : t // 2 + 1, :], bank, slice(t, t + 1))
         midpoint(0, EVEN_FIRST[2:])
         midpoint(1, EVEN_FIRST)
-        midpoint(2, EVEN_FIRST[:3])
-        midpoint(3, EVEN_FIRST[:2])
+        midpoint(2, EVEN_FIRST[:2])
+        midpoint(3, EVEN_FIRST[:1])
+        midpoint(2, EVEN_FIRST[2:3])
+        midpoint(3, EVEN_FIRST[1:3])
         midpoint(2, EVEN_FIRST[3:])
-        midpoint(3, EVEN_FIRST[2:])
+        midpoint(3, EVEN_FIRST[3:])
 
         rows_for(2, 0)
-        rows_for(2, 1)
+        rows_for(2, 1, room=2)
         gather(2, 0, (0, 2), on_scalar)
         gather(2, 0, (1, 3), on_vector)
         gather(2, 1, EVEN_FIRST, on_scalar)
-        partial(0, even, after="gy3")
+        rows_for(2, 2, after="gy3")
+        gather(2, 2, EVEN_FIRST, on_scalar)
+        partial(0, even, after="half_gain")
         interleave(2, 0)
-        rows_for(2, 2, after="rows2_0")
-        gather(2, 2, (0, 2), on_scalar)
         partial(0, odd, after="k1_0_0")
-        quantise(2, 0)
+        quantise(2, 0, after="rows2_1", at=SLOT)
         passes(2, 0, (4, 5, 4, 5))
         second_velocity(0, 4, even)
         second_velocity(0, 5, odd)
-        rows_for(2, 3, after="codes2_0")
-        gather(2, 3, EVEN_FIRST, on_scalar)
-        gather(2, 2, (1, 3), on_vector)
-        partial(1, even, after="k1_0_1")
-        interleave(2, 1, after="woven2_0")
+        rows_for(2, 3, after="rows2_1", at=SLOT // 2)
+        gather(2, 3, EVEN_FIRST[:3], on_scalar)
+        partial(1, even, after="rows2_0")
+        interleave(2, 1, after="rows2_0", at=SLOT // 2)
         partial(1, odd, after="k1_1_0")
         quantise(2, 1)
         passes(2, 1, (6, 6, 6, 6))
         second_velocity(1, 6, every)
+        gather(2, 3, EVEN_FIRST[3:], on_vector)
         interleave(2, 2, after="rows2_1")
-        partial(2, even, after="rows2_1", at=SLOT // 2)
+        partial(2, even, after="woven2_1")
         quantise(2, 2)
         passes(2, 2, (7, 7, 7, 7))
         second_velocity(2, 7, every)
@@ -327,9 +331,8 @@ def tile_picked_heun_none_po_kernel(
         partial(3, odd, after="k2_1")
         out_scales = sbuf("out_scales", [P, S], U8, after="part3_0")
         finish(3, even)
-        store(3, even)
         finish(3, odd)
-        store(3, odd)
+        store(3, every)
         quantise_out(0)
         round_out(3, on_vector)
         quantise_out(1)

@@ -300,8 +300,9 @@ def tile_picked_heun_none_po_kernel(
         interleave(2, 1, after="rows2_0", at=SLOT // 2)
         partial(1, odd, after="k1_1_0")
         quantise(2, 1)
-        passes(2, 1, (6, 6, 6, 6))
-        second_velocity(1, 6, every)
+        passes(2, 1, (6, 0, 6, 0))
+        second_velocity(1, 6, even)
+        second_velocity(1, 0, odd)
         gather(2, 3, EVEN_FIRST[3:], on_vector)
         interleave(2, 2, after="rows2_1")
         partial(2, even, after="woven2_1")
@@ -314,20 +315,20 @@ def tile_picked_heun_none_po_kernel(
         round_out(0, on_scalar, after="codes2_2")
         partial(2, odd, after="woven2_2")
         interleave(2, 3)
-        partial(3, even, after="k1_2_1")
+        finish(1, even, after="k1_2_1")
         quantise(2, 3)
         last = (4, 5, 0, 1)
         passes(2, 3, last)
         for t in EVEN_FIRST:
             second_velocity(3, last[t], slice(t, t + 1))
-        finish(1, even, after="rows2_3")
         finish(1, odd)
         store(1, every)
         round_out(1, on_scalar, after="codes2_3")
-        finish(2, even, after="woven2_3")
+        finish(2, even, after="rows2_3")
         finish(2, odd)
         store(2, every)
         round_out(2, on_scalar)
+        partial(3, even, after="woven2_3")
         partial(3, odd, after="k2_1")
         out_scales = sbuf("out_scales", [P, S], U8, after="part3_0")
         finish(3, even)

from contextlib import ExitStack

import concourse.mybir as mybir

T, S, H = 2048, 512, 512
FLOPS = 3 * 2 * 512 * 512 * 512

F32 = mybir.dt.float32
BF16 = mybir.dt.bfloat16
I32 = mybir.dt.int32
U32 = mybir.dt.uint32
U16 = mybir.dt.uint16
U8 = mybir.dt.uint8
FP8X4 = mybir.dt.float8_e4m3fn_x4
FP4X4 = mybir.dt.float4_e2m1fn_x4
MULT = mybir.AluOpType.mult
ADD = mybir.AluOpType.add
ACT = mybir.ActivationFunctionType

P = 128
PLANES = 4
CH = 128
HALF = S // 2
SLOT = 4 * PLANES * CH
EVEN_FIRST = (0, 2, 1, 3)
PER_COLUMN = 16
PARKED = P - 16
X_FIRST = T // 2


def chunk(c):
    return slice(c * CH, (c + 1) * CH)


def load_scale_rows(nc, tile, scales):
    for r in range(4):
        nc.sync.dma_start(tile[r:P:32, :].bitcast(I32), scales[0, r:16:4, :].bitcast(I32))


def unpark(nc, tile, parked):
    for q in range(4):
        source = parked[PARKED + 4 * q : PARKED + 4 * q + 4, :]
        nc.sync.dma_start(tile[32 * q : 32 * q + 4, :].bitcast(I32), source.bitcast(I32))


def deal(nc, dealt, raw):
    nc.vector.tensor_copy(
        dealt.rearrange("p (t m) -> p t m", t=PLANES),
        raw.rearrange("p (m t) -> p t m", t=PLANES),
    )


def weave(copy, woven, planes):
    copy(
        woven.rearrange("p (c i t) -> p c t i", i=4, t=PLANES),
        planes.rearrange("p t (c i) -> p c t i", i=4),
    )


def tile_picked_heun_none_po_kernel(
    tc, x_words, x_scales, w1_words, w1_scales, gn, w2_words, w2_scales, offs, nb, out_0, out_1, out_2
):
    nc = tc.nc
    with ExitStack() as ctx:
        keep = ctx.enter_context(tc.tile_pool(name="keep", bufs=1))
        slots = ctx.enter_context(tc.tile_pool(name="slots", bufs=1))
        psum = ctx.enter_context(tc.psum_pool(name="psum", bufs=1))

        places, fresh = {}, []

        def sbuf(name, shape, dtype, after=None, at=0, room=1):
            if after:
                places[name] = places[after] + at
            else:
                places[name] = SLOT * len(fresh)
                fresh.extend([name] * room)
            return slots.tile(shape, dtype, name=name, offset=places[name], align_bytes=64)

        offs_sb = keep.tile([P, S // PER_COLUMN], U16, name="offs_sb")
        nb_sb = keep.tile([P, S // PER_COLUMN], U16, name="nb_sb")
        xw = keep.tile([P, T], U32, name="xw")
        xs = sbuf("xs", [P, T], U8)
        w1w_raw = sbuf("w1w_raw", [P, 2 * H], U8)
        w1s_raw = sbuf("w1s_raw", [P, H], U8)
        w2s_raw = sbuf("w2s_raw", [P, H], U8)
        xqs = sbuf("xqs", [P, S], U8)
        w2s = sbuf("w2s", [P, H], U8)
        gain = sbuf("gain", [P, PLANES], F32)
        half_gain = sbuf("half_gain", [P, PLANES], F32)

        nc.gpsimd.memset(w1s_raw[:].bitcast(F32), 0.0)
        nc.vector.memset(xs[:PARKED, :].bitcast(I32), 0)
        nc.vector.memset(xqs[:].bitcast(I32), 0)
        nc.vector.memset(w2s_raw[:PARKED, :].bitcast(I32), 0)
        nc.vector.memset(w2s[:].bitcast(I32), 0)
        nc.gpsimd.dma_start(gain[:], gn.rearrange("(p t) o -> p (t o)", t=PLANES))

        x_view = x_words[0].rearrange("p n r -> p (n r)").bitcast(I32)
        nc.sync.dma_start(offs_sb[:], offs)
        nc.sync.dma_start(xs[PARKED:, :].bitcast(I32), x_scales[0].bitcast(I32))
        nc.sync.dma_start(w1w_raw[:].bitcast(I32), w1_words[0].bitcast(I32))
        nc.sync.dma_start(xw[:, :X_FIRST].bitcast(I32), x_view[:, :X_FIRST])
        load_scale_rows(nc, w1s_raw, w1_scales)
        nc.sync.dma_start(xw[:, X_FIRST:].bitcast(I32), x_view[:, X_FIRST:])
        nc.sync.dma_start(w2s_raw[PARKED:, :].bitcast(I32), w2_scales[0].bitcast(I32))
        nc.sync.dma_start(nb_sb[:], nb)

        w1w = sbuf("w1w", [P, 2 * H], U8)
        w2w = sbuf("w2w", [P, 2 * H], U8)
        w1s = sbuf("w1s", [P, H], U8)
        xqw = [sbuf(f"xqw{half}", [P, HALF], U32) for half in range(2)]
        xqs_parked = sbuf("parked", [P, S], U8)
        w2s_parked = sbuf("w2s_parked", [P, H], U8)

        nc.scalar.activation(half_gain[:], gain[:], ACT.Copy, scale=0.5)
        nc.vector.tensor_copy(xqs_parked[:], xs[:].indirect(offs_sb[:]))
        deal(nc, w1w[:].bitcast(U16), w1w_raw[:].bitcast(U16))
        unpark(nc, xqs, xqs_parked)
        w2w_raw = sbuf("w2w_raw", [P, 2 * H], U8, after="w1w_raw")
        nc.sync.dma_start(w2w_raw[:].bitcast(I32), w2_words[0].bitcast(I32))
        deal(nc, w1s[:], w1s_raw[:])
        for half in range(2):
            entries = slice(half * HALF // PER_COLUMN, (half + 1) * HALF // PER_COLUMN)
            nc.vector.tensor_copy(xqw[half][:], xw[:].indirect(offs_sb[:, entries]))
        deal(nc, w2s_parked[:], w2s_raw[:])
        unpark(nc, w2s, w2s_parked)
        deal(nc, w2w[:].bitcast(U16), w2w_raw[:].bitcast(U16))

        banks = [psum.tile([P, S], F32, name=f"bank{b}") for b in range(8)]
        gy = [sbuf(f"gy{t}", [P, S], F32) for t in range(PLANES)]
        gh = [keep.tile([P, S], F32, name=f"gh{t}") for t in range(PLANES)]
        windows = {1: gy, 2: gh}
        woven, codes, scales, part, result, rounded = {}, {}, {}, {}, {}, {}
        k1 = {(c, odd): sbuf(f"k1_{c}_{odd}", [P, 2, CH], F32) for c in range(S // CH) for odd in range(2)}
        k2 = [sbuf(f"k2_{c}", [P, PLANES, CH], F32) for c in range(S // CH)]

        def on_scalar(out, in_):
            nc.scalar.activation(out, in_, ACT.Copy)

        on_vector = nc.vector.tensor_copy


        def product(acc, words, word_scales, t, moving, moving_scales):
            nc.tensor.matmul_mx(
                out=acc,
                lhsT=words[:, 2 * P * t : 2 * P * (t + 1)].bitcast(FP4X4),
                lhsT_scale=word_scales[:, P * t : P * (t + 1)],
                rhs=moving.bitcast(FP8X4),
                rhs_scale=moving_scales,
                start=True,
                stop=True,
            )

        def state_planes(half, odd):
            return banks[2 * half + odd][:].rearrange("p (t s) -> p t s", t=2)

        def state(t, half):
            cols = slice(half * HALF, (half + 1) * HALF)
            acc = state_planes(half, t % 2)[:, t // 2, :]
            product(acc, w1w, w1s, t, xqw[half][:], xqs[:, cols])
            nc.scalar.activation(gy[t][:, cols], acc, ACT.Copy, scale=gain[:, t : t + 1])

        rows = {}

        def rows_for(v, c, after=None, at=0, room=1):
            rows[v, c] = sbuf(f"rows{v}_{c}", [P, PLANES, CH], F32, after, at, room)[:]

        def gather(v, c, planes, copy):
            entries = nb_sb[:, c * CH // PER_COLUMN : (c + 1) * CH // PER_COLUMN]
            for t in planes:
                copy(rows[v, c][:, t, :], windows[v][t][:].indirect(entries))

        def interleave(v, c, after=None, at=0):
            woven[v, c] = sbuf(f"woven{v}_{c}", [P, PLANES * CH], BF16, after, at)[:]
            weave(on_vector, woven[v, c], rows[v, c])

        def quantise(v, c, after=None, at=0):
            codes[v, c] = sbuf(f"codes{v}_{c}", [P, CH], U32, after, at)
            scales[v, c] = sbuf(f"scales{v}_{c}", [P, CH], U8)
            nc.vector.quantize_mx(out=codes[v, c][:].bitcast(FP8X4), scales=scales[v, c][:], in_=woven[v, c])

        def passes(v, c, into, order=EVEN_FIRST):
            for t in order:
                product(banks[into[t]][:, chunk(t)], w2w, w2s, t, codes[v, c][:], scales[v, c][:])

        def tanh(out, bank, planes):
            acc = banks[bank][:].rearrange("p (t c) -> p t c", t=PLANES)
            nc.scalar.activation(out, acc[:, planes, :], ACT.Tanh)

        def first_velocity(c, even_bank, odd_bank):
            passes(1, c, (even_bank, odd_bank) * 2)
            tanh(k1[c, 0][:], even_bank, even)
            tanh(k1[c, 1][:], odd_bank, odd)

        def second_velocity(c, bank, planes):
            tanh(k2[c][:, planes, :], bank, planes)

        def midpoint(c, planes):
            for t in planes:
                factor = half_gain[:, t : t + 1]
                nc.vector.scalar_tensor_tensor(
                    gh[t][:, chunk(c)], k1[c, t % 2][:, t // 2, :], factor, gy[t][:, chunk(c)], MULT, ADD
                )

        def partial(c, planes, after=None, at=0):
            tile = part[c, planes.start] = sbuf(f"part{c}_{planes.start}", [P, 2, CH], F32, after, at)
            y = state_planes(c // 2, planes.start)[:, :, chunk(c % 2)]
            nc.vector.scalar_tensor_tensor(tile[:], k1[c, planes.start][:], 0.25, y, MULT, ADD)

        out_rows = out_0.rearrange("(p t) s -> p t s", t=PLANES)
        out_words = out_1[0].rearrange("p n r -> p (n r)").bitcast(I32)
        out_codes = sbuf("out_codes", [P, S], U32)

        def finish(c, planes, after=None, at=0):
            if c not in result:
                result[c] = sbuf(f"result{c}", [P, PLANES, CH], F32, after, at)
            nc.vector.scalar_tensor_tensor(
                result[c][:, planes, :], k2[c][:, planes, :], 0.25, part[c, planes.start][:], MULT, ADD
            )

        def store(c, planes):
            nc.sync.dma_start(out_rows[:, planes, chunk(c)], result[c][:, planes, :])

        def round_out(c, copy, after=None):
            rounded[c] = sbuf(f"rounded{c}", [P, PLANES * CH], BF16, after)
            weave(copy, rounded[c][:], result[c][:])

        def quantise_out(c):
            nc.vector.quantize_mx(
                out=out_codes[:, chunk(c)].bitcast(FP8X4), scales=out_scales[:, chunk(c)], in_=rounded[c][:]
            )

        def store_codes(first, last):
            cols = slice(first * CH, last * CH)
            nc.sync.dma_start(out_words[:, cols], out_codes[:, cols].bitcast(I32))

        every, even, odd = slice(0, PLANES), slice(0, PLANES, 2), slice(1, PLANES, 2)

        for pair in (0, 2):
            for half in range(2):
                state(pair, half)
                state(pair + 1, half)

        shared = sbuf("rows1_shared", [P, 2 * PLANES * CH], F32, room=2)
        for c, start in ((0, 0), (1, PLANES * CH), (3, CH)):
            rows[1, c] = shared[:, start : start + PLANES * CH].rearrange("p (t c) -> p t c", t=PLANES)
        rows_for(1, 2, after="gain")
        for t in (0, 1):
            gather(1, 0, (t,), on_vector)
            gather(1, 1, (t,), on_vector)
        gather(1, 0, (2, 3), on_vector)
        gather(1, 1, (3,), on_vector)
        gather(1, 1, (2,), on_scalar)
        gather(1, 2, range(PLANES), on_scalar)
        interleave(1, 0)
        interleave(1, 1)
        gather(1, 3, (1, 2), on_scalar)
        quantise(1, 0)
        first_velocity(0, 4, 5)
        gather(1, 3, (0,), on_vector)
        quantise(1, 1)
        first_velocity(1, 6, 7)
        woven[1, 2] = shared[:, (PLANES + 1) * CH : (PLANES + 3) * CH].bitcast(BF16)
        weave(on_vector, woven[1, 2], rows[1, 2])
        gather(1, 3, (3,), on_vector)
        quantise(1, 2)
        first_velocity(2, 4, 5)
        interleave(1, 3, after="rows1_2")
        midpoint(0, EVEN_FIRST[:2])
        quantise(1, 3)
        passes(1, 3, (6, 4, 7, 5))
        for t, bank in zip(EVEN_FIRST, (6, 7, 4, 5)):
            tanh(k1[3, t % 2][:, t // 2 : t // 2 + 1, :], bank, slice(t, t + 1))
        midpoint(0, EVEN_FIRST[2:])
        midpoint(1, EVEN_FIRST)
        midpoint(2, EVEN_FIRST[:2])
        midpoint(3, EVEN_FIRST[:1])
        midpoint(2, EVEN_FIRST[2:3])
        midpoint(3, EVEN_FIRST[1:3])
        midpoint(2, EVEN_FIRST[3:])
        midpoint(3, EVEN_FIRST[3:])

        rows_for(2, 0)
        rows_for(2, 1, room=2)
        gather(2, 0, (0, 2), on_scalar)
        gather(2, 0, (1, 3), on_vector)
        gather(2, 1, EVEN_FIRST, on_scalar)
        rows_for(2, 2, after="gy3")
        gather(2, 2, EVEN_FIRST, on_scalar)
        partial(0, even, after="half_gain")
        interleave(2, 0)
        partial(0, odd, after="k1_0_0")
        quantise(2, 0, after="rows2_1", at=SLOT)
        passes(2, 0, (4, 5, 4, 5))
        second_velocity(0, 4, even)
        second_velocity(0, 5, odd)
        rows_for(2, 3, after="rows2_1", at=SLOT // 2)
        gather(2, 3, EVEN_FIRST[:3], on_scalar)
        partial(1, even, after="rows2_0")
        interleave(2, 1, after="rows2_0", at=SLOT // 2)
        partial(1, odd, after="k1_1_0")
        quantise(2, 1)
        passes(2, 1, (6, 0, 6, 0))
        second_velocity(1, 6, even)
        second_velocity(1, 0, odd)
        gather(2, 3, EVEN_FIRST[3:], on_vector)
        interleave(2, 2, after="rows2_1")
        partial(2, even, after="woven2_1")
        quantise(2, 2)
        passes(2, 2, (7, 7, 7, 7))
        second_velocity(2, 7, every)
        finish(0, even, after="rows2_2")
        finish(0, odd)
        store(0, every)
        round_out(0, on_scalar, after="codes2_2")
        partial(2, odd, after="woven2_2")
        interleave(2, 3)
        finish(1, even, after="k1_2_1")
        quantise(2, 3)
        last = (4, 5, 0, 1)
        passes(2, 3, last)
        for t in EVEN_FIRST:
            second_velocity(3, last[t], slice(t, t + 1))
        finish(1, odd)
        store(1, every)
        round_out(1, on_scalar, after="codes2_3")
        finish(2, even, after="rows2_3")
        finish(2, odd)
        store(2, every)
        round_out(2, on_scalar)
        partial(3, even, after="woven2_3")
        partial(3, odd, after="k2_1")
        out_scales = sbuf("out_scales", [P, S], U8, after="part3_0")
        finish(3, even)
        finish(3, odd)
        store(3, every)
        quantise_out(0)
        round_out(3, on_vector)
        quantise_out(1)
        store_codes(0, 2)
        quantise_out(2)
        quantise_out(3)
        store_codes(2, 4)
        for q in range(4):
            queue = nc.sync if q % 2 == 0 else nc.scalar
            live = out_scales[32 * q : 32 * q + 4, :]
            queue.dma_start(out_2[0, 4 * q : 4 * q + 4, :].bitcast(I32), live.bitcast(I32))
